import numpy as np, ml_dtypes
CORES = [3,11,19,27,35,43,51,59]
N = 8
import mx_ref
BF = ml_dtypes.bfloat16
def gentries(a):
    return np.ascontiguousarray(a.reshape(8, 16, -1).transpose(0, 2, 1)).reshape(8, -1)
def gtable(e):
    e = np.asarray(e); return np.ascontiguousarray(e.reshape(8, -1, 16).transpose(0, 2, 1)).reshape(128, -1).astype(np.int32)
def gcols(t, e):
    v = np.concatenate([t.reshape(8, 16, -1, 4), np.zeros((8, 16, 1, 4), BF)], axis=2)
    return np.ascontiguousarray(np.stack([v[g][:, e[g]] for g in range(8)])).reshape(128, -1)
def tile(rs):
    return np.stack(rs, axis=2).reshape(128, -1).astype(BF)
def cut(t, i, w=512):
    return t[:, w * i:w * i + w]
def pick(q, e):
    c = np.concatenate([q[0].reshape(128, -1, 4), np.zeros((128, 1, 4), np.uint8)], axis=1); s = np.concatenate([q[1], np.ones((16, 1), np.uint8)], axis=1)
    return (np.ascontiguousarray(c[:, e].reshape(128, -1)), np.ascontiguousarray(s[:, e]))
def join(*qs):
    return (np.concatenate([q[0] for q in qs], axis=1), np.concatenate([q[1] for q in qs], axis=1))
def put(q, e, v):
    c, s = q[0].reshape(128, -1, 4).copy(), q[1].copy(); c[:, e] = v[0].reshape(128, -1, 4); s[:, e] = v[1]
    return (c.reshape(128, -1), s)
def pk(c, s):
    return (np.ascontiguousarray(c), mx_ref.live(s))
def emit(q):
    return q[0], q[1]
def packed(v, rng):
    q = [mx_ref.quantize(np.ascontiguousarray(v[r])) for r in range(N)]
    return np.stack([a for a, b in q]), np.stack([mx_ref.plane(b, rng) for a, b in q])
def values_of_codes():
    e, c = np.zeros((128, 128, 4), np.float32), np.zeros((128, 2, 4), np.uint8)
    e[np.arange(128), np.arange(128), 0] = 1
    c[:127, :, 0] = np.arange(256).reshape(2, 128).T[:127]
    return mx_ref.matmul(mx_ref.quantize(e.reshape(128, 512).astype(BF)), (c.reshape(128, 8), np.full((16, 2), 127, np.uint8))).T.reshape(-1).astype(np.float64)
CODE_VALUE, SCALE_VALUE = values_of_codes(), 2.0 ** (np.arange(256) - 127.0)
def decode(q):
    return (CODE_VALUE[q[0]].reshape(16, 8, -1, 4) * SCALE_VALUE[q[1]][:, None, :, None] + 0.0).reshape(128, -1).astype(np.float32)
def f(rng, *shape):
    return mx_ref.flush((rng.standard_normal(shape, dtype=np.float32) * np.exp2(rng.integers(-2, 3, shape[:-1] + (1,)))).astype(BF))
def wide(rng, *shape, cols=0):
    v = rng.standard_normal(shape, dtype=np.float32) * np.exp2(rng.integers(-12, 13, shape)).astype(np.float32)
    if cols: v *= np.repeat(np.exp2(rng.integers(-cols, cols + 1, shape[:-2] + (1, shape[-1] // 4))) * (rng.random(shape[:-2] + (1, shape[-1] // 4)) > 0.0625), 4, axis=-1).astype(np.float32)
    return mx_ref.flush(v.astype(BF))
C, K, A, R = 384, 128, 352, 3
def big(v):
    v = v.astype(np.float32)
    v[np.abs(v) < np.float32(2.0 ** -16)] = 0
    return v.astype(BF)
def numbers_of(rng):
    return {"x": big(f(rng, N, 128, 4 * C)), "u": np.array(f(rng, N, 128, 512)), "v": np.array(f(rng, N, 128, 512))}
def weights(rng, w):
    c, p = packed(w, rng)
    return {"wc": c, "ws": p}
def still(rng):
    w = np.zeros((N, 128, 4, 128, 4), np.float32)
    i = np.arange(128)
    for b in range(4): w[:, i, b, i, b] = 32
    return weights(rng, w.reshape(N, 128, 2048).astype(BF))
def clauses(rng):
    return rng.integers(0, C + K, (N, 8, A, 4))
def stored(l):
    return {"cl": np.stack([gtable(e) for e in l])}
def signs(rng):
    return np.stack([rng.permutation(8) % 2 * 2.0 - 1.0 for r in range(N)])
def setup_inputs(rng):
    return {**numbers_of(rng), **stored(clauses(rng)), **weights(rng, f(rng, N, 128, 2048))}
def setup_inputs_signs(rng):
    d = numbers_of(rng)
    o = rng.permutation(N)
    kinds = np.array([[0, 0, -1, -2, 1, 1, 1, 2], [0, 0, 0, -1, -1, -2, 1, 2], [0, -1, -1, -2, -2, -2, -1, -1], [1, 1, 1, 1, 2, 2, 1, 1]])
    small = rng.permutation(N) % 2 == 0
    x = d["x"].reshape(N, 8, 16, C, 4)
    u = d["u"].reshape(N, 128, 128, 4)
    x[:, :, :8] = 0
    u[:, :, ::16] = 0
    for r in range(N):
        i = rng.permuted(np.tile(np.arange(C) % 8, (8, 1)), axis=1)
        size = 2.0 ** -30 if small[r] else 1.0
        x[r, :, 0, :, 0] = ((12 + kinds[o[r] % 4][i]) * size).astype(np.float32).astype(BF)
        x[r, :, 0, :, 1] = 12 * size
        for h in range(0, 128, 16):
            u[r, h, h, 0] = size
            u[r, h, h, 1] = -size
    return {"x": x.reshape(N, 128, 4 * C), "u": u.reshape(N, 128, 512), "v": d["v"], **stored(clauses(rng)), **still(rng)}
def setup_inputs_near(rng):
    d = numbers_of(rng)
    x = d["x"].astype(np.float32).reshape(N, 8, 16, C, 4)
    s = np.minimum((np.arange(C) + 1) // 2, 255)
    g = ((s[:, None] >> np.arange(8)) & 1) * np.exp2(np.arange(8) - 23.0)
    x[:, :, 0] = 0
    x[:, :, 0, :, 0] = signs(rng)[:, :, None]
    x[:, :, 8] = g[:, :4]
    x[:, :, 9] = g[:, 4:]
    x[:, :, 10:] = rng.integers(4, 8, (N, 8, 6, C, 4)) * rng.choice([-1.0, 1.0], (N, 8, 6, C, 4)) * 2.0 ** -20
    u = d["u"].reshape(N, 128, 128, 4)
    k = np.where(rng.permutation(N) < N // 2, 2.0 ** -30, 1.0).astype(np.float32).astype(BF)
    u[:, :, ::16] = 0
    for h in range(0, 128, 16):
        u[:, h, h, 0] = k
        u[:, h + 8:h + 10, h] = k[:, None, None]
    return {"x": x.reshape(N, 128, 4 * C).astype(BF), "u": u.reshape(N, 128, 512), "v": d["v"], **stored(clauses(rng)), **still(rng)}
def setup_inputs_huge(rng):
    d = numbers_of(rng)
    x = 2.0 ** 30 * (0.8 + 0.2 * rng.random((N, 128, C, 4)))
    c = np.stack([rng.permutation(C) % 2 * 2.0 - 1.0 for r in range(N)])
    o = rng.permutation(N)
    c[o < N // 2] = 1
    for r in range(N):
        if o[r] >= N - N // 4: c[r] = np.where(np.arange(C) % 4 == rng.integers(4), 1.0, -1.0)
    x *= c[:, None, :, None]
    u = d["u"].reshape(N, 128, 128, 4)
    a = 2.0 ** 30 * (1 - 0.1 * rng.random((N, 128, 8, 4))) * signs(rng)[:, None, :, None]
    u[:, :, ::16] = a.astype(np.float32).astype(BF)
    return {"x": x.astype(np.float32).reshape(N, 128, 4 * C).astype(BF), "u": u.reshape(N, 128, 512), "v": d["v"], **stored(clauses(rng)), **still(rng)}
def setup_inputs_lists(rng):
    d = numbers_of(rng)
    l = clauses(rng)
    o = rng.permutation(N)
    for r in range(N):
        if o[r] % 4 == 0: l[r] = C + (np.argsort(rng.random((8, A)), axis=1) % K)[:, :, None]
        if o[r] % 4 == 1: l[r] = rng.integers(0, C, (8, A, 4))
        if o[r] % 4 == 2: l[r] = C + rng.integers(0, K, (8, 1, 1))
        if o[r] % 4 == 3:
            l[r, :, :256] = rng.integers(0, C, (8, 256, 4))
            l[r, :, 256:] = rng.integers(C, C + K, (8, A - 256, 4))
    return {**d, **stored(l), **weights(rng, f(rng, N, 128, 2048))}
def setup_inputs_spread(rng):
    d = setup_inputs(rng)
    d["x"] = big(wide(rng, N, 128, 4 * C, cols=6))
    return d
def check_inputs(d):
    b = []
    for k in ("x", "u", "v"):
        a = np.abs(d[k].astype(np.float32))
        if not (np.isfinite(a).all() and ((a == 0) | (a >= 2.0 ** -30) & (a <= 2.0 ** 30)).all()): b.append("a value of " + k)
    if ((d["cl"] < 0) | (d["cl"] >= C + K)).any(): b.append("an entry of cl")
    return b
def mean(a, b):
    return ((a.astype(np.float32) + b.astype(np.float32)) * np.float32(0.5)).astype(BF)
def reference(x, u, v, cl, wc, ws):
    qu = [mx_ref.quantize(u[r]) for r in range(N)]
    lay = [pk(wc[r], ws[r]) for r in range(N)]
    lit = [gentries(cl[r]).reshape(8, A, 4).astype(np.int64) for r in range(N)]
    now = [x[r] for r in range(N)]
    cur = [np.zeros((8, A), np.int64) for r in range(N)]
    for t in range(R):
        own, e, sent, back = [], [], [], []
        for r in range(N):
            own.append(mx_ref.matmul(qu[r], mx_ref.quantize(now[r]))[::16] + np.float32(0.0))
            e.append(np.argsort(-own[r], axis=1, kind="stable")[:, :K])
            sent.append(mx_ref.quantize(gcols(now[r], e[r])))
        came = decode(join(*sent)).astype(BF)
        for r in range(N):
            p = (r - 1) % N
            place = np.concatenate([now[r], cut(came, p, 4 * K)], axis=1)
            yes = np.concatenate([own[r], mx_ref.matmul(qu[r], sent[p])[::16]], axis=1) > 0
            named = np.stack([yes[g][lit[r][g]] for g in range(8)])
            turn = (cur[r][:, :, None] + np.arange(4)) % 4
            cur[r] = (cur[r] + np.argmax(np.take_along_axis(named, turn, axis=2), axis=2)) % 4
            one = np.take_along_axis(lit[r], cur[r][:, :, None], axis=2)[:, :, 0]
            two = np.take_along_axis(lit[r], (cur[r][:, :, None] + 1) % 4, axis=2)[:, :, 0]
            q = mx_ref.quantize(mean(gcols(place, one), gcols(place, two)))
            h = tile([mx_ref.matmul(pick(lay[r], np.arange(128 * b, 128 * b + 128)), q) * np.float32(0.03125) for b in range(4)])
            first = np.full((8, C + K), -1)
            for j in range(A - 1, -1, -1): first[np.arange(8), one[:, j]] = j
            back.append(mx_ref.quantize(gcols(h, first[:, C:])))
        home = decode(join(*back)).astype(BF)
        for r in range(N):
            new = now[r].copy().reshape(8, 16, C, 4)
            got = cut(home, (r + 1) % N, 4 * K).reshape(8, 16, K, 4)
            for g in range(8): new[g][:, e[r][g]] = mean(new[g][:, e[r][g]], got[g])
            now[r] = new.reshape(128, 4 * C)
    y, ow = np.zeros((N, 128, C), np.float32), np.zeros((N, 8, A), np.float32)
    oc, osc = np.zeros((N, 128, 4 * C), np.uint8), np.zeros((N, 16, C), np.uint8)
    for r in range(N):
        q = mx_ref.quantize(now[r])
        y[r] = mx_ref.matmul(mx_ref.quantize(v[r]), q)
        ow[r] = cur[r]
        oc[r], osc[r] = emit(q)
    return {"y": y, "ow": ow, "oc": oc, "osc": osc}

@@ -1,0 +1,436 @@
+from concourse.mybir import dt, AluOpType as OP, ActivationFunctionType as AF
+
+C, K, A, R = 384, 128, 352, 3
+ZA = 224
+BIG = float(2 ** 80)
+TOP = float(2 ** 22)
+MID = float(C // 2)
+NVROW = 7
+NSCMP = 4
+TW = [384, 320, 256, 192, 128, 128]
+TO = [0, 384, 704, 960, 1152, 1280]
+SOW = 184
+
+
+def _scratch():
+    s = {}
+    for n, w in dict(X=1536, ub=512, vb=512, E=512, Ph=2048, Eq=512, TT=5632, tau=2176, so=SOW * 8, dsc=384, rstb=384, Fl=512,
+                     Ft=1568, Z=1408, tmp=1408, Hs=2048, Vt=512, Ar=352, D0=2816, so2=2816, fd=352, Awin=512, cI=528, one=528,
+                     q25=528, cW=2048, cB=512, gm=512, M16=384, M16b=384, Rst=384, msk2=384, sc2=384, ew=384,
+                     val=384, M4=128, Rst4=128, m4o=128, s4o=128).items():
+        s[n] = ("sbuf", [128, w], "bfloat16")
+    for n, w in dict(i16=384, msk=384, sc=384, rowS=24, pre0=24, pre=24, cst=24, rank=24, jw=24, cf=8, cg=8, nth=8,
+                     Lf=112, P0=88, pay=88, base=88, cand=88, c1=44, xb=24, yb=384, owb=352).items():
+        s[n] = ("sbuf", [128, w], "float32")
+    for n, w in dict(pcol=1, ci=4, c2i=22, ot=44, cc=22, ti=88, cli=88, uoffi=8).items():
+        s[n] = ("sbuf", [128, w], "int32")
+    for n, w in dict(uoff=8, roff=24, eoff=32, xoff=24, zoff=44, foff=8, flist=88, c2u=88, Lu=88, coff=22).items():
+        s[n] = ("sbuf", [128, w], "uint16")
+    pairs = dict(U=128, U2=128, Vv=128, X=384, T=1408, I=512, W=512, B=128, L=512, F=392, Z=352)
+    for t in range(R):
+        for n in ("E", "G", "V", "H"):
+            pairs[n + str(t)] = 128
+    for n, w in pairs.items():
+        s["q" + n] = ("sbuf", [128, w], "float8_e4m3fn_x4")
+        s["s" + n] = ("sbuf", [128, w], "uint8")
+    s["d1"] = ("dram", [8, 4, 4, 88], "uint16")
+    s["d2"] = ("dram", [8, 4, 4, 4, 22], "uint16")
+    s["ps"] = ("psum", [128, 4096], "float32")
+    return s
+
+
+SCRATCH = _scratch()
+SEMAPHORES = ["cV", "cS", "cP", "cG", "sent"] + ["arr%d" % i for i in range(2 * R)] + ["dm%d" % i for i in range(16)]
+
+
+def rank_program(g, core, T, topo):
+    rank = T.rank_of(core)
+    if rank is None:
+        return
+    n = len(T.cores)
+    after, before = T.cores[(rank + 1) % n], T.cores[(rank - 1) % n]
+    V, S, P, Y = g.vector, g.scalar, g.tensor, g.sync
+    Q = {"V": V, "S": S, "P": P, "G": g, "Y": Y}
+    count, wrote, readers = {}, {}, {}
+    waited = {q: {} for q in Q}
+
+    def issue(q, own, calls, inc, r, w, acc=False):
+        deps = {}
+
+        def add(d):
+            for s_, v_ in d.items():
+                deps[s_] = max(deps.get(s_, 0), v_)
+        for k in r:
+            add(wrote.get(k, {}))
+            if k.startswith("ps"):
+                add({s_: v_ for s_, v_ in readers.get(k, {}).items() if s_ != own})
+        for k in w:
+            if not acc:
+                add(wrote.get(k, {}))
+            add(readers.get(k, {}))
+        need(q, deps)
+        for call in calls:
+            call().then_inc(T.sem[own], inc)
+            count[own] = count.get(own, 0) + inc
+        for k in r:
+            readers.setdefault(k, {})[own] = count[own]
+        for k in w:
+            wrote[k] = {own: count[own]}
+            readers[k] = {}
+
+    def need(q, deps):
+        for sem, val in deps.items():
+            if waited[q].get(sem, 0) < val:
+                Q[q].wait_ge(T.sem[sem], val)
+                waited[q][sem] = val
+
+    def op(q, call, r=(), w=(), acc=False):
+        issue(q, "c" + q, [call], 1, r, w, acc)
+
+    def dma(q, sem, pairs, r=(), w=()):
+        issue(q, sem, [lambda o=o, i=i: Q[q].dma_start(o, i) for o, i in pairs], 16, r, w)
+
+    def bank(b, w):
+        return T.ps[:, 512 * b:512 * b + w]
+
+    def ts(out, in0, s1, s2, o0, o1, r, w):
+        if o1 is None:
+            op("V", lambda: V.tensor_scalar(out, in0, s1, None, o0), r, w)
+        else:
+            op("V", lambda: V.tensor_scalar(out, in0, s1, s2, o0, o1), r, w)
+
+    def tt(out, a, b, o, r, w):
+        op("V", lambda: V.tensor_tensor(out, a, b, o), r, w)
+
+    def cp(out, a, r, w):
+        op("V", lambda: V.tensor_copy(out, a), r, w)
+
+    def scan(out, d0, d1, init, o0, o1, r, w):
+        op("V", lambda: V.tensor_tensor_scan(out, d0, d1, init, o0, o1), r, w)
+
+    def fill(ap, c, w):
+        op("V", lambda: V.memset(ap, c), (), w)
+
+    def act(out, a, f, r, w, **kw):
+        op("S", lambda: S.activation(out, a, f, **kw), r, w)
+
+    def sfill(buf, a, b, c, w):
+        act(buf[:, a:b], T.one[:, 0:b - a], AF.Copy, ["one"], w, scale=c)
+
+    def quant(name, a, b, src, r, key=None):
+        op("V", lambda: V.quantize_mx(T["q" + name][:, a:b], T["s" + name][:, a:b], src), r, [key or "q" + name])
+
+    def mm(b, st, sa, mv, ma, w, r, start=True, stop=True):
+        op("P", lambda: P.matmul_mx(bank(b, w), T["q" + st][:, sa:sa + 128], T["s" + st][:, sa:sa + 128],
+                                    T["q" + mv][:, ma:ma + w], T["s" + mv][:, ma:ma + w], start, stop),
+           r, ["ps%d" % b], acc=not start)
+
+    def iota(out, pat, base, mult, w, small=True):
+        if small:
+            op("G", lambda: g.iota(out, pat, base, mult, allow_small_or_imprecise_dtypes=True), (), w)
+        else:
+            op("G", lambda: g.iota(out, pat, base, mult), (), w)
+
+    def where0(out, a, pat, base, mult, r, w):
+        op("G", lambda: g.affine_select(out, a, pat, OP.is_equal, 0.0, base, mult), r, w)
+
+    def send(src, dst, to, sem):
+        rid, pid, _ = topo.addr(to)
+        m = topo.mask(core, to)
+        need("G", wrote["q" + src])
+        g.remote_dma(T["q" + dst][:].bitcast(dt.uint8), T["q" + src][:].bitcast(dt.uint8), T.sem[sem], T.sem.sent, pid, rid, m)
+        g.remote_dma(T["s" + dst][:], T["s" + src][:], T.sem[sem], T.sem.sent, pid, rid, m)
+        count["sent"] = count.get("sent", 0) + 2 * len(topo.engines(core, to))
+
+    def arrived(name, frm, sem):
+        count[sem] = 2 * len(topo.engines(frm, core))
+        wrote["q" + name] = {sem: count[sem]}
+
+    def four(name):
+        return [name + str(i) for i in range(4)]
+
+    XK = four("X")
+    dma("S", "dm0", [(T.ub[:], T.u[:])], (), ["ub"])
+    dma("Y", "dm1", [(T.X[:], T.x[:])], (), XK)
+    dma("Y", "dm2", [(T.cli[:], T.cl[:])], (), ["cli"])
+
+    k0 = 24 - NVROW
+    iota(T.pcol[:], [[0, 1]], 0, 1, ["pcol"], False)
+    iota(T.uoffi[:], [[16, 8]], 0, 0, ["uoffi"], False)
+    iota(T.i16[:], [[0, 24], [1, 16]], 0, 0, ["i16"])
+    iota(T.pre0[:], [[16, 24]], 0, 0, ["pre0"])
+    iota(T.s4o[:], [[0, 32], [1, 4]], 0, 0, ["s4o"])
+    iota(T.gm[:], [[1, 8], [0, 64]], 0, 0, ["gm"])
+    iota(T.val[:], [[1, C]], -int(MID), 0, ["val"])
+    fill(T.one[:], 1.0, ["one"])
+    fill(T.Rst[:], BIG, ["Rst"])
+    fill(T.rstb[:], 1.0, ["rstb"])
+    fill(T.Rst4[:], BIG, ["Rst4"])
+    fill(T.rowS[:, 0:1], 0.0, ["row0"])
+    fill(T.Rst[:, 0:C:16], -BIG, ["Rst"])
+    fill(T.rstb[:, 0:C:16], 0.0, ["rstb"])
+    fill(T.Rst4[:, 0:K:4], -BIG, ["Rst4"])
+    sfill(T.q25, 0, 528, 0.25, ["q25"])
+    for m in range(6):
+        sfill(T.TT, 4 * (TO[m] + 16 * (21 - 4 * m)), 4 * (TO[m] + TW[m]), 0.0, four("T%d_" % m))
+    sfill(T.Ft, 1408, 1568, 0.0, ["FtP"])
+    for b in range(4):
+        sfill(T.Hs, 512 * b + ZA, 512 * b + 512, 0.0, ["HB%d" % b])
+    where0(T.cI[:], T.q25[:], [[-1, 528]], 3, 4, ["q25"], ["cI"])
+    for a in range(4):
+        where0(T.cW[:, 512 * a:512 * a + 512], T.one[:, 0:512], [[-512, 8], [1, 16], [-1, 4]], -4 * a, 32, ["one"], ["cW%d" % a])
+    ts(T.ci[:, 0:1], T.pcol[:], 15, None, OP.bitwise_and, None, ["pcol"], ["ci0"])
+    ts(T.ci[:, 1:2], T.pcol[:], 4, None, OP.arith_shift_right, None, ["pcol"], ["ci1"])
+    ts(T.ci[:, 2:3], T.pcol[:], 3, None, OP.bitwise_and, None, ["pcol"], ["ci2"])
+    ts(T.ci[:, 3:4], T.pcol[:], 2, 3, OP.arith_shift_right, OP.bitwise_and, ["pcol"], ["ci3"])
+    cp(T.uoff[:], T.uoffi[:], ["uoffi"], ["uoff"])
+    cp(T.cf[:, 0:4], T.ci[:], four("ci"), ["cf"])
+    pr, pg, pt, pq = T.cf[:, 0:1], T.cf[:, 1:2], T.cf[:, 2:3], T.cf[:, 3:4]
+    ts(T.msk2[:], T.i16[:], pr, 0.5, OP.is_equal, OP.subtract, ["i16", "cf"], ["msk2"])
+    ts(T.cg[:, 0:1], pr, -2.0, 15.0 + MID, OP.mult, OP.add, ["cf"], ["cg0"])
+    ts(T.cg[:, 1:2], pr, -1.5, 15.0 + MID, OP.mult, OP.add, ["cf"], ["cg1"])
+    ts(T.cg[:, 2:3], pt, 4 * MID, None, OP.add, None, ["cf"], ["cg2"])
+    ts(T.M16[:], T.msk2[:], 2 * BIG, None, OP.mult, None, ["msk2"], ["M16"])
+    ts(T.M16b[:], T.msk2[:], 2 * BIG, -MID, OP.mult, OP.min, ["msk2"], ["M16b"])
+    ts(T.jw[:], T.pre0[:], pr, None, OP.add, None, ["pre0", "cf"], ["jw"])
+    ts(T.m4o[:], T.s4o[:], pq, 0.5, OP.is_equal, OP.subtract, ["s4o", "cf"], ["m4o"])
+    ts(T.cst[:, 0:k0], T.jw[:, 0:k0], T.cg[:, 0:1], None, OP.add, None, ["jw", "cg0"], ["cstA"])
+    ts(T.cst[:, k0:24], T.jw[:, k0:24], 0.5, T.cg[:, 1:2], OP.mult, OP.add, ["jw", "cg1"], ["cstB"])
+    ts(T.M4[:], T.m4o[:], 2 * BIG, None, OP.mult, None, ["m4o"], ["M4"])
+    quant("U", 0, 128, T.ub[:], ["ub"])
+    cp(T.qU2[:].bitcast(dt.uint32), T.qU[:].bitcast(dt.uint32).indirect(T.uoff[:]), ["qU", "uoff"], ["qU2"])
+    cp(T.sU2[:], T.sU[:].indirect(T.uoff[:]), ["qU", "uoff"], ["sU2"])
+    for a in range(4):
+        cp(T.c2u[:, 22 * a:22 * a + 22], T.cli[:, a:88:4], ["cli"], ["c2u%d" % a])
+    ts(T.cB[:], T.gm[:], pg, None, OP.is_equal, None, ["gm", "cf"], ["cB"])
+    dma("Y", "dm3", [(T.qL[:].bitcast(dt.uint8), T.wc[:]), (T.sL[:], T.ws[:])], XK, ["qL"])
+    dma("Y", "dm4", [(T.vb[:], T.v[:])], (), ["vb"])
+    dma("Y", "dm5", [(T.d1[:, i], T.c2u[i:128:4, :]) for i in range(4)], four("c2u"), ["d1"])
+    dma("Y", "dm6", [(T.d2[:, a], T.c2u[:, 22 * a:22 * a + 22]) for a in range(4)], four("c2u"), ["d2"])
+    dma("Y", "dm7", [(T.flist[:], T.d1[:])], ["d1"], ["flist"])
+    dma("Y", "dm8", [(T.Lu[:], T.d2[:])], ["d2"], ["Lu"])
+
+    def late():
+        iota(T.Awin[:, 0:C], [[0, C]], -1, 0, ["AwinA"])
+        iota(T.Awin[:, C:512], [[1, K]], 0, 0, ["AwinB"])
+        iota(T.fd[:, 0:A - ZA], [[-2, A - ZA]], 2 * (A - 1) - ZA, 0, ["fdA"])
+        iota(T.fd[:, A - ZA:A], [[-1, ZA]], ZA - 1, 0, ["fdB"])
+        cp(T.Lf[:, 0:88], T.Lu[:], ["Lu"], ["Lf"])
+        cp(T.Lf[:, 88:110], T.Lu[:, 0:22], ["Lu"], ["Lf2"])
+        quant("I", 0, 128, T.cI[:, 3:515], ["cI"], "qI0")
+        ts(T.cand[:], T.Lf[:, 22:110], 512.0, None, OP.mult, None, ["Lf", "Lf2"], ["cand"])
+        quant("I", 128, 256, T.cI[:, 2:514], ["cI"], "qI1")
+        tt(T.pay[:], T.cand[:], T.Lf[:, 0:88], OP.add, ["cand", "Lf"], ["pay"])
+        quant("I", 256, 384, T.cI[:, 1:513], ["cI"], "qI2")
+        quant("I", 384, 512, T.cI[:, 0:512], ["cI"], "qI3")
+        quant("W", 0, 512, T.cW[:], four("cW"))
+        for i in range(4):
+            ts(T.base[:, i:88:4], T.pay[:, 22 * i:22 * i + 22], float(i * 2 ** 18 + (3 - i) * 2 ** 20), None, OP.add, None,
+               ["pay"], ["base%d" % i])
+        act(T.nth[:], T.jw[:, 0:8], AF.Copy, ["jw"], ["nth"], scale=-1024.0)
+
+    def slot(k):
+        return (24 - k) // 4, (24 - k) % 4
+
+    def row_view(k, a, b):
+        m, s = slot(k)
+        return T.TT[:, 4 * (TO[m] + a) + s:4 * (TO[m] + b):4]
+
+    def rkey(k):
+        return "T%d_%d" % slot(k)
+
+    def tile_q(m, first, last):
+        quant("T", TO[m], TO[m] + TW[m], T.TT[:, 4 * TO[m]:4 * (TO[m] + TW[m])], four("T%d_" % m), "qT%d" % m)
+        mm(2, "B", 0, "T", TO[m], TW[m], ["qB", "qT%d" % m], first, last)
+
+    def plane(buf, b):
+        return buf[:, 512 * b:512 * b + 512]
+
+    for t in range(R):
+        quant("X", 0, C, T.X[:], XK)
+        mm(0, "U2", 0, "X", 0, C, ["qU2", "sU2", "qX"])
+        mm(1, "U2", 0, "X", 0, C, ["qU2", "sU2", "qX"])
+        if t == 0:
+            quant("B", 0, 128, T.cB[:], ["cB"])
+        tt(T.msk[:], bank(0, C), T.M16[:], OP.min, ["ps0", "M16"], ["msk"])
+        scan(T.sc[:], T.Rst[:], T.msk[:], -BIG, OP.min, OP.max, ["Rst", "msk"], ["sc"])
+        srows = list(range(k0 - 1, 0, -1))
+
+        def s1(k):
+            o = 8 * k * (k - 1)
+            act(T.tau[:, o:o + 16 * k], bank(1, 16 * k), AF.Sign, ["ps1", "sc"], ["tau%d" % k], scale=-1.0,
+                bias=T.sc[:, 16 * k + 15:16 * k + 16])
+
+        def s2(k):
+            o = 8 * k * (k - 1)
+            act(row_view(k, 0, 16 * k), T.tau[:, o:o + 16 * k], AF.Relu, ["tau%d" % k], [rkey(k), "row%d" % k],
+                accum_out=T.rowS[:, k:k + 1])
+        s1(srows[0])
+        for i, k in enumerate(srows):
+            if i + 1 < len(srows):
+                s1(srows[i + 1])
+            s2(k)
+
+        def v1(k):
+            ts(row_view(k, 0, 16 * k), bank(0, 16 * k), T.sc[:, 16 * k + 15:16 * k + 16], None, OP.is_lt, None, ["ps0", "sc"], [rkey(k)])
+
+        def v2(k):
+            e = SOW * (k - k0 + 1)
+            scan(T.so[:, e - 8 * k:e], row_view(k, 0, 8 * k), row_view(k, 8 * k, 16 * k), float(-8 * k), OP.add, OP.add,
+                 [rkey(k)], ["so%d" % k])
+        tt(row_view(24, 0, C), bank(0, C), T.sc[:], OP.is_le, ["ps0", "sc"], [rkey(24)])
+        v1(23); v1(22); v1(21)
+        scan(T.dsc[:], T.rstb[:], row_view(24, 0, C), 0.0, OP.mult, OP.add, ["rstb", rkey(24)], ["dsc"])
+        tile_q(0, True, False)
+        v1(20); v2(23); v1(19); v2(22)
+        tile_q(2, False, False)
+        v1(18); v2(21); v1(17); v2(20)
+        tile_q(3, False, False)
+        tile_q(1, False, False)
+        v2(19); v2(18)
+        tile_q(4, False, False)
+        v2(17)
+        tt(T.pre0[:], T.cst[:], T.dsc[:, 15:C:16], OP.subtract, ["cstA", "cstB", "dsc"], ["pre0"])
+        cp(T.rowS[:, k0:24], T.so[:, SOW - 1:SOW * NVROW:SOW], ["so%d" % k for k in range(k0, 24)], ["rowV"])
+        tile_q(5, False, True)
+        tt(T.pre[:], T.pre0[:], T.rowS[:], OP.subtract, ["pre0", "rowV"] + ["row%d" % k for k in range(k0)], ["pre"])
+        tt(T.msk2[:], bank(2, C), T.M16b[:], OP.add, ["ps2", "M16b"], ["msk2"])
+        scan(T.sc2[:], T.Rst[:], T.msk2[:], -BIG, OP.min, OP.max, ["Rst", "msk2"], ["sc2"])
+        tt(T.rank[:], T.pre[:], T.sc2[:, 15:C:16], OP.add, ["pre", "sc2"], ["rank"])
+        cp(T.roff[:], T.rank[:], ["rank"], ["roff"])
+        cp(T.ew[:].indirect(T.roff[:]), T.val[:], ["roff", "val"], ["ew"])
+        tt(T.m4o[:], T.ew[:, 0:K], T.M4[:], OP.min, ["ew", "M4"], ["m4o"])
+        scan(T.s4o[:], T.Rst4[:], T.m4o[:], -BIG, OP.min, OP.max, ["Rst4", "m4o"], ["s4o"])
+        ts(T.eoff[:], T.s4o[:, 3:K:4], 4.0, T.cg[:, 2:3], OP.mult, OP.add, ["s4o", "cg2"], ["eoff"])
+        act(T.E[:, 256:512], T.X[:].indirect(T.eoff[:, 16:32]), AF.Copy, XK + ["eoff"], ["Eb"])
+        cp(T.E[:, 0:256], T.X[:].indirect(T.eoff[:, 0:16]), XK + ["eoff"], ["Ea"])
+        quant("E%d" % t, 0, K, T.E[:], ["Ea", "Eb"])
+        send("E%d" % t, "G%d" % t, after, "arr%d" % (2 * t))
+        if t == 0:
+            late()
+        ts(T.Fl[:, 0:C], bank(0, C), 0.0, TOP, OP.is_gt, OP.mult, ["ps0"], ["FlA"])
+        for b in range(4):
+            if b < 2 or t == 0:
+                act(T.Ph[:, 512 * b:512 * b + C], T.X[:, b:4 * C:4], AF.Copy, XK, ["PhA%d" % b], scale=0.5)
+            else:
+                ts(T.Ph[:, 512 * b:512 * b + C], T.X[:, b:4 * C:4], 0.5, None, OP.mult, None, XK, ["PhA%d" % b])
+        Gn = "G%d" % t
+        arrived(Gn, before, "arr%d" % (2 * t))
+        mm(3, "U2", 0, Gn, 0, K, ["qU2", "sU2", "q" + Gn])
+        for b in range(4):
+            mm(4 + b, "I", 128 * b, Gn, 0, K, ["qI%d" % b, "q" + Gn])
+        ts(T.Fl[:, C:512], bank(3, K), 0.0, TOP, OP.is_gt, OP.mult, ["ps3"], ["FlB"])
+        act(T.Ft[:, 704:1408], T.Fl[:].indirect(T.flist[:, 44:88]), AF.Copy, ["FlA", "FlB", "flist"], ["Ftb"])
+        cp(T.Ft[:, 0:704], T.Fl[:].indirect(T.flist[:, 0:44]), ["FlA", "FlB", "flist"], ["Fta"])
+        quant("F", 0, 176, T.Ft[:, 0:704], ["Fta"], "qFa")
+        quant("F", 176, 392, T.Ft[:, 704:1568], ["Ftb", "FtP"], "qFb")
+        for b in range(4):
+            act(T.Ph[:, 512 * b + C:512 * b + 512], bank(4 + b, K), AF.Copy, ["ps%d" % (4 + b)], ["PhB%d" % b], scale=2.0)
+        for a in range(4):
+            mm(2, "W", 128 * a, "F", 88 * a, 128, ["qW", "qFa"] + (["qFb"] if a else []), a == 0, a == 3)
+        tt(T.cand[:], bank(2, 88), T.base[:], OP.add, ["ps2"] + four("base"), ["cand"])
+        tt(T.c1[:], T.cand[:, 0:88:2], T.cand[:, 1:88:2], OP.max, ["cand"], ["c1"])
+        tt(T.c2i[:], T.c1[:, 0:44:2], T.c1[:, 1:44:2], OP.max, ["c1"], ["c2i"])
+        ts(T.ot[:, 0:22], T.c2i[:], 511, None, OP.bitwise_and, None, ["c2i"], ["ot1"])
+        ts(T.ot[:, 22:44], T.c2i[:], 9, 511, OP.arith_shift_right, OP.bitwise_and, ["c2i"], ["ot2"])
+        cp(T.zoff[:], T.ot[:], ["ot1", "ot2"], ["zoff"])
+
+        def zs(b, j0, j1, h):
+            act(T.tmp[:, A * b + j0:A * b + j1], plane(T.Ph, b).indirect(T.zoff[:, 22 + j0 // 16:22 + j1 // 16]),
+                AF.Copy, ["PhA%d" % b, "PhB%d" % b, "zoff"], ["tmp%s%d" % (h, b)])
+
+        def zv(b, j0, j1, h):
+            tt(T.Z[:, 4 * j0 + b:4 * j1:4], plane(T.Ph, b).indirect(T.zoff[:, j0 // 16:j1 // 16]),
+               T.tmp[:, A * b + j0:A * b + j1], OP.add, ["PhA%d" % b, "PhB%d" % b, "zoff", "tmp%s%d" % (h, b)], ["Z%s%d" % (h, b)])
+
+        def cmp_v(s):
+            ts(T.D0[:, A * s:A * s + A], T.Ar[:], T.jw[:, s:s + 1], 1024.0, OP.not_equal, OP.mult, ["Ar", "jw"], ["D0_%d" % s])
+
+        def cmp_s(s):
+            act(T.D0[:, A * s:A * s + A], T.Ar[:], AF.Abs, ["Ar", "nth"], ["D0_%d" % s], scale=1024.0, bias=T.nth[:, s:s + 1])
+
+        def hit(s):
+            scan(T.so2[:, A * s:A * s + A], T.D0[:, A * s:A * s + A], T.fd[:], float(2 * A - ZA), OP.min, OP.max,
+                 ["D0_%d" % s, "fdA", "fdB"], ["so2_%d" % s])
+        for b in range(4):
+            zs(b, 0, ZA, "A")
+        cp(T.Ar[:, ::-1], T.Awin[:].indirect(T.zoff[:, 0:22]), ["AwinA", "AwinB", "zoff"], ["Ar"])
+        for b in range(4):
+            zs(b, ZA, A, "B")
+        for b in range(4):
+            zv(b, 0, ZA, "A")
+        quant("Z", 0, ZA, T.Z[:, 0:4 * ZA], four("ZA"), "qZA")
+        for b in range(4):
+            mm(b, "L", 128 * b, "Z", 0, ZA, ["qL", "qZA"])
+        for b in range(4):
+            zv(b, ZA, A, "B")
+        quant("Z", ZA, A, T.Z[:, 4 * ZA:4 * A], four("ZB"), "qZB")
+        for b in range(4):
+            mm(4 + b, "L", 128 * b, "Z", ZA, A - ZA, ["qL", "qZB"])
+        nv = 8 - NSCMP
+        for s in range(nv, 8):
+            cmp_s(s)
+        for b in range(4):
+            act(T.Hs[:, 512 * b:512 * b + ZA], bank(b, ZA), AF.Copy, ["ps%d" % b], ["HA%d" % b], scale=0.03125)
+        for b in range(4):
+            act(T.Hs[:, 512 * b + ZA:512 * b + 2 * A - ZA:2], bank(4 + b, A - ZA), AF.Copy, ["ps%d" % (4 + b)], ["HB%d" % b],
+                scale=0.03125)
+        cmp_v(0)
+        for s in range(8):
+            if s + 1 < nv:
+                cmp_v(s + 1)
+            hit(s)
+        cp(T.foff[:], T.so2[:, A - 1:8 * A:A], ["so2_%d" % s for s in range(8)], ["foff"])
+        for b in (2, 3):
+            act(T.Vt[:, b:512:4], plane(T.Hs, b).indirect(T.foff[:]), AF.Copy, ["HA%d" % b, "HB%d" % b, "foff"], ["Vt%d" % b])
+        for b in (0, 1):
+            cp(T.Vt[:, b:512:4], plane(T.Hs, b).indirect(T.foff[:]), ["HA%d" % b, "HB%d" % b, "foff"], ["Vt%d" % b])
+        quant("V%d" % t, 0, K, T.Vt[:], four("Vt"))
+        send("V%d" % t, "H%d" % t, before, "arr%d" % (2 * t + 1))
+        for b in range(4):
+            act(T.Eq[:, K * b:K * b + K], T.E[:, b:512:4], AF.Copy, ["Ea", "Eb"], ["Eq%d" % b], scale=0.25)
+        ts(T.pre0[:], T.rank[:], float(K), None, OP.is_lt, None, ["rank"], ["pre0"])
+        tt(T.xb[:], T.rank[:], T.jw[:], OP.subtract, ["rank", "jw"], ["xb"])
+        ts(T.cc[:], T.c2i[:], 18, 3, OP.arith_shift_right, OP.bitwise_and, ["c2i"], ["cc"])
+        ts(T.pre[:], T.xb[:], float(C), None, OP.add, None, ["xb"], ["pre"])
+        tt(T.xb[:], T.pre[:], T.pre0[:], OP.mult, ["pre", "pre0"], ["xb"])
+        tt(T.pre[:], T.xb[:], T.jw[:], OP.add, ["xb", "jw"], ["pre"])
+        cp(T.xoff[:], T.pre[:], ["pre"], ["xoff"])
+        if t + 1 < R:
+            for i in range(4):
+                if t == 0:
+                    ts(T.P0[:, i:88:4], T.pay[:, 22 * i:22 * i + 22], float(i * 2 ** 18), None, OP.add, None, ["pay"], ["P0_%d" % i])
+                ts(T.ti[:, i:88:4], T.cc[:], float(3 - i), None, OP.add, None, ["cc"], ["ti%d" % i])
+            ts(T.cli[:], T.ti[:], 3, None, OP.bitwise_and, None, four("ti"), ["cli"])
+            ts(T.cand[:], T.cli[:], float(2 ** 20), None, OP.mult, None, ["cli"], ["cand"])
+            tt(T.base[:], T.cand[:], T.P0[:], OP.add, ["cand"] + four("P0_"), four("base"))
+        else:
+            cp(T.coff[:], T.cc[:], ["cc"], ["coff"])
+            act(T.owb[:], T.i16[:, 0:16].indirect(T.coff[:]), AF.Copy, ["i16", "coff"], ["owb"])
+            dma("Y", "dm9", [(T.ow[:], T.owb[0:128:16, :])], ["owb"], ())
+            quant("Vv", 0, 128, T.vb[:], ["vb"])
+        Hn = "H%d" % t
+        arrived(Hn, after, "arr%d" % (2 * t + 1))
+        for b in range(4):
+            mm(b, "I", 128 * b, Hn, 0, K, ["qI%d" % b, "q" + Hn])
+        for b in range(4):
+            tt(T.Ph[:, 512 * b + C:512 * b + 512], bank(b, K), T.Eq[:, K * b:K * b + K], OP.add, ["ps%d" % b, "Eq%d" % b], ["PhB%d" % b])
+        for b in (0, 1):
+            act(T.X[:, b:4 * C:4], plane(T.Ph, b).indirect(T.xoff[:]), AF.Copy, ["PhA%d" % b, "PhB%d" % b, "xoff"], ["X%d" % b], scale=2.0)
+        for b in (2, 3):
+            ts(T.X[:, b:4 * C:4], plane(T.Ph, b).indirect(T.xoff[:]), 2.0, None, OP.mult, None,
+               ["PhA%d" % b, "PhB%d" % b, "xoff"], ["X%d" % b])
+
+    quant("X", 0, C, T.X[:], XK)
+    h = C // 2
+    mm(0, "Vv", 0, "X", 0, h, ["qVv", "qX"])
+    mm(1, "Vv", 0, "X", h, h, ["qVv", "qX"])
+    dma("Y", "dm10", [(T.oc[:], T.qX[:].bitcast(dt.uint8))], ["qX"], ())
+    cp(T.yb[:, 0:h], bank(0, h), ["ps0"], ["yb0"])
+    act(T.yb[:, h:C], bank(1, h), AF.Copy, ["ps1"], ["yb1"])
+    dma("S", "dm11", [(T.y[:, h:C], T.yb[:, h:C])], ["yb1"], ())
+    dma("Y", "dm12", [(T.y[:, 0:h], T.yb[:, 0:h])], ["yb0"], ())
+    dma("S", "dm13", [(T.osc[4 * k:4 * k + 4, :], T.sX[32 * k:32 * k + 4, :]) for k in (0, 1)], ["qX"], ())
+    dma("Y", "dm14", [(T.osc[4 * k:4 * k + 4, :], T.sX[32 * k:32 * k + 4, :]) for k in (2, 3)], ["qX"], ())
+    need("G", {"sent": count["sent"]})
+    need("Y", {s_: v_ for s_, v_ in count.items() if s_ != "sent"})

@@ -1,12 +1,15 @@
 from concourse.mybir import dt, AluOpType as OP, ActivationFunctionType as AF
 
 C, K, A, R = 384, 128, 352, 3
+HC = C // 2
 ZA = 224
+MA = ZA // 16
+FB = 296
 BIG = float(2 ** 80)
 TOP = float(2 ** 22)
 MID = float(C // 2)
 NVROW = 7
-NSCMP = 4
+NSH = 2
 TW = [384, 320, 256, 192, 128, 128]
 TO = [0, 384, 704, 960, 1152, 1280]
 SOW = 184
@@ -14,19 +17,19 @@ SOW = 184
 
 def _scratch():
     s = {}
-    for n, w in dict(X=1536, ub=512, vb=512, E=512, Ph=2048, Eq=512, TT=5632, tau=2176, so=SOW * 8, dsc=384, rstb=384, Fl=512,
-                     Ft=1568, Z=1408, tmp=1408, Hs=2048, Vt=512, Ar=352, D0=2816, so2=2816, fd=352, Awin=512, cI=528, one=528,
+    for n, w in dict(X=1536, ub=512, vb=512, E=512, Ph=2048, Eq=512, TT=5632, tau=3072, so=SOW * 8, dsc=384, rstb=384, Fl=512,
+                     Ft=1408, Z=1408, tmp=1408, Hs=2048, Vt=512, D0=2816, so2=1408, fd=352, Awin=512, cI=528, one=528,
                      q25=528, cW=2048, cB=512, gm=512, M16=384, M16b=384, Rst=384, msk2=384, sc2=384, ew=384,
                      val=384, M4=128, Rst4=128, m4o=128, s4o=128).items():
         s[n] = ("sbuf", [128, w], "bfloat16")
-    for n, w in dict(i16=384, msk=384, sc=384, rowS=24, pre0=24, pre=24, cst=24, rank=24, jw=24, cf=8, cg=8, nth=8,
+    for n, w in dict(i16=384, msk=384, sc=384, rowS=24, pre0=24, pre=24, cst=24, rank=24, jw=24, cf=8, cg=8, nth=8, Ar=352,
                      Lf=112, P0=88, pay=88, base=88, cand=88, c1=44, xb=24, yb=384, owb=352).items():
         s[n] = ("sbuf", [128, w], "float32")
     for n, w in dict(pcol=1, ci=4, c2i=22, ot=44, cc=22, ti=88, cli=88, uoffi=8).items():
         s[n] = ("sbuf", [128, w], "int32")
-    for n, w in dict(uoff=8, roff=24, eoff=32, xoff=24, zoff=44, foff=8, flist=88, c2u=88, Lu=88, coff=22).items():
+    for n, w in dict(uoff=8, roff=24, eoff=32, xoff=24, zoff=44, foff=8, flist=88, c2u=176, Lu=88, coff=22).items():
         s[n] = ("sbuf", [128, w], "uint16")
-    pairs = dict(U=128, U2=128, Vv=128, X=384, T=1408, I=512, W=512, B=128, L=512, F=392, Z=352)
+    pairs = dict(U=128, U2=128, Vv=128, X=384, T=1408, I=512, W=512, B=128, L=512, F=520, Z=352)
     for t in range(R):
         for n in ("E", "G", "V", "H"):
             pairs[n + str(t)] = 128
@@ -40,7 +43,7 @@ def _scratch():
 
 
 SCRATCH = _scratch()
-SEMAPHORES = ["cV", "cS", "cP", "cG", "sent"] + ["arr%d" % i for i in range(2 * R)] + ["dm%d" % i for i in range(16)]
+SEMAPHORES = ["cV", "cS", "cP", "cG", "sent"] + ["arr%d" % i for i in range(2 * R)] + ["dm%d" % i for i in range(18)]
 
 
 def rank_program(g, core, T, topo):
@@ -51,8 +54,19 @@ def rank_program(g, core, T, topo):
     after, before = T.cores[(rank + 1) % n], T.cores[(rank - 1) % n]
     V, S, P, Y = g.vector, g.scalar, g.tensor, g.sync
     Q = {"V": V, "S": S, "P": P, "G": g, "Y": Y}
-    count, wrote, readers = {}, {}, {}
+    count, wrote, readers, knew = {}, {}, {}, {}
     waited = {q: {} for q in Q}
+
+    def need(q, deps):
+        w = waited[q]
+        todo = {s_: v_ for s_, v_ in deps.items() if w.get(s_, 0) < v_}
+        for sem, val in todo.items():
+            if any(o != sem and knew.get((o, ov), {}).get(sem, 0) >= val for o, ov in todo.items()):
+                continue
+            Q[q].wait_ge(T.sem[sem], val)
+        for sem, val in todo.items():
+            for s_, v_ in list(knew.get((sem, val), {}).items()) + [(sem, val)]:
+                w[s_] = max(w.get(s_, 0), v_)
 
     def issue(q, own, calls, inc, r, w, acc=False):
         deps = {}
@@ -72,17 +86,12 @@ def rank_program(g, core, T, topo):
         for call in calls:
             call().then_inc(T.sem[own], inc)
             count[own] = count.get(own, 0) + inc
+        knew[(own, count[own])] = dict(waited[q])
         for k in r:
             readers.setdefault(k, {})[own] = count[own]
         for k in w:
             wrote[k] = {own: count[own]}
             readers[k] = {}
-
-    def need(q, deps):
-        for sem, val in deps.items():
-            if waited[q].get(sem, 0) < val:
-                Q[q].wait_ge(T.sem[sem], val)
-                waited[q][sem] = val
 
     def op(q, call, r=(), w=(), acc=False):
         issue(q, "c" + q, [call], 1, r, w, acc)
@@ -90,8 +99,8 @@ def rank_program(g, core, T, topo):
     def dma(q, sem, pairs, r=(), w=()):
         issue(q, sem, [lambda o=o, i=i: Q[q].dma_start(o, i) for o, i in pairs], 16, r, w)
 
-    def bank(b, w):
-        return T.ps[:, 512 * b:512 * b + w]
+    def bank(b, w, a=0):
+        return T.ps[:, 512 * b + a:512 * b + w]
 
     def ts(out, in0, s1, s2, o0, o1, r, w):
         if o1 is None:
@@ -117,8 +126,14 @@ def rank_program(g, core, T, topo):
     def sfill(buf, a, b, c, w):
         act(buf[:, a:b], T.one[:, 0:b - a], AF.Copy, ["one"], w, scale=c)
 
+    def scaled(q, out, a, c, r, w):
+        if q == "S":
+            act(out, a, AF.Copy, r, w, scale=c)
+        else:
+            ts(out, a, c, None, OP.mult, None, r, w)
+
     def quant(name, a, b, src, r, key=None):
-        op("V", lambda: V.quantize_mx(T["q" + name][:, a:b], T["s" + name][:, a:b], src), r, [key or "q" + name])
+        op("V", lambda: V.quantize_mx(T["q" + name][:, a:b], T["s" + name][:, a:b], src), r, key or ["q" + name])
 
     def mm(b, st, sa, mv, ma, w, r, start=True, stop=True):
         op("P", lambda: P.matmul_mx(bank(b, w), T["q" + st][:, sa:sa + 128], T["s" + st][:, sa:sa + 128],
@@ -149,9 +164,11 @@ def rank_program(g, core, T, topo):
     def four(name):
         return [name + str(i) for i in range(4)]
 
-    XK = four("X")
+    XA, XB = four("XA"), four("XB")
+    XK = XA + XB
     dma("S", "dm0", [(T.ub[:], T.u[:])], (), ["ub"])
-    dma("Y", "dm1", [(T.X[:], T.x[:])], (), XK)
+    dma("Y", "dm1", [(T.X[:, 0:4 * HC], T.x[:, 0:4 * HC])], (), XA)
+    dma("Y", "dm15", [(T.X[:, 4 * HC:4 * C], T.x[:, 4 * HC:4 * C])], (), XB)
     dma("Y", "dm2", [(T.cli[:], T.cl[:])], (), ["cli"])
 
     k0 = 24 - NVROW
@@ -171,11 +188,8 @@ def rank_program(g, core, T, topo):
     fill(T.rstb[:, 0:C:16], 0.0, ["rstb"])
     fill(T.Rst4[:, 0:K:4], -BIG, ["Rst4"])
     sfill(T.q25, 0, 528, 0.25, ["q25"])
-    for m in range(6):
-        sfill(T.TT, 4 * (TO[m] + 16 * (21 - 4 * m)), 4 * (TO[m] + TW[m]), 0.0, four("T%d_" % m))
-    sfill(T.Ft, 1408, 1568, 0.0, ["FtP"])
-    for b in range(4):
-        sfill(T.Hs, 512 * b + ZA, 512 * b + 512, 0.0, ["HB%d" % b])
+    for m in range(5, -1, -1):
+        sfill(T.TT, 4 * (TO[m] + 16 * (21 - 4 * m)), 4 * (TO[m] + TW[m]), 0.0, four("T%d_" % m) + ["dg"] * (m == 0))
     where0(T.cI[:], T.q25[:], [[-1, 528]], 3, 4, ["q25"], ["cI"])
     for a in range(4):
         where0(T.cW[:, 512 * a:512 * a + 512], T.one[:, 0:512], [[-512, 8], [1, 16], [-1, 4]], -4 * a, 32, ["one"], ["cW%d" % a])
@@ -191,43 +205,52 @@ def rank_program(g, core, T, topo):
     ts(T.cg[:, 1:2], pr, -1.5, 15.0 + MID, OP.mult, OP.add, ["cf"], ["cg1"])
     ts(T.cg[:, 2:3], pt, 4 * MID, None, OP.add, None, ["cf"], ["cg2"])
     ts(T.M16[:], T.msk2[:], 2 * BIG, None, OP.mult, None, ["msk2"], ["M16"])
-    ts(T.M16b[:], T.msk2[:], 2 * BIG, -MID, OP.mult, OP.min, ["msk2"], ["M16b"])
-    ts(T.jw[:], T.pre0[:], pr, None, OP.add, None, ["pre0", "cf"], ["jw"])
-    ts(T.m4o[:], T.s4o[:], pq, 0.5, OP.is_equal, OP.subtract, ["s4o", "cf"], ["m4o"])
-    ts(T.cst[:, 0:k0], T.jw[:, 0:k0], T.cg[:, 0:1], None, OP.add, None, ["jw", "cg0"], ["cstA"])
-    ts(T.cst[:, k0:24], T.jw[:, k0:24], 0.5, T.cg[:, 1:2], OP.mult, OP.add, ["jw", "cg1"], ["cstB"])
-    ts(T.M4[:], T.m4o[:], 2 * BIG, None, OP.mult, None, ["m4o"], ["M4"])
     quant("U", 0, 128, T.ub[:], ["ub"])
+    ts(T.M16b[:], T.msk2[:], 2 * BIG, -MID, OP.mult, OP.min, ["msk2"], ["M16b"])
     cp(T.qU2[:].bitcast(dt.uint32), T.qU[:].bitcast(dt.uint32).indirect(T.uoff[:]), ["qU", "uoff"], ["qU2"])
     cp(T.sU2[:], T.sU[:].indirect(T.uoff[:]), ["qU", "uoff"], ["sU2"])
-    for a in range(4):
-        cp(T.c2u[:, 22 * a:22 * a + 22], T.cli[:, a:88:4], ["cli"], ["c2u%d" % a])
-    ts(T.cB[:], T.gm[:], pg, None, OP.is_equal, None, ["gm", "cf"], ["cB"])
-    dma("Y", "dm3", [(T.qL[:].bitcast(dt.uint8), T.wc[:]), (T.sL[:], T.ws[:])], XK, ["qL"])
-    dma("Y", "dm4", [(T.vb[:], T.v[:])], (), ["vb"])
-    dma("Y", "dm5", [(T.d1[:, i], T.c2u[i:128:4, :]) for i in range(4)], four("c2u"), ["d1"])
-    dma("Y", "dm6", [(T.d2[:, a], T.c2u[:, 22 * a:22 * a + 22]) for a in range(4)], four("c2u"), ["d2"])
-    dma("Y", "dm7", [(T.flist[:], T.d1[:])], ["d1"], ["flist"])
-    dma("Y", "dm8", [(T.Lu[:], T.d2[:])], ["d2"], ["Lu"])
+
+    def early():
+        ts(T.jw[:], T.pre0[:], pr, None, OP.add, None, ["pre0", "cf"], ["jw"])
+        ts(T.m4o[:], T.s4o[:], pq, 0.5, OP.is_equal, OP.subtract, ["s4o", "cf"], ["m4o"])
+        ts(T.cB[:], T.gm[:], pg, None, OP.is_equal, None, ["gm", "cf"], ["cB"])
+        ts(T.cst[:, 0:k0], T.jw[:, 0:k0], T.cg[:, 0:1], None, OP.add, None, ["jw", "cg0"], ["cstA"])
+        ts(T.cst[:, k0:24], T.jw[:, k0:24], 0.5, T.cg[:, 1:2], OP.mult, OP.add, ["jw", "cg1"], ["cstB"])
+        ts(T.M4[:], T.m4o[:], 2 * BIG, None, OP.mult, None, ["m4o"], ["M4"])
+
+    def lists():
+        for a in range(4):
+            cp(T.c2u[:, 22 * a:22 * a + 22], T.cli[:, a:88:4], ["cli"], ["c2u%d" % a])
+        quant("B", 0, 128, T.cB[:], ["cB"])
+        for a in range(4):
+            cp(T.c2u[:, 88 + MA * a:88 + MA * a + MA], T.c2u[:, 22 * a:22 * a + MA], ["c2u%d" % a], ["c2a%d" % a])
+            cp(T.c2u[:, 144 + 8 * a:152 + 8 * a], T.c2u[:, 22 * a + MA:22 * a + 22], ["c2u%d" % a], ["c2b%d" % a])
+        dma("Y", "dm3", [(T.qL[:].bitcast(dt.uint8), T.wc[:]), (T.sL[:], T.ws[:])], XK, ["qL"])
+        dma("Y", "dm4", [(T.vb[:], T.v[:])], (), ["vb"])
+        dma("Y", "dm6", [(T.d2[:, a], T.c2u[:, 22 * a:22 * a + 22]) for a in range(4)], four("c2u"), ["d2"])
+        dma("Y", "dm5", [(T.d1[:, i], T.c2u[i:128:4, 88:176]) for i in range(4)], four("c2a") + four("c2b"), ["d1"])
+        dma("Y", "dm8", [(T.Lu[:], T.d2[:])], ["d2"], ["Lu"])
+        dma("Y", "dm7", [(T.flist[:], T.d1[:])], ["d1"], ["flist"])
 
     def late():
-        iota(T.Awin[:, 0:C], [[0, C]], -1, 0, ["AwinA"])
-        iota(T.Awin[:, C:512], [[1, K]], 0, 0, ["AwinB"])
-        iota(T.fd[:, 0:A - ZA], [[-2, A - ZA]], 2 * (A - 1) - ZA, 0, ["fdA"])
-        iota(T.fd[:, A - ZA:A], [[-1, ZA]], ZA - 1, 0, ["fdB"])
+        iota(T.Awin[:, 0:C], [[0, C]], -1024, 0, ["AwinA"])
+        iota(T.Awin[:, C:512], [[1024, K]], 0, 0, ["AwinB"])
+        iota(T.fd[:, 0:ZA], [[1, ZA]], 0, 0, ["fdA"])
+        iota(T.fd[:, ZA:A], [[2, A - ZA]], ZA, 0, ["fdB"])
         cp(T.Lf[:, 0:88], T.Lu[:], ["Lu"], ["Lf"])
         cp(T.Lf[:, 88:110], T.Lu[:, 0:22], ["Lu"], ["Lf2"])
-        quant("I", 0, 128, T.cI[:, 3:515], ["cI"], "qI0")
-        ts(T.cand[:], T.Lf[:, 22:110], 512.0, None, OP.mult, None, ["Lf", "Lf2"], ["cand"])
-        quant("I", 128, 256, T.cI[:, 2:514], ["cI"], "qI1")
-        tt(T.pay[:], T.cand[:], T.Lf[:, 0:88], OP.add, ["cand", "Lf"], ["pay"])
-        quant("I", 256, 384, T.cI[:, 1:513], ["cI"], "qI2")
-        quant("I", 384, 512, T.cI[:, 0:512], ["cI"], "qI3")
+        quant("I", 0, 128, T.cI[:, 3:515], ["cI"], ["qI0"])
+        ts(T.cand[:], T.Lf[:, 22:110], 512.0, None, OP.mult, None, ["Lf", "Lf2"], ["candA", "candB"])
+        quant("I", 128, 256, T.cI[:, 2:514], ["cI"], ["qI1"])
+        tt(T.pay[:], T.cand[:], T.Lf[:, 0:88], OP.add, ["candA", "candB", "Lf"], ["pay"])
+        quant("I", 256, 384, T.cI[:, 1:513], ["cI"], ["qI2"])
+        quant("I", 384, 512, T.cI[:, 0:512], ["cI"], ["qI3"])
         quant("W", 0, 512, T.cW[:], four("cW"))
         for i in range(4):
             ts(T.base[:, i:88:4], T.pay[:, 22 * i:22 * i + 22], float(i * 2 ** 18 + (3 - i) * 2 ** 20), None, OP.add, None,
                ["pay"], ["base%d" % i])
-        act(T.nth[:], T.jw[:, 0:8], AF.Copy, ["jw"], ["nth"], scale=-1024.0)
+        quant("F", FB - 128, FB, T.Ft[:, 0:512], ["Fta"], ["qFA"])
+        quant("F", 392, 520, T.Ft[:, 0:512], ["Fta"], ["qFB"])
 
     def slot(k):
         return (24 - k) // 4, (24 - k) % 4
@@ -240,64 +263,138 @@ def rank_program(g, core, T, topo):
         return "T%d_%d" % slot(k)
 
     def tile_q(m, first, last):
-        quant("T", TO[m], TO[m] + TW[m], T.TT[:, 4 * TO[m]:4 * (TO[m] + TW[m])], four("T%d_" % m), "qT%d" % m)
+        quant("T", TO[m], TO[m] + TW[m], T.TT[:, 4 * TO[m]:4 * (TO[m] + TW[m])], four("T%d_" % m) + ["dg"] * (m == 0), ["qT%d" % m])
         mm(2, "B", 0, "T", TO[m], TW[m], ["qB", "qT%d" % m], first, last)
 
     def plane(buf, b):
         return buf[:, 512 * b:512 * b + 512]
 
-    for t in range(R):
-        quant("X", 0, C, T.X[:], XK)
-        mm(0, "U2", 0, "X", 0, C, ["qU2", "sU2", "qX"])
-        mm(1, "U2", 0, "X", 0, C, ["qU2", "sU2", "qX"])
+    def xnew(q, b, h):
+        scaled(q, T.X[:, 4 * HC * h + b:4 * HC * (h + 1):4], plane(T.Ph, b).indirect(T.xoff[:, 12 * h:12 * h + 12]), 2.0,
+               ["PhA%d" % b, "PhB%d" % b, "xoff"], ["X%s%d" % ("AB"[h], b)])
+
+    def s1(k):
+        o, b = 8 * k * (k - 1), 7 if k < 12 else 1
+        act(T.tau[:, o:o + 16 * k], bank(b, 16 * k), AF.Sign, ["ps%d" % b, "scA" if k < 12 else "scB"], ["tau%d" % k], scale=-1.0,
+            bias=T.sc[:, 16 * k + 15:16 * k + 16])
+
+    def s2(k):
+        o = 8 * k * (k - 1)
+        act(row_view(k, 0, 16 * k), T.tau[:, o:o + 16 * k], AF.Relu, ["tau%d" % k], [rkey(k), "row%d" % k], accum_out=T.rowS[:, k:k + 1])
+
+    def v1(k):
+        if k >= k0:
+            ts(row_view(k, 0, 16 * k), bank(0, 16 * k), T.sc[:, 16 * k + 15:16 * k + 16], None, OP.is_lt, None, ["ps0", "scB"], [rkey(k)])
+
+    def v2(k):
+        if k >= k0:
+            e = SOW * (k - k0 + 1)
+            scan(T.so[:, e - 8 * k:e], row_view(k, 0, 8 * k), row_view(k, 8 * k, 16 * k), float(-8 * k), OP.add, OP.add,
+                 [rkey(k)], ["so%d" % k])
+
+    PIECE = {"A": (0, MA, 2), "B": (MA, 22, 3)}
+
+    def cursor(h, step):
+        m0, m1, b = PIECE[h]
+        w = m1 - m0
+        if step == 0:
+            tt(T.cand[:, 4 * m0:4 * m1], bank(b, 4 * w), T.base[:, 4 * m0:4 * m1], OP.add, ["ps%d" % b] + four("base"), ["cand" + h])
+        if step == 1:
+            tt(T.c1[:, 2 * m0:2 * m1], T.cand[:, 4 * m0:4 * m1:2], T.cand[:, 4 * m0 + 1:4 * m1:2], OP.max, ["cand" + h], ["c1" + h])
+        if step == 2:
+            tt(T.c2i[:, m0:m1], T.c1[:, 2 * m0:2 * m1:2], T.c1[:, 2 * m0 + 1:2 * m1:2], OP.max, ["c1" + h], ["c2i" + h])
+        if step == 3:
+            ts(T.ot[:, 2 * m0:2 * m0 + w], T.c2i[:, m0:m1], 511, None, OP.bitwise_and, None, ["c2i" + h], ["ot1" + h])
+            ts(T.ot[:, 2 * m0 + w:2 * m1], T.c2i[:, m0:m1], 9, 511, OP.arith_shift_right, OP.bitwise_and, ["c2i" + h], ["ot2" + h])
+        if step == 4:
+            cp(T.zoff[:, 2 * m0:2 * m1], T.ot[:, 2 * m0:2 * m1], ["ot1" + h, "ot2" + h], ["zoff" + h])
+
+    def zs(b, h):
+        m0, m1, _ = PIECE[h]
+        act(T.tmp[:, A * b + 16 * m0:A * b + 16 * m1], plane(T.Ph, b).indirect(T.zoff[:, m0 + m1:2 * m1]),
+            AF.Copy, ["PhA%d" % b, "PhB%d" % b, "zoff" + h], ["tmp%s%d" % (h, b)])
+
+    def zv(b, h):
+        m0, m1, _ = PIECE[h]
+        tt(T.Z[:, 64 * m0 + b:64 * m1:4], plane(T.Ph, b).indirect(T.zoff[:, 2 * m0:m0 + m1]), T.tmp[:, A * b + 16 * m0:A * b + 16 * m1],
+           OP.add, ["PhA%d" % b, "PhB%d" % b, "zoff" + h, "tmp%s%d" % (h, b)], ["Z%s%d" % (h, b)])
+
+    def keys(h):
+        m0, m1, _ = PIECE[h]
+        tt(T.Ar[:, 16 * m0:16 * m1], T.Awin[:].indirect(T.zoff[:, 2 * m0:m0 + m1]), T.fd[:, 16 * m0:16 * m1], OP.add,
+           ["AwinA", "AwinB", "fd" + h, "zoff" + h], ["Ar" + h])
+
+    def hit(s):
+        scan(T.so2[:, A // 2 * s:A // 2 * (s + 1)], T.D0[:, A * s:A * s + A // 2], T.D0[:, A * s + A // 2:A * s + A],
+             float(2 * A - ZA), OP.min, OP.min, ["D0_%d" % s], ["so2_%d" % s])
+
+    def hb(q, b):
+        scaled(q, T.Hs[:, 512 * b + ZA:512 * b + 2 * A - ZA:2], bank(4 + b, A - ZA), 0.03125, ["ps%d" % (4 + b)], ["HB%d" % b])
+
+    UK = ["qU2", "sU2"]
+    for t in range(R + 1):
+        if t > 0:
+            Hn = "H%d" % (t - 1)
+            arrived(Hn, after, "arr%d" % (2 * t - 1))
+            for b in range(4):
+                mm(b, "I", 128 * b, Hn, 0, K, ["qI%d" % b, "q" + Hn])
+            for b in range(4):
+                tt(T.Ph[:, 512 * b + C:512 * b + 512], bank(b, K), T.Eq[:, K * b:K * b + K], OP.add, ["ps%d" % b, "Eq%d" % b],
+                   ["PhB%d" % b])
+            for q, b, h in (("S", 0, 0), ("S", 1, 0), ("V", 2, 0), ("V", 3, 0), ("S", 0, 1), ("S", 1, 1), ("S", 2, 1)):
+                xnew(q, b, h)
+        quant("X", 0, HC, T.X[:, 0:4 * HC], XA, ["qXA"])
+        if t == R:
+            break
+        mm(6, "U2", 0, "X", 0, HC, UK + ["qXA"])
+        mm(7, "U2", 0, "X", 0, HC, UK + ["qXA"])
+        if t > 0:
+            xnew("V", 3, 1)
+        else:
+            early()
+        tt(T.msk[:, 0:HC], bank(6, HC), T.M16[:, 0:HC], OP.min, ["ps6", "M16"], ["mskA"])
+        quant("X", HC, C, T.X[:, 4 * HC:4 * C], XB, ["qXB"])
+        mm(0, "U2", 0, "X", 0, C, UK + ["qXA", "qXB"])
+        mm(1, "U2", 0, "X", 0, C, UK + ["qXA", "qXB"])
+        scan(T.sc[:, 0:HC], T.Rst[:, 0:HC], T.msk[:, 0:HC], -BIG, OP.min, OP.max, ["Rst", "mskA"], ["scA"])
         if t == 0:
-            quant("B", 0, 128, T.cB[:], ["cB"])
-        tt(T.msk[:], bank(0, C), T.M16[:], OP.min, ["ps0", "M16"], ["msk"])
-        scan(T.sc[:], T.Rst[:], T.msk[:], -BIG, OP.min, OP.max, ["Rst", "msk"], ["sc"])
-        srows = list(range(k0 - 1, 0, -1))
-
-        def s1(k):
-            o = 8 * k * (k - 1)
-            act(T.tau[:, o:o + 16 * k], bank(1, 16 * k), AF.Sign, ["ps1", "sc"], ["tau%d" % k], scale=-1.0,
-                bias=T.sc[:, 16 * k + 15:16 * k + 16])
-
-        def s2(k):
-            o = 8 * k * (k - 1)
-            act(row_view(k, 0, 16 * k), T.tau[:, o:o + 16 * k], AF.Relu, ["tau%d" % k], [rkey(k), "row%d" % k],
-                accum_out=T.rowS[:, k:k + 1])
+            lists()
+        tt(T.msk[:, HC:C], bank(0, C, HC), T.M16[:, HC:C], OP.min, ["ps0", "M16"], ["mskB"])
+        tt(row_view(24, 0, HC), bank(6, HC), T.sc[:, 0:HC], OP.is_le, ["ps6", "scA"], ["dg"])
+        scan(T.sc[:, HC:C], T.Rst[:, HC:C], T.msk[:, HC:C], -BIG, OP.min, OP.max, ["Rst", "mskB"], ["scB"])
+        srows = list(range(11, 0, -1)) + list(range(k0 - 1, 11, -1))
         s1(srows[0])
         for i, k in enumerate(srows):
             if i + 1 < len(srows):
                 s1(srows[i + 1])
             s2(k)
-
-        def v1(k):
-            ts(row_view(k, 0, 16 * k), bank(0, 16 * k), T.sc[:, 16 * k + 15:16 * k + 16], None, OP.is_lt, None, ["ps0", "sc"], [rkey(k)])
-
-        def v2(k):
-            e = SOW * (k - k0 + 1)
-            scan(T.so[:, e - 8 * k:e], row_view(k, 0, 8 * k), row_view(k, 8 * k, 16 * k), float(-8 * k), OP.add, OP.add,
-                 [rkey(k)], ["so%d" % k])
-        tt(row_view(24, 0, C), bank(0, C), T.sc[:], OP.is_le, ["ps0", "sc"], [rkey(24)])
         v1(23); v1(22); v1(21)
-        scan(T.dsc[:], T.rstb[:], row_view(24, 0, C), 0.0, OP.mult, OP.add, ["rstb", rkey(24)], ["dsc"])
+        tt(row_view(24, HC, C), bank(0, C, HC), T.sc[:, HC:C], OP.is_le, ["ps0", "scB"], [rkey(24)])
+        v2(23); v2(22)
         tile_q(0, True, False)
-        v1(20); v2(23); v1(19); v2(22)
-        tile_q(2, False, False)
-        v1(18); v2(21); v1(17); v2(20)
-        tile_q(3, False, False)
-        tile_q(1, False, False)
-        v2(19); v2(18)
+        v1(20); v2(21)
         tile_q(4, False, False)
-        v2(17)
+        v1(19)
+        scan(T.dsc[:], T.rstb[:], row_view(24, 0, C), 0.0, OP.mult, OP.add, ["rstb", rkey(24), "dg"], ["dsc"])
+        tile_q(5, False, False)
+        v1(18); v1(17); v2(20); v2(19)
+        tile_q(1, False, False)
+        tile_q(2, False, False)
+        tile_q(3, False, True)
+        v2(18); v2(17)
         tt(T.pre0[:], T.cst[:], T.dsc[:, 15:C:16], OP.subtract, ["cstA", "cstB", "dsc"], ["pre0"])
         cp(T.rowS[:, k0:24], T.so[:, SOW - 1:SOW * NVROW:SOW], ["so%d" % k for k in range(k0, 24)], ["rowV"])
-        tile_q(5, False, True)
-        tt(T.pre[:], T.pre0[:], T.rowS[:], OP.subtract, ["pre0", "rowV"] + ["row%d" % k for k in range(k0)], ["pre"])
         tt(T.msk2[:], bank(2, C), T.M16b[:], OP.add, ["ps2", "M16b"], ["msk2"])
+        tt(T.pre[:], T.pre0[:], T.rowS[:], OP.subtract, ["pre0", "rowV"] + ["row%d" % k for k in range(k0)], ["pre"])
         scan(T.sc2[:], T.Rst[:], T.msk2[:], -BIG, OP.min, OP.max, ["Rst", "msk2"], ["sc2"])
         tt(T.rank[:], T.pre[:], T.sc2[:, 15:C:16], OP.add, ["pre", "sc2"], ["rank"])
         cp(T.roff[:], T.rank[:], ["rank"], ["roff"])
+        for b in range(4):
+            scaled("S", T.Ph[:, 512 * b:512 * b + C], T.X[:, b:4 * C:4], 0.5, XK, ["PhA%d" % b])
+        act(T.Fl[:, 0:C], bank(1, C), AF.Sign, ["ps1"], ["FlS"])
+        if t == 0:
+            sfill(T.Ft, 0, 512, 0.0, ["Fta"])
+        act(T.Fl[:, 0:C], T.Fl[:, 0:C], AF.Relu, ["FlS"], ["FlA"], scale=TOP)
         cp(T.ew[:].indirect(T.roff[:]), T.val[:], ["roff", "val"], ["ew"])
         tt(T.m4o[:], T.ew[:, 0:K], T.M4[:], OP.min, ["ew", "M4"], ["m4o"])
         scan(T.s4o[:], T.Rst4[:], T.m4o[:], -BIG, OP.min, OP.max, ["Rst4", "m4o"], ["s4o"])
@@ -307,130 +404,107 @@ def rank_program(g, core, T, topo):
         quant("E%d" % t, 0, K, T.E[:], ["Ea", "Eb"])
         send("E%d" % t, "G%d" % t, after, "arr%d" % (2 * t))
         if t == 0:
+            act(T.nth[:], T.jw[:, 0:8], AF.Copy, ["jw"], ["nth"], scale=-1024.0)
+            for b in range(4):
+                sfill(T.Hs, 512 * b + ZA, 512 * b + 512, 0.0, ["HB%d" % b])
             late()
-        ts(T.Fl[:, 0:C], bank(0, C), 0.0, TOP, OP.is_gt, OP.mult, ["ps0"], ["FlA"])
-        for b in range(4):
-            if b < 2 or t == 0:
-                act(T.Ph[:, 512 * b:512 * b + C], T.X[:, b:4 * C:4], AF.Copy, XK, ["PhA%d" % b], scale=0.5)
-            else:
-                ts(T.Ph[:, 512 * b:512 * b + C], T.X[:, b:4 * C:4], 0.5, None, OP.mult, None, XK, ["PhA%d" % b])
         Gn = "G%d" % t
+        FK = ["FlS", "FlA", "FlB", "flist"]
         arrived(Gn, before, "arr%d" % (2 * t))
-        mm(3, "U2", 0, Gn, 0, K, ["qU2", "sU2", "q" + Gn])
+        mm(3, "U2", 0, Gn, 0, K, UK + ["q" + Gn])
         for b in range(4):
             mm(4 + b, "I", 128 * b, Gn, 0, K, ["qI%d" % b, "q" + Gn])
         ts(T.Fl[:, C:512], bank(3, K), 0.0, TOP, OP.is_gt, OP.mult, ["ps3"], ["FlB"])
-        act(T.Ft[:, 704:1408], T.Fl[:].indirect(T.flist[:, 44:88]), AF.Copy, ["FlA", "FlB", "flist"], ["Ftb"])
-        cp(T.Ft[:, 0:704], T.Fl[:].indirect(T.flist[:, 0:44]), ["FlA", "FlB", "flist"], ["Fta"])
-        quant("F", 0, 176, T.Ft[:, 0:704], ["Fta"], "qFa")
-        quant("F", 176, 392, T.Ft[:, 704:1568], ["Ftb", "FtP"], "qFb")
-        for b in range(4):
-            act(T.Ph[:, 512 * b + C:512 * b + 512], bank(4 + b, K), AF.Copy, ["ps%d" % (4 + b)], ["PhB%d" % b], scale=2.0)
+        act(T.Ft[:, 512:896], T.Fl[:].indirect(T.flist[:, 32:56]), AF.Copy, FK, ["Ftb"])
+        cp(T.Ft[:, 0:512], T.Fl[:].indirect(T.flist[:, 0:32]), FK, ["Fta"])
+        act(T.Ft[:, 896:1408], T.Fl[:].indirect(T.flist[:, 56:88]), AF.Copy, FK, ["Ftc"])
+        quant("F", 0, ZA, T.Ft[:, 0:896], ["Fta", "Ftb"], ["qFA"])
         for a in range(4):
-            mm(2, "W", 128 * a, "F", 88 * a, 128, ["qW", "qFa"] + (["qFb"] if a else []), a == 0, a == 3)
-        tt(T.cand[:], bank(2, 88), T.base[:], OP.add, ["ps2"] + four("base"), ["cand"])
-        tt(T.c1[:], T.cand[:, 0:88:2], T.cand[:, 1:88:2], OP.max, ["cand"], ["c1"])
-        tt(T.c2i[:], T.c1[:, 0:44:2], T.c1[:, 1:44:2], OP.max, ["c1"], ["c2i"])
-        ts(T.ot[:, 0:22], T.c2i[:], 511, None, OP.bitwise_and, None, ["c2i"], ["ot1"])
-        ts(T.ot[:, 22:44], T.c2i[:], 9, 511, OP.arith_shift_right, OP.bitwise_and, ["c2i"], ["ot2"])
-        cp(T.zoff[:], T.ot[:], ["ot1", "ot2"], ["zoff"])
-
-        def zs(b, j0, j1, h):
-            act(T.tmp[:, A * b + j0:A * b + j1], plane(T.Ph, b).indirect(T.zoff[:, 22 + j0 // 16:22 + j1 // 16]),
-                AF.Copy, ["PhA%d" % b, "PhB%d" % b, "zoff"], ["tmp%s%d" % (h, b)])
-
-        def zv(b, j0, j1, h):
-            tt(T.Z[:, 4 * j0 + b:4 * j1:4], plane(T.Ph, b).indirect(T.zoff[:, j0 // 16:j1 // 16]),
-               T.tmp[:, A * b + j0:A * b + j1], OP.add, ["PhA%d" % b, "PhB%d" % b, "zoff", "tmp%s%d" % (h, b)], ["Z%s%d" % (h, b)])
-
-        def cmp_v(s):
-            ts(T.D0[:, A * s:A * s + A], T.Ar[:], T.jw[:, s:s + 1], 1024.0, OP.not_equal, OP.mult, ["Ar", "jw"], ["D0_%d" % s])
-
-        def cmp_s(s):
-            act(T.D0[:, A * s:A * s + A], T.Ar[:], AF.Abs, ["Ar", "nth"], ["D0_%d" % s], scale=1024.0, bias=T.nth[:, s:s + 1])
-
-        def hit(s):
-            scan(T.so2[:, A * s:A * s + A], T.D0[:, A * s:A * s + A], T.fd[:], float(2 * A - ZA), OP.min, OP.max,
-                 ["D0_%d" % s, "fdA", "fdB"], ["so2_%d" % s])
+            mm(2, "W", 128 * a, "F", 4 * MA * a, 128, ["qW", "qFA"], a == 0, a == 3)
         for b in range(4):
-            zs(b, 0, ZA, "A")
-        cp(T.Ar[:, ::-1], T.Awin[:].indirect(T.zoff[:, 0:22]), ["AwinA", "AwinB", "zoff"], ["Ar"])
-        for b in range(4):
-            zs(b, ZA, A, "B")
-        for b in range(4):
-            zv(b, 0, ZA, "A")
-        quant("Z", 0, ZA, T.Z[:, 0:4 * ZA], four("ZA"), "qZA")
+            scaled("S", T.Ph[:, 512 * b + C:512 * b + 512], bank(4 + b, K), 2.0, ["ps%d" % (4 + b)], ["PhB%d" % b])
+        quant("F", FB, FB + 128, T.Ft[:, 896:1408], ["Ftc"], ["qFB"])
+        for a in range(4):
+            mm(3, "W", 128 * a, "F", FB + 32 * a, 128, ["qW", "qFB"], a == 0, a == 3)
+        for h, step in (("A", 0), ("A", 1), ("B", 0), ("A", 2), ("B", 1), ("A", 3), ("B", 2), ("A", 4), ("B", 3), ("B", 4)):
+            cursor(h, step)
+        for h in "AB":
+            for b in range(4):
+                zs(b, h)
+        keys("A")
+        zv(0, "A")
+        keys("B")
+        for s in range(8):
+            act(T.D0[:, A * s:A * s + A], T.Ar[:], AF.Abs, ["ArA", "ArB", "nth"], ["D0_%d" % s], bias=T.nth[:, s:s + 1])
+        for b in range(1, 4):
+            zv(b, "A")
+        zv(0, "B")
+        quant("Z", 0, ZA, T.Z[:, 0:4 * ZA], four("ZA"), ["qZA"])
         for b in range(4):
             mm(b, "L", 128 * b, "Z", 0, ZA, ["qL", "qZA"])
-        for b in range(4):
-            zv(b, ZA, A, "B")
-        quant("Z", ZA, A, T.Z[:, 4 * ZA:4 * A], four("ZB"), "qZB")
+        for b in range(1, 4):
+            zv(b, "B")
+        scaled("V", T.Hs[:, 0:ZA], bank(0, ZA), 0.03125, ["ps0"], ["HA0"])
+        quant("Z", ZA, A, T.Z[:, 4 * ZA:4 * A], four("ZB"), ["qZB"])
         for b in range(4):
             mm(4 + b, "L", 128 * b, "Z", ZA, A - ZA, ["qL", "qZB"])
-        nv = 8 - NSCMP
-        for s in range(nv, 8):
-            cmp_s(s)
-        for b in range(4):
-            act(T.Hs[:, 512 * b:512 * b + ZA], bank(b, ZA), AF.Copy, ["ps%d" % b], ["HA%d" % b], scale=0.03125)
-        for b in range(4):
-            act(T.Hs[:, 512 * b + ZA:512 * b + 2 * A - ZA:2], bank(4 + b, A - ZA), AF.Copy, ["ps%d" % (4 + b)], ["HB%d" % b],
-                scale=0.03125)
-        cmp_v(0)
-        for s in range(8):
-            if s + 1 < nv:
-                cmp_v(s + 1)
+        for b in range(NSH):
+            hb("S", b)
+        for b in range(1, 4):
+            scaled("V", T.Hs[:, 512 * b:512 * b + ZA], bank(b, ZA), 0.03125, ["ps%d" % b], ["HA%d" % b])
+        for s in range(4):
             hit(s)
-        cp(T.foff[:], T.so2[:, A - 1:8 * A:A], ["so2_%d" % s for s in range(8)], ["foff"])
-        for b in (2, 3):
-            act(T.Vt[:, b:512:4], plane(T.Hs, b).indirect(T.foff[:]), AF.Copy, ["HA%d" % b, "HB%d" % b, "foff"], ["Vt%d" % b])
+        hb("V", 3)
+        for s in range(4, 8):
+            hit(s)
+        hb("V", 2)
+        cp(T.foff[:], T.so2[:, A // 2 - 1:4 * A:A // 2], ["so2_%d" % s for s in range(8)], ["foff"])
         for b in (0, 1):
+            act(T.Vt[:, b:512:4], plane(T.Hs, b).indirect(T.foff[:]), AF.Copy, ["HA%d" % b, "HB%d" % b, "foff"], ["Vt%d" % b])
+        for b in (3, 2):
             cp(T.Vt[:, b:512:4], plane(T.Hs, b).indirect(T.foff[:]), ["HA%d" % b, "HB%d" % b, "foff"], ["Vt%d" % b])
         quant("V%d" % t, 0, K, T.Vt[:], four("Vt"))
         send("V%d" % t, "H%d" % t, before, "arr%d" % (2 * t + 1))
         for b in range(4):
-            act(T.Eq[:, K * b:K * b + K], T.E[:, b:512:4], AF.Copy, ["Ea", "Eb"], ["Eq%d" % b], scale=0.25)
+            scaled("S", T.Eq[:, K * b:K * b + K], T.E[:, b:512:4], 0.25, ["Ea", "Eb"], ["Eq%d" % b])
         ts(T.pre0[:], T.rank[:], float(K), None, OP.is_lt, None, ["rank"], ["pre0"])
         tt(T.xb[:], T.rank[:], T.jw[:], OP.subtract, ["rank", "jw"], ["xb"])
-        ts(T.cc[:], T.c2i[:], 18, 3, OP.arith_shift_right, OP.bitwise_and, ["c2i"], ["cc"])
+        ts(T.cc[:], T.c2i[:], 18, 3, OP.arith_shift_right, OP.bitwise_and, ["c2iA", "c2iB"], ["cc"])
         ts(T.pre[:], T.xb[:], float(C), None, OP.add, None, ["xb"], ["pre"])
-        tt(T.xb[:], T.pre[:], T.pre0[:], OP.mult, ["pre", "pre0"], ["xb"])
-        tt(T.pre[:], T.xb[:], T.jw[:], OP.add, ["xb", "jw"], ["pre"])
-        cp(T.xoff[:], T.pre[:], ["pre"], ["xoff"])
         if t + 1 < R:
             for i in range(4):
-                if t == 0:
-                    ts(T.P0[:, i:88:4], T.pay[:, 22 * i:22 * i + 22], float(i * 2 ** 18), None, OP.add, None, ["pay"], ["P0_%d" % i])
                 ts(T.ti[:, i:88:4], T.cc[:], float(3 - i), None, OP.add, None, ["cc"], ["ti%d" % i])
+        tt(T.xb[:], T.pre[:], T.pre0[:], OP.mult, ["pre", "pre0"], ["xb"])
+        if t + 1 < R:
             ts(T.cli[:], T.ti[:], 3, None, OP.bitwise_and, None, four("ti"), ["cli"])
-            ts(T.cand[:], T.cli[:], float(2 ** 20), None, OP.mult, None, ["cli"], ["cand"])
-            tt(T.base[:], T.cand[:], T.P0[:], OP.add, ["cand"] + four("P0_"), four("base"))
+        tt(T.pre[:], T.xb[:], T.jw[:], OP.add, ["xb", "jw"], ["pre"])
+        if t + 1 < R:
+            ts(T.cand[:], T.cli[:], float(2 ** 20), None, OP.mult, None, ["cli"], ["candA", "candB"])
+        cp(T.xoff[:], T.pre[:], ["pre"], ["xoff"])
+        if t + 1 < R:
+            if t == 0:
+                for i in range(4):
+                    ts(T.P0[:, i:88:4], T.pay[:, 22 * i:22 * i + 22], float(i * 2 ** 18), None, OP.add, None, ["pay"], ["P0_%d" % i])
+            tt(T.base[:], T.cand[:], T.P0[:], OP.add, ["candA", "candB"] + four("P0_"), four("base"))
         else:
             cp(T.coff[:], T.cc[:], ["cc"], ["coff"])
             act(T.owb[:], T.i16[:, 0:16].indirect(T.coff[:]), AF.Copy, ["i16", "coff"], ["owb"])
             dma("Y", "dm9", [(T.ow[:], T.owb[0:128:16, :])], ["owb"], ())
             quant("Vv", 0, 128, T.vb[:], ["vb"])
-        Hn = "H%d" % t
-        arrived(Hn, after, "arr%d" % (2 * t + 1))
-        for b in range(4):
-            mm(b, "I", 128 * b, Hn, 0, K, ["qI%d" % b, "q" + Hn])
-        for b in range(4):
-            tt(T.Ph[:, 512 * b + C:512 * b + 512], bank(b, K), T.Eq[:, K * b:K * b + K], OP.add, ["ps%d" % b, "Eq%d" % b], ["PhB%d" % b])
-        for b in (0, 1):
-            act(T.X[:, b:4 * C:4], plane(T.Ph, b).indirect(T.xoff[:]), AF.Copy, ["PhA%d" % b, "PhB%d" % b, "xoff"], ["X%d" % b], scale=2.0)
-        for b in (2, 3):
-            ts(T.X[:, b:4 * C:4], plane(T.Ph, b).indirect(T.xoff[:]), 2.0, None, OP.mult, None,
-               ["PhA%d" % b, "PhB%d" % b, "xoff"], ["X%d" % b])
 
-    quant("X", 0, C, T.X[:], XK)
-    h = C // 2
-    mm(0, "Vv", 0, "X", 0, h, ["qVv", "qX"])
-    mm(1, "Vv", 0, "X", h, h, ["qVv", "qX"])
-    dma("Y", "dm10", [(T.oc[:], T.qX[:].bitcast(dt.uint8))], ["qX"], ())
-    cp(T.yb[:, 0:h], bank(0, h), ["ps0"], ["yb0"])
-    act(T.yb[:, h:C], bank(1, h), AF.Copy, ["ps1"], ["yb1"])
-    dma("S", "dm11", [(T.y[:, h:C], T.yb[:, h:C])], ["yb1"], ())
-    dma("Y", "dm12", [(T.y[:, 0:h], T.yb[:, 0:h])], ["yb0"], ())
-    dma("S", "dm13", [(T.osc[4 * k:4 * k + 4, :], T.sX[32 * k:32 * k + 4, :]) for k in (0, 1)], ["qX"], ())
-    dma("Y", "dm14", [(T.osc[4 * k:4 * k + 4, :], T.sX[32 * k:32 * k + 4, :]) for k in (2, 3)], ["qX"], ())
+    mm(6, "Vv", 0, "X", 0, HC, ["qVv", "qXA"])
+    dma("Y", "dm10", [(T.oc[:, 0:4 * HC], T.qX[:, 0:HC].bitcast(dt.uint8))], ["qXA"], ())
+    xnew("V", 3, 1)
+    act(T.yb[:, 0:HC], bank(6, HC), AF.Copy, ["ps6"], ["yb0"])
+    quant("X", HC, C, T.X[:, 4 * HC:4 * C], XB, ["qXB"])
+    mm(7, "Vv", 0, "X", HC, HC, ["qVv", "qXB"])
+    dma("S", "dm11", [(T.y[:, 0:HC], T.yb[:, 0:HC])], ["yb0"], ())
+    dma("Y", "dm16", [(T.oc[:, 4 * HC:4 * C], T.qX[:, HC:C].bitcast(dt.uint8))], ["qXB"], ())
+    cp(T.yb[:, HC:C], bank(7, HC), ["ps7"], ["yb1"])
+    dma("S", "dm13", [(T.osc[4 * k:4 * k + 4, :], T.sX[32 * k:32 * k + 4, :]) for k in range(3)], ["qXA", "qXB"], ())
+    dma("Y", "dm14", [(T.osc[12:16, :], T.sX[96:100, :])], ["qXA", "qXB"], ())
+    dma("Y", "dm12", [(T.y[:, HC:C], T.yb[:, HC:C])], ["yb1"], ())
     need("G", {"sent": count["sent"]})
-    need("Y", {s_: v_ for s_, v_ in count.items() if s_ != "sent"})
+    for s_, v_ in count.items():
+        if s_ != "sent":
+            Y.wait_ge(T.sem[s_], v_)

@@ -1,49 +1,111 @@
 from concourse.mybir import dt, AluOpType as OP, ActivationFunctionType as AF
 
 C, K, A, R = 384, 128, 352, 3
-HC = C // 2
+XP = [(0, 192), (192, 384)]
+ZP = [(0, 14), (14, 22)]
+FP = [(0, 28), (28, 56), (56, 88)]
+KH = 18
 ZA = 224
-MA = ZA // 16
-FB = 296
 BIG = float(2 ** 80)
 TOP = float(2 ** 22)
-MID = float(C // 2)
-NVROW = 7
-NSH = 2
-TW = [384, 320, 256, 192, 128, 128]
+LIFT = 2 * TOP
+APART = 7 * 1024
+ON = dict(su="S", e="SSVV", eq="SSSS", x="SSVVSSSV", ph="SSSS", fl="VSS", phb="SSSS", z="SSSSSSSS", h="SSSVSVVV", vt="SSVV")
+ROWS = "V" * 4 + "S" * 13 + "V" * 6
+TW = [384, 320, 256, 192, 128, 64]
 TO = [0, 384, 704, 960, 1152, 1280]
 SOW = 184
+STEP = 1024.0
+CYC, GA, SC, SAME, OTHER, LOAD, TRIP = 0.83, 1.3, 3.1, 205.0, 205.0, 1900.0, 1500.0
+FIRST = 800.0
+LEAST, FIXED = dict(V=35.0, S=90.0), dict(V=30.0, S=20.0)
+TURNS = 5000
+LAID = []
+
+MASKS = dict(i16=208, w16=32, v16=32, M16=192, Rst=192, rstb=384, MF=512)
+PART = {n: ("masks", sum(list(MASKS.values())[:i]), w) for i, (n, w) in enumerate(MASKS.items())}
 
 
 def _scratch():
-    s = {}
-    for n, w in dict(X=1536, ub=512, vb=512, E=512, Ph=2048, Eq=512, TT=5632, tau=3072, so=SOW * 8, dsc=384, rstb=384, Fl=512,
+    s = {"masks": ("sbuf", [128, sum(MASKS.values())], "bfloat16")}
+    for n, w in dict(X=1536, ub=512, vb=512, E=512, Ph=2048, Eq=512, TT=5632, tau=4416, so=SOW * 24, dsc=384, Fl=512,
                      Ft=1408, Z=1408, tmp=1408, Hs=2048, Vt=512, D0=2816, so2=1408, fd=352, Awin=512, cI=528, one=528,
-                     q25=528, cW=2048, cB=512, gm=512, M16=384, M16b=384, Rst=384, msk2=384, sc2=384, ew=384,
-                     val=384, M4=128, Rst4=128, m4o=128, s4o=128).items():
+                     q25=528, cB=512, gm=512, Fs=1408).items():
         s[n] = ("sbuf", [128, w], "bfloat16")
-    for n, w in dict(i16=384, msk=384, sc=384, rowS=24, pre0=24, pre=24, cst=24, rank=24, jw=24, cf=8, cg=8, nth=8, Ar=352,
-                     Lf=112, P0=88, pay=88, base=88, cand=88, c1=44, xb=24, yb=384, owb=352).items():
+    for n, w in dict(n16=16, msk=384, sc=384, sc2=384, ew=384, val=384, s4o=128, eq=16, rowS=24, k16=24, pre0=24, MR=384, cst=24,
+                     rank=24, jw=24, cf=8, cg=8, Ar=352, Lf=112, P0=88, pay=88, base=88, cand=88, c1=44, xs=72,
+                     prio=88, yb=384, owb=352).items():
         s[n] = ("sbuf", [128, w], "float32")
-    for n, w in dict(pcol=1, ci=4, c2i=22, ot=44, cc=22, ti=88, cli=88, uoffi=8).items():
+    for n, w in dict(pcol=1, ci=2, c2i=22, ot=44, cc=22, ti=176, cli=88, uoffi=8).items():
         s[n] = ("sbuf", [128, w], "int32")
-    for n, w in dict(uoff=8, roff=24, eoff=32, xoff=24, zoff=44, foff=8, flist=88, c2u=176, Lu=88, coff=22).items():
+    for n, w in dict(uoff=8, roff=24, eoff=8, xoff=24, zoff=44, foff=8, flist=88, c2u=88, Lu=88, coff=22).items():
         s[n] = ("sbuf", [128, w], "uint16")
-    pairs = dict(U=128, U2=128, Vv=128, X=384, T=1408, I=512, W=512, B=128, L=512, F=520, Z=352)
+    pairs = dict(U=128, U2=128, Vv=128, X=384, T=1408, I=512, B=128, L=512, Z=352)
     for t in range(R):
         for n in ("E", "G", "V", "H"):
             pairs[n + str(t)] = 128
     for n, w in pairs.items():
         s["q" + n] = ("sbuf", [128, w], "float8_e4m3fn_x4")
         s["s" + n] = ("sbuf", [128, w], "uint8")
-    s["d1"] = ("dram", [8, 4, 4, 88], "uint16")
     s["d2"] = ("dram", [8, 4, 4, 4, 22], "uint16")
     s["ps"] = ("psum", [128, 4096], "float32")
     return s
 
 
 SCRATCH = _scratch()
-SEMAPHORES = ["cV", "cS", "cP", "cG", "sent"] + ["arr%d" % i for i in range(2 * R)] + ["dm%d" % i for i in range(18)]
+SEMAPHORES = ["cV", "cS", "cP", "cG", "sent"] + ["arr%d" % i for i in range(2 * R)] + ["dm%d" % i for i in range(24)]
+
+
+def lay_out(tasks):
+    n = len(tasks)
+    q = [t["q"] for t in tasks]
+    cost = [t["cost"] for t in tasks]
+    pre, post = [[] for _ in tasks], [[] for _ in tasks]
+    for i, t in enumerate(tasks):
+        for d, waits in t["deps"].items():
+            gap = tasks[d]["lag"] + (0.0 if not waits else SAME if q[d] == q[i] and not tasks[d]["lag"] else OTHER)
+            pre[i].append((d, gap))
+            post[d].append((i, gap))
+
+    def lay(order, edges, lead):
+        busy, end = {}, [0.0] * n
+        for i in order:
+            s = max([end[d] + gap for d, gap in edges[i]], default=lead[i])
+            row = busy.setdefault(q[i], [])
+            k = len(row)
+            while k and row[k - 1][1] > s:
+                k -= 1
+            while k < len(row) and row[k][0] < s + cost[i] - 1e-6:
+                s = max(s, row[k][1])
+                k += 1
+            row.insert(k, (s, s + cost[i]))
+            end[i] = s + cost[i]
+        return end
+    none, lag, seed = [0.0] * n, [t["lag"] for t in tasks], [1]
+
+    def turn(end):
+        back = lay(sorted(range(n), key=lambda i: (-end[i], -i)), post, lag)
+        return lay(sorted(range(n), key=lambda i: (-back[i], i)), pre, none)
+
+    def span(end):
+        return max(end[i] + lag[i] for i in range(n))
+
+    def draw():
+        seed[0] = (seed[0] * 1103515245 + 12345) % 2 ** 31
+        return seed[0] / 2 ** 31
+    best = turn(lay(range(n), pre, none))
+    for j in range(TURNS):
+        at, width, amp = draw() * span(best), (2000.0, 5000.0)[j % 2], (300.0, 1000.0, 2000.0)[j % 3]
+        key = [0.0] * n
+        for i in range(n):
+            own = best[i] - cost[i] + ((draw() - 0.5) * amp if abs(best[i] - at) < width else 0.0)
+            key[i] = max([own] + [key[d] for d, _ in pre[i]])
+        end = lay(sorted(range(n), key=lambda i: (key[i], i)), pre, none)
+        if j % 4 == 0:
+            end = turn(end)
+        if span(end) <= span(best):
+            best = end
+    return sorted(range(n), key=lambda i: (best[i] - cost[i], i))
 
 
 def rank_program(g, core, T, topo):
@@ -54,457 +116,385 @@ def rank_program(g, core, T, topo):
     after, before = T.cores[(rank + 1) % n], T.cores[(rank - 1) % n]
     V, S, P, Y = g.vector, g.scalar, g.tensor, g.sync
     Q = {"V": V, "S": S, "P": P, "G": g, "Y": Y}
-    count, wrote, readers, knew = {}, {}, {}, {}
-    waited = {q: {} for q in Q}
+    tasks, touched, masks, dmas, behind = [], {}, {}, [0], []
 
-    def need(q, deps):
-        w = waited[q]
-        todo = {s_: v_ for s_, v_ in deps.items() if w.get(s_, 0) < v_}
-        for sem, val in todo.items():
-            if any(o != sem and knew.get((o, ov), {}).get(sem, 0) >= val for o, ov in todo.items()):
-                continue
-            Q[q].wait_ge(T.sem[sem], val)
-        for sem, val in todo.items():
-            for s_, v_ in list(knew.get((sem, val), {}).items()) + [(sem, val)]:
-                w[s_] = max(w.get(s_, 0), v_)
+    def vw(name, a=0, b=None, step=1):
+        if name in PART:
+            name, o, w = PART[name]
+            a, b = o + a, o + (w if b is None else b)
+        where, shape, kind = SCRATCH[name]
+        b = shape[1] if b is None else b
+        if (a, b, step) not in masks:
+            masks[(a, b, step)] = sum(1 << i for i in range(a, b, step))
+        m = masks[(a, b, step)]
+        if where == "psum":
+            m = ((1 << 512) - 1) << (a // 512 * 512)
+        return (T[name][:, a:b:step] if step > 1 else T[name][:, a:b], name, m, len(range(a, b, step)),
+                kind in ("bfloat16", "uint16"), None)
 
-    def issue(q, own, calls, inc, r, w, acc=False):
-        deps = {}
-
-        def add(d):
-            for s_, v_ in d.items():
-                deps[s_] = max(deps.get(s_, 0), v_)
-        for k in r:
-            add(wrote.get(k, {}))
-            if k.startswith("ps"):
-                add({s_: v_ for s_, v_ in readers.get(k, {}).items() if s_ != own})
-        for k in w:
-            if not acc:
-                add(wrote.get(k, {}))
-            add(readers.get(k, {}))
-        need(q, deps)
-        for call in calls:
-            call().then_inc(T.sem[own], inc)
-            count[own] = count.get(own, 0) + inc
-        knew[(own, count[own])] = dict(waited[q])
-        for k in r:
-            readers.setdefault(k, {})[own] = count[own]
-        for k in w:
-            wrote[k] = {own: count[own]}
-            readers[k] = {}
-
-    def op(q, call, r=(), w=(), acc=False):
-        issue(q, "c" + q, [call], 1, r, w, acc)
-
-    def dma(q, sem, pairs, r=(), w=()):
-        issue(q, sem, [lambda o=o, i=i: Q[q].dma_start(o, i) for o, i in pairs], 16, r, w)
+    def by(win, off, words=False):
+        ap = win[0].bitcast(dt.uint32) if words else win[0]
+        return (ap.indirect(off[0]), win[1], win[2], 16 * off[3], win[4], off)
 
     def bank(b, w, a=0):
-        return T.ps[:, 512 * b + a:512 * b + w]
+        return vw("ps", 512 * b + a, 512 * b + w)
 
-    def ts(out, in0, s1, s2, o0, o1, r, w):
-        if o1 is None:
-            op("V", lambda: V.tensor_scalar(out, in0, s1, None, o0), r, w)
+    def ap(x):
+        return x[0] if isinstance(x, tuple) else x
+
+    def add(q, cost, make, r, w, sem=None, lag=0.0, acc=False):
+        r = [x for x in r if isinstance(x, tuple)]
+        r += [x[5] for x in r + w if x[5] is not None]
+        deps, me = {d: False for d in behind if tasks[d]["q"] == q}, len(tasks)
+        for x, writes in [(x, False) for x in r] + [(x, True) for x in w]:
+            for m, d, wr in touched.get(x[1], []):
+                if m & x[2] and d != me:
+                    if wr and writes and acc:
+                        deps.setdefault(d, False)
+                    elif wr or writes or x[1] == "ps" and tasks[d]["q"] != q:
+                        deps[d] = True
+        for x in w:
+            touched[x[1]] = [e for e in touched.get(x[1], []) if e[0] & ~x[2]]
+        for x, writes in [(x, False) for x in r] + [(x, True) for x in w]:
+            touched.setdefault(x[1], []).append((x[2], me, writes))
+        tasks.append(dict(q=q, cost=cost, make=make, deps=deps, sem=sem, lag=lag))
+
+    def length(q, out, a, each=1.0):
+        if out[5] is not None:
+            return 50 + SC * out[3]
+        if a[5] is not None:
+            return (50 if q == "V" else 65) + GA * out[3]
+        return max(LEAST[q], each * out[3]) * CYC + FIXED[q]
+
+    def half(*xs):
+        return 0.5 if all(x[4] for x in xs) else 1.0
+
+    def ts(out, a, s1, s2, o0, o1=None):
+        more = () if o1 is None else (o1,)
+        add("V", length("V", out, a, half(out, a)), lambda: [V.tensor_scalar(out[0], a[0], ap(s1), ap(s2), o0, *more)],
+            [a, s1, s2], [out])
+
+    def tt(out, a, b, o):
+        add("V", length("V", out, a, 1.0 if "ps" in (a[1], b[1]) else 2.0), lambda: [V.tensor_tensor(out[0], a[0], b[0], o)],
+            [a, b], [out])
+
+    def cp(out, a):
+        add("V", length("V", out, a, half(out, a)), lambda: [V.tensor_copy(out[0], a[0])], [a], [out])
+
+    def scan(out, d0, d1, init, o0, o1):
+        add("V", length("V", out, d0, half(out, d0, d1)), lambda: [V.tensor_tensor_scan(out[0], d0[0], d1[0], init, o0, o1)],
+            [d0, d1], [out])
+
+    def wrap(out, data):
+        scan(out, vw("MF", 0, out[3]), data, 0.0, OP.add, OP.max)
+
+    def fill(out, c):
+        add("V", length("V", out, out, half(out)), lambda: [V.memset(out[0], c)], [], [out])
+
+    def act(out, a, f, sums=None, **kw):
+        given = {k: ap(x) for k, x in kw.items()}
+        if sums is not None:
+            given["accum_out"] = sums[0]
+        add("S", length("S", out, a) + (20 if sums else 0), lambda: [S.activation(out[0], a[0], f, **given)],
+            [a] + list(kw.values()), [out] + ([sums] if sums else []))
+
+    def move(out, a, c=None, on="S"):
+        if on == "S":
+            act(out, a, AF.Copy, **({} if c is None else {"scale": c}))
+        elif c is None:
+            cp(out, a)
         else:
-            op("V", lambda: V.tensor_scalar(out, in0, s1, s2, o0, o1), r, w)
+            ts(out, a, c, None, OP.mult)
 
-    def tt(out, a, b, o, r, w):
-        op("V", lambda: V.tensor_tensor(out, a, b, o), r, w)
+    def quant(name, a, b, src):
+        c, s = vw("q" + name, a, b), vw("s" + name, a, b)
+        add("V", 12 + 0.22 * src[3], lambda: [V.quantize_mx(c[0], s[0], src[0])], [src], [c, s])
 
-    def cp(out, a, r, w):
-        op("V", lambda: V.tensor_copy(out, a), r, w)
+    def mm(b, st, sa, mv, ma, w, start=True, stop=True):
+        x = [vw("q" + st, sa, sa + 128), vw("s" + st, sa, sa + 128), vw("q" + mv, ma, ma + w), vw("s" + mv, ma, ma + w)]
+        out = bank(b, w)
+        add("P", (w + 16) * CYC, lambda: [P.matmul_mx(out[0], x[0][0], x[1][0], x[2][0], x[3][0], start, stop)], x, [out],
+            acc=not start)
 
-    def scan(out, d0, d1, init, o0, o1, r, w):
-        op("V", lambda: V.tensor_tensor_scan(out, d0, d1, init, o0, o1), r, w)
+    def iota(out, pat, base=0, mult=0):
+        kw = {} if SCRATCH[out[1]][2] == "int32" else {"allow_small_or_imprecise_dtypes": True}
+        add("G", 130 + 2 * CYC * out[3], lambda: [g.iota(out[0], pat, base, mult, **kw)], [], [out])
 
-    def fill(ap, c, w):
-        op("V", lambda: V.memset(ap, c), (), w)
+    def where0(out, a, pat, base, mult):
+        add("G", 170 + 2 * CYC * out[3], lambda: [g.affine_select(out[0], a[0], pat, OP.is_equal, 0.0, base, mult)], [a], [out])
 
-    def act(out, a, f, r, w, **kw):
-        op("S", lambda: S.activation(out, a, f, **kw), r, w)
+    def dma(q, pairs, r=(), w=(), lag=LOAD):
+        dmas[0] += 1
+        add(q, 60.0 * len(pairs), lambda: [Q[q].dma_start(o, i) for o, i in pairs], list(r), list(w), "dm%d" % dmas[0], lag)
 
-    def sfill(buf, a, b, c, w):
-        act(buf[:, a:b], T.one[:, 0:b - a], AF.Copy, ["one"], w, scale=c)
-
-    def scaled(q, out, a, c, r, w):
-        if q == "S":
-            act(out, a, AF.Copy, r, w, scale=c)
-        else:
-            ts(out, a, c, None, OP.mult, None, r, w)
-
-    def quant(name, a, b, src, r, key=None):
-        op("V", lambda: V.quantize_mx(T["q" + name][:, a:b], T["s" + name][:, a:b], src), r, key or ["q" + name])
-
-    def mm(b, st, sa, mv, ma, w, r, start=True, stop=True):
-        op("P", lambda: P.matmul_mx(bank(b, w), T["q" + st][:, sa:sa + 128], T["s" + st][:, sa:sa + 128],
-                                    T["q" + mv][:, ma:ma + w], T["s" + mv][:, ma:ma + w], start, stop),
-           r, ["ps%d" % b], acc=not start)
-
-    def iota(out, pat, base, mult, w, small=True):
-        if small:
-            op("G", lambda: g.iota(out, pat, base, mult, allow_small_or_imprecise_dtypes=True), (), w)
-        else:
-            op("G", lambda: g.iota(out, pat, base, mult), (), w)
-
-    def where0(out, a, pat, base, mult, r, w):
-        op("G", lambda: g.affine_select(out, a, pat, OP.is_equal, 0.0, base, mult), r, w)
-
-    def send(src, dst, to, sem):
+    def exchange(src, dst, to, frm, sem):
         rid, pid, _ = topo.addr(to)
         m = topo.mask(core, to)
-        need("G", wrote["q" + src])
-        g.remote_dma(T["q" + dst][:].bitcast(dt.uint8), T["q" + src][:].bitcast(dt.uint8), T.sem[sem], T.sem.sent, pid, rid, m)
-        g.remote_dma(T["s" + dst][:], T["s" + src][:], T.sem[sem], T.sem.sent, pid, rid, m)
-        count["sent"] = count.get("sent", 0) + 2 * len(topo.engines(core, to))
 
-    def arrived(name, frm, sem):
-        count[sem] = 2 * len(topo.engines(frm, core))
-        wrote["q" + name] = {sem: count[sem]}
+        def make():
+            g.remote_dma(T["q" + dst][:].bitcast(dt.uint8), T["q" + src][:].bitcast(dt.uint8), T.sem[sem], T.sem.sent, pid, rid, m)
+            g.remote_dma(T["s" + dst][:], T["s" + src][:], T.sem[sem], T.sem.sent, pid, rid, m)
+            return (2 * len(topo.engines(core, to)), 2 * len(topo.engines(frm, core)))
+        add("G", 200.0, make, [vw("q" + src), vw("s" + src)], [vw("q" + dst), vw("s" + dst)], sem, TRIP + FIRST * (sem == "arr0"))
 
-    def four(name):
-        return [name + str(i) for i in range(4)]
+    def col(name, j):
+        return vw(name, j, j + 1)
 
-    XA, XB = four("XA"), four("XB")
-    XK = XA + XB
-    dma("S", "dm0", [(T.ub[:], T.u[:])], (), ["ub"])
-    dma("Y", "dm1", [(T.X[:, 0:4 * HC], T.x[:, 0:4 * HC])], (), XA)
-    dma("Y", "dm15", [(T.X[:, 4 * HC:4 * C], T.x[:, 4 * HC:4 * C])], (), XB)
-    dma("Y", "dm2", [(T.cli[:], T.cl[:])], (), ["cli"])
+    def plane(name, b, w=512):
+        return vw(name, 512 * b, 512 * b + w)
 
-    k0 = 24 - NVROW
-    iota(T.pcol[:], [[0, 1]], 0, 1, ["pcol"], False)
-    iota(T.uoffi[:], [[16, 8]], 0, 0, ["uoffi"], False)
-    iota(T.i16[:], [[0, 24], [1, 16]], 0, 0, ["i16"])
-    iota(T.pre0[:], [[16, 24]], 0, 0, ["pre0"])
-    iota(T.s4o[:], [[0, 32], [1, 4]], 0, 0, ["s4o"])
-    iota(T.gm[:], [[1, 8], [0, 64]], 0, 0, ["gm"])
-    iota(T.val[:], [[1, C]], -int(MID), 0, ["val"])
-    fill(T.one[:], 1.0, ["one"])
-    fill(T.Rst[:], BIG, ["Rst"])
-    fill(T.rstb[:], 1.0, ["rstb"])
-    fill(T.Rst4[:], BIG, ["Rst4"])
-    fill(T.rowS[:, 0:1], 0.0, ["row0"])
-    fill(T.Rst[:, 0:C:16], -BIG, ["Rst"])
-    fill(T.rstb[:, 0:C:16], 0.0, ["rstb"])
-    fill(T.Rst4[:, 0:K:4], -BIG, ["Rst4"])
-    sfill(T.q25, 0, 528, 0.25, ["q25"])
-    for m in range(5, -1, -1):
-        sfill(T.TT, 4 * (TO[m] + 16 * (21 - 4 * m)), 4 * (TO[m] + TW[m]), 0.0, four("T%d_" % m) + ["dg"] * (m == 0))
-    where0(T.cI[:], T.q25[:], [[-1, 528]], 3, 4, ["q25"], ["cI"])
+    def const(out, c):
+        move(out, vw("one", 0, out[3]), c)
+
+    dma("S", [(T.ub[:], T.u[:])], (), [vw("ub")])
+    for a, b in XP:
+        dma("Y", [(T.X[:, 4 * a:4 * b], T.x[:, 4 * a:4 * b])], (), [vw("X", 4 * a, 4 * b)], LOAD + 500)
+    dma("Y", [(T.cli[:], T.cl[:])], (), [vw("cli")])
+    dma("Y", [(T.qL[:].bitcast(dt.uint8), T.wc[:]), (T.sL[:], T.ws[:])], [vw("X")], [vw("qL"), vw("sL")])
+    dma("Y", [(T.vb[:], T.v[:])], [vw("X")], [vw("vb")])
+
+    fill(vw("one"), 1.0)
+    iota(vw("pcol"), [[0, 1]], 0, 1)
+    iota(vw("uoffi"), [[16, 8]])
+    iota(vw("i16"), [[0, 13], [1, 16]])
+    iota(vw("k16"), [[16, 24]])
+    iota(vw("gm"), [[1, 8], [0, 64]])
+    iota(vw("val"), [[1, C]])
+    iota(vw("n16"), [[1, 16]])
+    iota(vw("fd", 0, ZA), [[1, ZA]])
+    iota(vw("fd", ZA, A), [[2, A - ZA]], ZA)
+    const(vw("Awin", 0, C), float(APART))
+    fill(vw("rstb"), 1.0)
+    fill(col("rowS", 0), 0.0)
+    fill(vw("rstb", 0, C, 16), 0.0)
+    const(vw("q25"), 0.25)
+    for m in range(6):
+        const(vw("TT", 4 * (TO[m] + 16 * (21 - 4 * m)), 4 * (TO[m] + TW[m])), 0.0)
+    for b in range(4):
+        const(vw("Hs", 512 * b + ZA, 512 * b + 512), 0.0)
+    where0(vw("cI"), vw("q25"), [[-1, 528]], 3, 4)
+    const(vw("Ft", 0, 512), 0.0)
+    ts(col("ci", 0), vw("pcol"), 15, None, OP.bitwise_and)
+    ts(col("ci", 1), vw("pcol"), 4, None, OP.arith_shift_right)
+    cp(vw("uoff"), vw("uoffi"))
+    cp(vw("cf", 0, 2), vw("ci"))
+    pr, pg = col("cf", 0), col("cf", 1)
+    lift = col("cg", 0)
+    ts(lift, pr, 15.0, -LIFT, OP.is_lt, OP.mult)
+    ts(col("cg", 1), pr, 15.0, -STEP, OP.is_lt, OP.mult)
+    ts(col("cg", 2), col("cg", 1), pr, 15.0 - STEP, OP.subtract, OP.add)
+    ts(vw("MR", 0, 32), vw("i16", 1, 33), pr, -BIG, OP.is_equal, OP.mult)
+    ts(vw("MR", 32, 64), vw("i16", 0, 32), pr, STEP, OP.is_equal, OP.mult)
+    tt(vw("MR", 64, 96), vw("MR", 0, 32), vw("MR", 32, 64), OP.add)
+    for a, w in ((0, 32), (32, 32), (96, 96), (192, 192)):
+        move(vw("MR", a, a + w), vw("MR", 64, 96) if a < 64 else vw("MR", 0, w))
+    ts(vw("Rst"), vw("i16", 0, 192), 0.5, 2 * BIG, OP.subtract, OP.mult)
+    ts(vw("M16"), vw("i16", 0, 192), pr, -BIG, OP.not_equal, OP.mult)
+    ts(vw("v16"), vw("i16", 0, 32), pr, -BIG, OP.is_equal, OP.mult)
+    ts(vw("w16"), vw("i16", 15, 47), pr, LIFT, OP.is_equal, OP.mult)
+    tt(vw("MF", 0, 32), vw("w16"), vw("v16"), OP.add)
+    for a, w in ((32, 32), (64, 64), (128, 128), (256, 256)):
+        move(vw("MF", a, a + w), vw("MF", 0, w))
+    ts(vw("jw"), vw("k16"), pr, None, OP.add)
+    ts(vw("cB"), vw("gm"), pg, None, OP.is_equal)
+    kc = min([k for k in range(17, 24) if ROWS[k - 1] == "V"] + [24])
+    ts(vw("cst", 0, kc), vw("k16", 0, kc), col("cg", 2), None, OP.add)
+    ts(vw("cst", kc, 24), vw("k16", kc, 24), 0.5, col("cg", 2), OP.mult, OP.add)
+    ts(vw("eq"), vw("i16", 0, 16), pr, None, OP.is_equal)
+    for j in range(8):
+        act(vw("Awin", C + 16 * j, C + 16 * j + 16), vw("eq"), AF.Identity, scale=2048.0 * j - APART, bias=float(APART))
+    quant("B", 0, 128, vw("cB"))
+    quant("T", TO[5], TO[5] + 128, vw("Ft", 0, 512))
+    for b in range(4):
+        quant("I", 128 * b, 128 * b + 128, vw("cI", 3 - b, 515 - b))
+    quant("U", 0, 128, vw("ub"))
+    cp((T.qU2[:].bitcast(dt.uint32),) + vw("qU2")[1:], by(vw("qU"), vw("uoff"), True))
+    move(vw("sU2"), by(vw("sU"), vw("uoff")), None, ON["su"])
+    runs = [(k, k + len(ROWS[k - 1:].split("S")[0])) for k in range(1, 24) if ROWS[k - 1] == "V" and (k == 1 or ROWS[k - 2] == "S")]
+
+    d2 = (None, "d2", 1, 1, True, None)
     for a in range(4):
-        where0(T.cW[:, 512 * a:512 * a + 512], T.one[:, 0:512], [[-512, 8], [1, 16], [-1, 4]], -4 * a, 32, ["one"], ["cW%d" % a])
-    ts(T.ci[:, 0:1], T.pcol[:], 15, None, OP.bitwise_and, None, ["pcol"], ["ci0"])
-    ts(T.ci[:, 1:2], T.pcol[:], 4, None, OP.arith_shift_right, None, ["pcol"], ["ci1"])
-    ts(T.ci[:, 2:3], T.pcol[:], 3, None, OP.bitwise_and, None, ["pcol"], ["ci2"])
-    ts(T.ci[:, 3:4], T.pcol[:], 2, 3, OP.arith_shift_right, OP.bitwise_and, ["pcol"], ["ci3"])
-    cp(T.uoff[:], T.uoffi[:], ["uoffi"], ["uoff"])
-    cp(T.cf[:, 0:4], T.ci[:], four("ci"), ["cf"])
-    pr, pg, pt, pq = T.cf[:, 0:1], T.cf[:, 1:2], T.cf[:, 2:3], T.cf[:, 3:4]
-    ts(T.msk2[:], T.i16[:], pr, 0.5, OP.is_equal, OP.subtract, ["i16", "cf"], ["msk2"])
-    ts(T.cg[:, 0:1], pr, -2.0, 15.0 + MID, OP.mult, OP.add, ["cf"], ["cg0"])
-    ts(T.cg[:, 1:2], pr, -1.5, 15.0 + MID, OP.mult, OP.add, ["cf"], ["cg1"])
-    ts(T.cg[:, 2:3], pt, 4 * MID, None, OP.add, None, ["cf"], ["cg2"])
-    ts(T.M16[:], T.msk2[:], 2 * BIG, None, OP.mult, None, ["msk2"], ["M16"])
-    quant("U", 0, 128, T.ub[:], ["ub"])
-    ts(T.M16b[:], T.msk2[:], 2 * BIG, -MID, OP.mult, OP.min, ["msk2"], ["M16b"])
-    cp(T.qU2[:].bitcast(dt.uint32), T.qU[:].bitcast(dt.uint32).indirect(T.uoff[:]), ["qU", "uoff"], ["qU2"])
-    cp(T.sU2[:], T.sU[:].indirect(T.uoff[:]), ["qU", "uoff"], ["sU2"])
+        cp(vw("c2u", 22 * a, 22 * a + 22), vw("cli", a, 88, 4))
+    dma("Y", [(T.d2[:, a], T.c2u[:, 22 * a:22 * a + 22]) for a in range(4)], [vw("c2u")], [d2])
+    dma("Y", [(T.Lu[:], T.d2[:])], [d2], [vw("Lu")])
+    for i in range(4):
+        cp(vw("flist", i, 88, 4), vw("Lu", 22 * i, 22 * i + 22))
+    cp(vw("Lf", 0, 88), vw("Lu"))
+    move(vw("Lf", 88, 110), vw("Lf", 0, 22))
+    act(vw("prio"), vw("Lf", 22, 110), AF.Identity, scale=512.0, bias=lift)
+    tt(vw("pay"), vw("prio"), vw("Lf", 0, 88), OP.add)
+    for i in range(4):
+        act(vw("P0", i, 88, 4), vw("pay", 22 * i, 22 * i + 22), AF.Identity, bias=float(i * 2 ** 18))
+        act(vw("base", i, 88, 4), vw("pay", 22 * i, 22 * i + 22), AF.Identity, bias=float(i * 2 ** 18 + (3 - i) * 2 ** 20))
 
-    def early():
-        ts(T.jw[:], T.pre0[:], pr, None, OP.add, None, ["pre0", "cf"], ["jw"])
-        ts(T.m4o[:], T.s4o[:], pq, 0.5, OP.is_equal, OP.subtract, ["s4o", "cf"], ["m4o"])
-        ts(T.cB[:], T.gm[:], pg, None, OP.is_equal, None, ["gm", "cf"], ["cB"])
-        ts(T.cst[:, 0:k0], T.jw[:, 0:k0], T.cg[:, 0:1], None, OP.add, None, ["jw", "cg0"], ["cstA"])
-        ts(T.cst[:, k0:24], T.jw[:, k0:24], 0.5, T.cg[:, 1:2], OP.mult, OP.add, ["jw", "cg1"], ["cstB"])
-        ts(T.M4[:], T.m4o[:], 2 * BIG, None, OP.mult, None, ["m4o"], ["M4"])
+    def row(k, a, b):
+        m, s = (24 - k) // 4, (24 - k) % 4
+        return vw("TT", 4 * (TO[m] + a) + s, 4 * (TO[m] + b), 4)
 
-    def lists():
-        for a in range(4):
-            cp(T.c2u[:, 22 * a:22 * a + 22], T.cli[:, a:88:4], ["cli"], ["c2u%d" % a])
-        quant("B", 0, 128, T.cB[:], ["cB"])
-        for a in range(4):
-            cp(T.c2u[:, 88 + MA * a:88 + MA * a + MA], T.c2u[:, 22 * a:22 * a + MA], ["c2u%d" % a], ["c2a%d" % a])
-            cp(T.c2u[:, 144 + 8 * a:152 + 8 * a], T.c2u[:, 22 * a + MA:22 * a + 22], ["c2u%d" % a], ["c2b%d" % a])
-        dma("Y", "dm3", [(T.qL[:].bitcast(dt.uint8), T.wc[:]), (T.sL[:], T.ws[:])], XK, ["qL"])
-        dma("Y", "dm4", [(T.vb[:], T.v[:])], (), ["vb"])
-        dma("Y", "dm6", [(T.d2[:, a], T.c2u[:, 22 * a:22 * a + 22]) for a in range(4)], four("c2u"), ["d2"])
-        dma("Y", "dm5", [(T.d1[:, i], T.c2u[i:128:4, 88:176]) for i in range(4)], four("c2a") + four("c2b"), ["d1"])
-        dma("Y", "dm8", [(T.Lu[:], T.d2[:])], ["d2"], ["Lu"])
-        dma("Y", "dm7", [(T.flist[:], T.d1[:])], ["d1"], ["flist"])
+    def position(m):
+        return (16 * m, 1) if 16 * m < ZA else (32 * m - ZA, 2)
 
-    def late():
-        iota(T.Awin[:, 0:C], [[0, C]], -1024, 0, ["AwinA"])
-        iota(T.Awin[:, C:512], [[1024, K]], 0, 0, ["AwinB"])
-        iota(T.fd[:, 0:ZA], [[1, ZA]], 0, 0, ["fdA"])
-        iota(T.fd[:, ZA:A], [[2, A - ZA]], ZA, 0, ["fdB"])
-        cp(T.Lf[:, 0:88], T.Lu[:], ["Lu"], ["Lf"])
-        cp(T.Lf[:, 88:110], T.Lu[:, 0:22], ["Lu"], ["Lf2"])
-        quant("I", 0, 128, T.cI[:, 3:515], ["cI"], ["qI0"])
-        ts(T.cand[:], T.Lf[:, 22:110], 512.0, None, OP.mult, None, ["Lf", "Lf2"], ["candA", "candB"])
-        quant("I", 128, 256, T.cI[:, 2:514], ["cI"], ["qI1"])
-        tt(T.pay[:], T.cand[:], T.Lf[:, 0:88], OP.add, ["candA", "candB", "Lf"], ["pay"])
-        quant("I", 256, 384, T.cI[:, 1:513], ["cI"], ["qI2"])
-        quant("I", 384, 512, T.cI[:, 0:512], ["cI"], ["qI3"])
-        quant("W", 0, 512, T.cW[:], four("cW"))
-        for i in range(4):
-            ts(T.base[:, i:88:4], T.pay[:, 22 * i:22 * i + 22], float(i * 2 ** 18 + (3 - i) * 2 ** 20), None, OP.add, None,
-               ["pay"], ["base%d" % i])
-        quant("F", FB - 128, FB, T.Ft[:, 0:512], ["Fta"], ["qFA"])
-        quant("F", 392, 520, T.Ft[:, 0:512], ["Fta"], ["qFB"])
-
-    def slot(k):
-        return (24 - k) // 4, (24 - k) % 4
-
-    def row_view(k, a, b):
-        m, s = slot(k)
-        return T.TT[:, 4 * (TO[m] + a) + s:4 * (TO[m] + b):4]
-
-    def rkey(k):
-        return "T%d_%d" % slot(k)
-
-    def tile_q(m, first, last):
-        quant("T", TO[m], TO[m] + TW[m], T.TT[:, 4 * TO[m]:4 * (TO[m] + TW[m])], four("T%d_" % m) + ["dg"] * (m == 0), ["qT%d" % m])
-        mm(2, "B", 0, "T", TO[m], TW[m], ["qB", "qT%d" % m], first, last)
-
-    def plane(buf, b):
-        return buf[:, 512 * b:512 * b + 512]
-
-    def xnew(q, b, h):
-        scaled(q, T.X[:, 4 * HC * h + b:4 * HC * (h + 1):4], plane(T.Ph, b).indirect(T.xoff[:, 12 * h:12 * h + 12]), 2.0,
-               ["PhA%d" % b, "PhB%d" % b, "xoff"], ["X%s%d" % ("AB"[h], b)])
-
-    def s1(k):
-        o, b = 8 * k * (k - 1), 7 if k < 12 else 1
-        act(T.tau[:, o:o + 16 * k], bank(b, 16 * k), AF.Sign, ["ps%d" % b, "scA" if k < 12 else "scB"], ["tau%d" % k], scale=-1.0,
-            bias=T.sc[:, 16 * k + 15:16 * k + 16])
-
-    def s2(k):
-        o = 8 * k * (k - 1)
-        act(row_view(k, 0, 16 * k), T.tau[:, o:o + 16 * k], AF.Relu, ["tau%d" % k], [rkey(k), "row%d" % k], accum_out=T.rowS[:, k:k + 1])
-
-    def v1(k):
-        if k >= k0:
-            ts(row_view(k, 0, 16 * k), bank(0, 16 * k), T.sc[:, 16 * k + 15:16 * k + 16], None, OP.is_lt, None, ["ps0", "scB"], [rkey(k)])
-
-    def v2(k):
-        if k >= k0:
-            e = SOW * (k - k0 + 1)
-            scan(T.so[:, e - 8 * k:e], row_view(k, 0, 8 * k), row_view(k, 8 * k, 16 * k), float(-8 * k), OP.add, OP.add,
-                 [rkey(k)], ["so%d" % k])
-
-    PIECE = {"A": (0, MA, 2), "B": (MA, 22, 3)}
-
-    def cursor(h, step):
-        m0, m1, b = PIECE[h]
-        w = m1 - m0
-        if step == 0:
-            tt(T.cand[:, 4 * m0:4 * m1], bank(b, 4 * w), T.base[:, 4 * m0:4 * m1], OP.add, ["ps%d" % b] + four("base"), ["cand" + h])
-        if step == 1:
-            tt(T.c1[:, 2 * m0:2 * m1], T.cand[:, 4 * m0:4 * m1:2], T.cand[:, 4 * m0 + 1:4 * m1:2], OP.max, ["cand" + h], ["c1" + h])
-        if step == 2:
-            tt(T.c2i[:, m0:m1], T.c1[:, 2 * m0:2 * m1:2], T.c1[:, 2 * m0 + 1:2 * m1:2], OP.max, ["c1" + h], ["c2i" + h])
-        if step == 3:
-            ts(T.ot[:, 2 * m0:2 * m0 + w], T.c2i[:, m0:m1], 511, None, OP.bitwise_and, None, ["c2i" + h], ["ot1" + h])
-            ts(T.ot[:, 2 * m0 + w:2 * m1], T.c2i[:, m0:m1], 9, 511, OP.arith_shift_right, OP.bitwise_and, ["c2i" + h], ["ot2" + h])
-        if step == 4:
-            cp(T.zoff[:, 2 * m0:2 * m1], T.ot[:, 2 * m0:2 * m1], ["ot1" + h, "ot2" + h], ["zoff" + h])
-
-    def zs(b, h):
-        m0, m1, _ = PIECE[h]
-        act(T.tmp[:, A * b + 16 * m0:A * b + 16 * m1], plane(T.Ph, b).indirect(T.zoff[:, m0 + m1:2 * m1]),
-            AF.Copy, ["PhA%d" % b, "PhB%d" % b, "zoff" + h], ["tmp%s%d" % (h, b)])
-
-    def zv(b, h):
-        m0, m1, _ = PIECE[h]
-        tt(T.Z[:, 64 * m0 + b:64 * m1:4], plane(T.Ph, b).indirect(T.zoff[:, 2 * m0:m0 + m1]), T.tmp[:, A * b + 16 * m0:A * b + 16 * m1],
-           OP.add, ["PhA%d" % b, "PhB%d" % b, "zoff" + h, "tmp%s%d" % (h, b)], ["Z%s%d" % (h, b)])
-
-    def keys(h):
-        m0, m1, _ = PIECE[h]
-        tt(T.Ar[:, 16 * m0:16 * m1], T.Awin[:].indirect(T.zoff[:, 2 * m0:m0 + m1]), T.fd[:, 16 * m0:16 * m1], OP.add,
-           ["AwinA", "AwinB", "fd" + h, "zoff" + h], ["Ar" + h])
-
-    def hit(s):
-        scan(T.so2[:, A // 2 * s:A // 2 * (s + 1)], T.D0[:, A * s:A * s + A // 2], T.D0[:, A * s + A // 2:A * s + A],
-             float(2 * A - ZA), OP.min, OP.min, ["D0_%d" % s], ["so2_%d" % s])
-
-    def hb(q, b):
-        scaled(q, T.Hs[:, 512 * b + ZA:512 * b + 2 * A - ZA:2], bank(4 + b, A - ZA), 0.03125, ["ps%d" % (4 + b)], ["HB%d" % b])
-
-    UK = ["qU2", "sU2"]
     for t in range(R + 1):
+        behind.clear()
         if t > 0:
-            Hn = "H%d" % (t - 1)
-            arrived(Hn, after, "arr%d" % (2 * t - 1))
             for b in range(4):
-                mm(b, "I", 128 * b, Hn, 0, K, ["qI%d" % b, "q" + Hn])
+                mm(b, "I", 128 * b, "H%d" % (t - 1), 0, K)
             for b in range(4):
-                tt(T.Ph[:, 512 * b + C:512 * b + 512], bank(b, K), T.Eq[:, K * b:K * b + K], OP.add, ["ps%d" % b, "Eq%d" % b],
-                   ["PhB%d" % b])
-            for q, b, h in (("S", 0, 0), ("S", 1, 0), ("V", 2, 0), ("V", 3, 0), ("S", 0, 1), ("S", 1, 1), ("S", 2, 1)):
-                xnew(q, b, h)
-        quant("X", 0, HC, T.X[:, 0:4 * HC], XA, ["qXA"])
+                tt(vw("Ph", 512 * b + C, 512 * b + 512), bank(b, K), vw("Eq", K * b, K * b + K), OP.add)
+            for i, (a, e) in enumerate(XP):
+                for b in range(4):
+                    move(vw("X", 4 * a + b, 4 * e, 4), by(plane("Ph", b), vw("xoff", a // 16, e // 16)), 2.0, ON["x"][4 * i + b])
+        for a, e in XP:
+            quant("X", a, e, vw("X", 4 * a, 4 * e))
         if t == R:
             break
-        mm(6, "U2", 0, "X", 0, HC, UK + ["qXA"])
-        mm(7, "U2", 0, "X", 0, HC, UK + ["qXA"])
-        if t > 0:
-            xnew("V", 3, 1)
-        else:
-            early()
-        tt(T.msk[:, 0:HC], bank(6, HC), T.M16[:, 0:HC], OP.min, ["ps6", "M16"], ["mskA"])
-        quant("X", HC, C, T.X[:, 4 * HC:4 * C], XB, ["qXB"])
-        mm(0, "U2", 0, "X", 0, C, UK + ["qXA", "qXB"])
-        mm(1, "U2", 0, "X", 0, C, UK + ["qXA", "qXB"])
-        scan(T.sc[:, 0:HC], T.Rst[:, 0:HC], T.msk[:, 0:HC], -BIG, OP.min, OP.max, ["Rst", "mskA"], ["scA"])
-        if t == 0:
-            lists()
-        tt(T.msk[:, HC:C], bank(0, C, HC), T.M16[:, HC:C], OP.min, ["ps0", "M16"], ["mskB"])
-        tt(row_view(24, 0, HC), bank(6, HC), T.sc[:, 0:HC], OP.is_le, ["ps6", "scA"], ["dg"])
-        scan(T.sc[:, HC:C], T.Rst[:, HC:C], T.msk[:, HC:C], -BIG, OP.min, OP.max, ["Rst", "mskB"], ["scB"])
-        srows = list(range(11, 0, -1)) + list(range(k0 - 1, 11, -1))
-        s1(srows[0])
-        for i, k in enumerate(srows):
-            if i + 1 < len(srows):
-                s1(srows[i + 1])
-            s2(k)
-        v1(23); v1(22); v1(21)
-        tt(row_view(24, HC, C), bank(0, C, HC), T.sc[:, HC:C], OP.is_le, ["ps0", "scB"], [rkey(24)])
-        v2(23); v2(22)
-        tile_q(0, True, False)
-        v1(20); v2(21)
-        tile_q(4, False, False)
-        v1(19)
-        scan(T.dsc[:], T.rstb[:], row_view(24, 0, C), 0.0, OP.mult, OP.add, ["rstb", rkey(24), "dg"], ["dsc"])
-        tile_q(5, False, False)
-        v1(18); v1(17); v2(20); v2(19)
-        tile_q(1, False, False)
-        tile_q(2, False, False)
-        tile_q(3, False, True)
-        v2(18); v2(17)
-        tt(T.pre0[:], T.cst[:], T.dsc[:, 15:C:16], OP.subtract, ["cstA", "cstB", "dsc"], ["pre0"])
-        cp(T.rowS[:, k0:24], T.so[:, SOW - 1:SOW * NVROW:SOW], ["so%d" % k for k in range(k0, 24)], ["rowV"])
-        tt(T.msk2[:], bank(2, C), T.M16b[:], OP.add, ["ps2", "M16b"], ["msk2"])
-        tt(T.pre[:], T.pre0[:], T.rowS[:], OP.subtract, ["pre0", "rowV"] + ["row%d" % k for k in range(k0)], ["pre"])
-        scan(T.sc2[:], T.Rst[:], T.msk2[:], -BIG, OP.min, OP.max, ["Rst", "msk2"], ["sc2"])
-        tt(T.rank[:], T.pre[:], T.sc2[:, 15:C:16], OP.add, ["pre", "sc2"], ["rank"])
-        cp(T.roff[:], T.rank[:], ["rank"], ["roff"])
+        (_, h), _ = XP
+        mm(6, "U2", 0, "X", 0, h)
+        mm(7, "U2", 0, "X", 0, h)
+        mm(3, "U2", 0, "X", h, C - h)
+        mm(0, "U2", 0, "X", 0, C)
+        mm(1, "U2", 0, "X", 0, C)
+        for (a, e), b in zip(XP, (6, 3)):
+            tt(vw("msk", a, e), bank(b, e - a), vw("M16", 0, e - a), OP.add)
+            scan(vw("sc", a, e), vw("Rst", 0, e - a), vw("msk", a, e), -BIG, OP.min, OP.max)
+            tt(row(24, a, e), bank(b, e - a), vw("sc", a, e), OP.is_le)
+        scan(vw("dsc"), vw("rstb"), row(24, 0, C), 0.0, OP.mult, OP.add)
+        for k in range(23, 0, -1):
+            mine = col("sc", 16 * k + 15)
+            if ROWS[k - 1] == "V":
+                e = SOW * (k + 1)
+                ts(row(k, 0, 16 * k), bank(6 if 16 * k < h else 0, 16 * k), mine, None, OP.is_lt)
+                scan(vw("so", e - 8 * k, e), row(k, 0, 8 * k), row(k, 8 * k, 16 * k), -8.0 * k * (k >= kc), OP.add, OP.add)
+            else:
+                o = 8 * k * (k - 1)
+                act(vw("tau", o, o + 16 * k), bank(7 if 16 * k < h else 1, 16 * k), AF.Sign, scale=-1.0, bias=mine)
+                act(row(k, 0, 16 * k), vw("tau", o, o + 16 * k), AF.Relu, col("rowS", k))
+        for m in range(5):
+            w = TW[m] + TW[5] * (m == 4)
+            quant("T", TO[m], TO[m] + w, vw("TT", 4 * TO[m], 4 * (TO[m] + w)))
+            if m < 2:
+                mm(4, "B", 0, "T", TO[m] + 192, TW[m] - 192, m == 0, m == 1)
+            mm(2, "B", 0, "T", TO[m], min(TW[m], 16 * KH), m == 0, False)
+        mm(2, "B", 0, "T", TO[5], 128, False, True)
+        tt(vw("pre0"), vw("cst"), vw("dsc", 15, C, 16), OP.subtract)
+        for a, e in runs:
+            cp(vw("rowS", a, e), vw("so", SOW * (a + 1) - 1, SOW * e, SOW))
+        for a, e, sums in ((KH, 24, bank(4, 192, 16 * KH - 192)), (0, KH, bank(2, 16 * KH))):
+            tt(vw("MR", 16 * a + 15, 16 * e, 16), vw("pre0", a, e), vw("rowS", a, e), OP.subtract)
+            scan(vw("sc2", 16 * a, 16 * e), sums, vw("MR", 16 * a, 16 * e), -1.0, OP.max, OP.add)
+            ts(vw("roff", a, e), vw("sc2", 16 * a + 15, 16 * e, 16), STEP, None, OP.add)
+            cp(by(vw("ew"), vw("roff", a, e)), vw("val", 16 * a, 16 * e))
+        wrap(vw("s4o"), vw("ew", 0, K))
+        ts(vw("eoff"), vw("s4o", 15, K, 16), lift, None, OP.add)
         for b in range(4):
-            scaled("S", T.Ph[:, 512 * b:512 * b + C], T.X[:, b:4 * C:4], 0.5, XK, ["PhA%d" % b])
-        act(T.Fl[:, 0:C], bank(1, C), AF.Sign, ["ps1"], ["FlS"])
-        if t == 0:
-            sfill(T.Ft, 0, 512, 0.0, ["Fta"])
-        act(T.Fl[:, 0:C], T.Fl[:, 0:C], AF.Relu, ["FlS"], ["FlA"], scale=TOP)
-        cp(T.ew[:].indirect(T.roff[:]), T.val[:], ["roff", "val"], ["ew"])
-        tt(T.m4o[:], T.ew[:, 0:K], T.M4[:], OP.min, ["ew", "M4"], ["m4o"])
-        scan(T.s4o[:], T.Rst4[:], T.m4o[:], -BIG, OP.min, OP.max, ["Rst4", "m4o"], ["s4o"])
-        ts(T.eoff[:], T.s4o[:, 3:K:4], 4.0, T.cg[:, 2:3], OP.mult, OP.add, ["s4o", "cg2"], ["eoff"])
-        act(T.E[:, 256:512], T.X[:].indirect(T.eoff[:, 16:32]), AF.Copy, XK + ["eoff"], ["Eb"])
-        cp(T.E[:, 0:256], T.X[:].indirect(T.eoff[:, 0:16]), XK + ["eoff"], ["Ea"])
-        quant("E%d" % t, 0, K, T.E[:], ["Ea", "Eb"])
-        send("E%d" % t, "G%d" % t, after, "arr%d" % (2 * t))
-        if t == 0:
-            act(T.nth[:], T.jw[:, 0:8], AF.Copy, ["jw"], ["nth"], scale=-1024.0)
-            for b in range(4):
-                sfill(T.Hs, 512 * b + ZA, 512 * b + 512, 0.0, ["HB%d" % b])
-            late()
+            move(plane("Ph", b, C), vw("X", b, 4 * C, 4), 0.5, ON["ph"][b])
+            move(vw("E", b, 512, 4), by(plane("Ph", b, C), vw("eoff")), 2.0, ON["e"][b])
+        act(vw("Fl", 0, C), bank(1, C), AF.Sign)
+        act(vw("Fl", 0, C), vw("Fl", 0, C), AF.Relu, scale=TOP)
+        quant("E%d" % t, 0, K, vw("E"))
+        exchange("E%d" % t, "G%d" % t, after, before, "arr%d" % (2 * t))
         Gn = "G%d" % t
-        FK = ["FlS", "FlA", "FlB", "flist"]
-        arrived(Gn, before, "arr%d" % (2 * t))
-        mm(3, "U2", 0, Gn, 0, K, UK + ["q" + Gn])
+        mm(3, "U2", 0, Gn, 0, K)
         for b in range(4):
-            mm(4 + b, "I", 128 * b, Gn, 0, K, ["qI%d" % b, "q" + Gn])
-        ts(T.Fl[:, C:512], bank(3, K), 0.0, TOP, OP.is_gt, OP.mult, ["ps3"], ["FlB"])
-        act(T.Ft[:, 512:896], T.Fl[:].indirect(T.flist[:, 32:56]), AF.Copy, FK, ["Ftb"])
-        cp(T.Ft[:, 0:512], T.Fl[:].indirect(T.flist[:, 0:32]), FK, ["Fta"])
-        act(T.Ft[:, 896:1408], T.Fl[:].indirect(T.flist[:, 56:88]), AF.Copy, FK, ["Ftc"])
-        quant("F", 0, ZA, T.Ft[:, 0:896], ["Fta", "Ftb"], ["qFA"])
-        for a in range(4):
-            mm(2, "W", 128 * a, "F", 4 * MA * a, 128, ["qW", "qFA"], a == 0, a == 3)
+            mm(4 + b, "I", 128 * b, Gn, 0, K)
+        ts(vw("Fl", C, 512), bank(3, K), 0.0, TOP, OP.is_gt, OP.mult)
+        for i, (a, b) in enumerate(FP):
+            move(vw("Ft", 16 * a, 16 * b), by(vw("Fl"), vw("flist", a, b)), None, ON["fl"][i])
+            wrap(vw("Fs", 16 * a, 16 * b), vw("Ft", 16 * a, 16 * b))
         for b in range(4):
-            scaled("S", T.Ph[:, 512 * b + C:512 * b + 512], bank(4 + b, K), 2.0, ["ps%d" % (4 + b)], ["PhB%d" % b])
-        quant("F", FB, FB + 128, T.Ft[:, 896:1408], ["Ftc"], ["qFB"])
-        for a in range(4):
-            mm(3, "W", 128 * a, "F", FB + 32 * a, 128, ["qW", "qFB"], a == 0, a == 3)
-        for h, step in (("A", 0), ("A", 1), ("B", 0), ("A", 2), ("B", 1), ("A", 3), ("B", 2), ("A", 4), ("B", 3), ("B", 4)):
-            cursor(h, step)
-        for h in "AB":
+            move(vw("Ph", 512 * b + C, 512 * b + 512), bank(4 + b, K), 2.0, ON["phb"][b])
+        for a, e in ZP:
+            tt(vw("cand", 4 * a, 4 * e), vw("Fs", 64 * a + 15, 64 * e, 16), vw("base", 4 * a, 4 * e), OP.add)
+            tt(vw("c1", 2 * a, 2 * e), vw("cand", 4 * a, 4 * e, 2), vw("cand", 4 * a + 1, 4 * e, 2), OP.max)
+            tt(vw("c2i", a, e), vw("c1", 2 * a, 2 * e, 2), vw("c1", 2 * a + 1, 2 * e, 2), OP.max)
+            ts(vw("ot", 2 * a, a + e), vw("c2i", a, e), 511, None, OP.bitwise_and)
+            ts(vw("ot", a + e, 2 * e), vw("c2i", a, e), 9, 511, OP.arith_shift_right, OP.bitwise_and)
+            cp(vw("zoff", 2 * a, 2 * e), vw("ot", 2 * a, 2 * e))
+            tt(vw("Ar", 16 * a, 16 * e), by(vw("Awin"), vw("zoff", 2 * a, a + e)), vw("fd", 16 * a, 16 * e), OP.add)
+        for i, (a, e) in enumerate(ZP):
+            one, two = vw("zoff", 2 * a, a + e), vw("zoff", a + e, 2 * e)
             for b in range(4):
-                zs(b, h)
-        keys("A")
-        zv(0, "A")
-        keys("B")
+                part = vw("tmp", A * b + 16 * a, A * b + 16 * e)
+                move(part, by(plane("Ph", b), two), None, ON["z"][4 * i + b])
+                tt(vw("Z", 64 * a + b, 64 * e, 4), by(plane("Ph", b), one), part, OP.add)
+            quant("Z", 16 * a, 16 * e, vw("Z", 64 * a, 64 * e))
+            o, step = position(a)
+            for b in range(4):
+                mm(4 * (i % 2) + b, "L", 128 * b, "Z", 16 * a, 16 * (e - a))
+                move(vw("Hs", 512 * b + o, 512 * b + o + 16 * (e - a) * step, step), bank(4 * (i % 2) + b, 16 * (e - a)), 0.03125,
+                     ON["h"][4 * i + b])
         for s in range(8):
-            act(T.D0[:, A * s:A * s + A], T.Ar[:], AF.Abs, ["ArA", "ArB", "nth"], ["D0_%d" % s], bias=T.nth[:, s:s + 1])
-        for b in range(1, 4):
-            zv(b, "A")
-        zv(0, "B")
-        quant("Z", 0, ZA, T.Z[:, 0:4 * ZA], four("ZA"), ["qZA"])
+            if s:
+                act(vw("D0", A * s, A * s + A), vw("Ar"), AF.Abs, bias=-2048.0 * s)
+            name, o = ("D0", A * s) if s else ("Ar", 0)
+            scan(vw("so2", A // 2 * s, A // 2 * (s + 1)), vw(name, o, o + A // 2), vw(name, o + A // 2, o + A),
+                 float(2 * A - ZA), OP.min, OP.min)
+        cp(vw("foff"), vw("so2", A // 2 - 1, 4 * A, A // 2))
         for b in range(4):
-            mm(b, "L", 128 * b, "Z", 0, ZA, ["qL", "qZA"])
-        for b in range(1, 4):
-            zv(b, "B")
-        scaled("V", T.Hs[:, 0:ZA], bank(0, ZA), 0.03125, ["ps0"], ["HA0"])
-        quant("Z", ZA, A, T.Z[:, 4 * ZA:4 * A], four("ZB"), ["qZB"])
+            move(vw("Vt", b, 512, 4), by(plane("Hs", b), vw("foff")), None, ON["vt"][b])
+        quant("V%d" % t, 0, K, vw("Vt"))
+        behind.append(len(tasks) - 1)
+        exchange("V%d" % t, "H%d" % t, before, after, "arr%d" % (2 * t + 1))
         for b in range(4):
-            mm(4 + b, "L", 128 * b, "Z", ZA, A - ZA, ["qL", "qZB"])
-        for b in range(NSH):
-            hb("S", b)
-        for b in range(1, 4):
-            scaled("V", T.Hs[:, 512 * b:512 * b + ZA], bank(b, ZA), 0.03125, ["ps%d" % b], ["HA%d" % b])
-        for s in range(4):
-            hit(s)
-        hb("V", 3)
-        for s in range(4, 8):
-            hit(s)
-        hb("V", 2)
-        cp(T.foff[:], T.so2[:, A // 2 - 1:4 * A:A // 2], ["so2_%d" % s for s in range(8)], ["foff"])
-        for b in (0, 1):
-            act(T.Vt[:, b:512:4], plane(T.Hs, b).indirect(T.foff[:]), AF.Copy, ["HA%d" % b, "HB%d" % b, "foff"], ["Vt%d" % b])
-        for b in (3, 2):
-            cp(T.Vt[:, b:512:4], plane(T.Hs, b).indirect(T.foff[:]), ["HA%d" % b, "HB%d" % b, "foff"], ["Vt%d" % b])
-        quant("V%d" % t, 0, K, T.Vt[:], four("Vt"))
-        send("V%d" % t, "H%d" % t, before, "arr%d" % (2 * t + 1))
-        for b in range(4):
-            scaled("S", T.Eq[:, K * b:K * b + K], T.E[:, b:512:4], 0.25, ["Ea", "Eb"], ["Eq%d" % b])
-        ts(T.pre0[:], T.rank[:], float(K), None, OP.is_lt, None, ["rank"], ["pre0"])
-        tt(T.xb[:], T.rank[:], T.jw[:], OP.subtract, ["rank", "jw"], ["xb"])
-        ts(T.cc[:], T.c2i[:], 18, 3, OP.arith_shift_right, OP.bitwise_and, ["c2iA", "c2iB"], ["cc"])
-        ts(T.pre[:], T.xb[:], float(C), None, OP.add, None, ["xb"], ["pre"])
+            move(vw("Eq", K * b, K * b + K), vw("E", b, 512, 4), 0.25, ON["eq"][b])
+        xa, xb, xc = (vw("xs", 24 * j, 24 * j + 24) for j in range(3))
+        cp(vw("rank"), vw("roff"))
+        ts(xa, vw("rank"), float(K), None, OP.is_lt)
+        tt(xb, vw("rank"), vw("jw"), OP.subtract)
+        ts(xc, xb, float(C), None, OP.add)
+        tt(xb, xc, xa, OP.mult)
+        tt(xc, xb, vw("jw"), OP.add)
+        cp(vw("xoff"), xc)
+        if t == 0:
+            quant("Vv", 0, 128, vw("vb"))
+        ts(vw("cc"), vw("c2i"), 18, 3, OP.arith_shift_right, OP.bitwise_and)
         if t + 1 < R:
             for i in range(4):
-                ts(T.ti[:, i:88:4], T.cc[:], float(3 - i), None, OP.add, None, ["cc"], ["ti%d" % i])
-        tt(T.xb[:], T.pre[:], T.pre0[:], OP.mult, ["pre", "pre0"], ["xb"])
-        if t + 1 < R:
-            ts(T.cli[:], T.ti[:], 3, None, OP.bitwise_and, None, four("ti"), ["cli"])
-        tt(T.pre[:], T.xb[:], T.jw[:], OP.add, ["xb", "jw"], ["pre"])
-        if t + 1 < R:
-            ts(T.cand[:], T.cli[:], float(2 ** 20), None, OP.mult, None, ["cli"], ["candA", "candB"])
-        cp(T.xoff[:], T.pre[:], ["pre"], ["xoff"])
-        if t + 1 < R:
-            if t == 0:
-                for i in range(4):
-                    ts(T.P0[:, i:88:4], T.pay[:, 22 * i:22 * i + 22], float(i * 2 ** 18), None, OP.add, None, ["pay"], ["P0_%d" % i])
-            tt(T.base[:], T.cand[:], T.P0[:], OP.add, ["candA", "candB"] + four("P0_"), four("base"))
+                ts(vw("ti", i, 88, 4), vw("cc"), float(3 - i), None, OP.add)
+            ts(vw("ti", 88), vw("ti", 0, 88), 3, None, OP.bitwise_and)
+            ts(vw("prio"), vw("ti", 88), float(2 ** 20), None, OP.mult)
+            tt(vw("base"), vw("prio"), vw("P0"), OP.add)
         else:
-            cp(T.coff[:], T.cc[:], ["cc"], ["coff"])
-            act(T.owb[:], T.i16[:, 0:16].indirect(T.coff[:]), AF.Copy, ["i16", "coff"], ["owb"])
-            dma("Y", "dm9", [(T.ow[:], T.owb[0:128:16, :])], ["owb"], ())
-            quant("Vv", 0, 128, T.vb[:], ["vb"])
+            cp(vw("coff"), vw("cc"))
+            move(vw("owb"), by(vw("n16"), vw("coff")))
+            dma("Y", [(T.ow[:], T.owb[0:128:16, :])], [vw("owb")])
 
-    mm(6, "Vv", 0, "X", 0, HC, ["qVv", "qXA"])
-    dma("Y", "dm10", [(T.oc[:, 0:4 * HC], T.qX[:, 0:HC].bitcast(dt.uint8))], ["qXA"], ())
-    xnew("V", 3, 1)
-    act(T.yb[:, 0:HC], bank(6, HC), AF.Copy, ["ps6"], ["yb0"])
-    quant("X", HC, C, T.X[:, 4 * HC:4 * C], XB, ["qXB"])
-    mm(7, "Vv", 0, "X", HC, HC, ["qVv", "qXB"])
-    dma("S", "dm11", [(T.y[:, 0:HC], T.yb[:, 0:HC])], ["yb0"], ())
-    dma("Y", "dm16", [(T.oc[:, 4 * HC:4 * C], T.qX[:, HC:C].bitcast(dt.uint8))], ["qXB"], ())
-    cp(T.yb[:, HC:C], bank(7, HC), ["ps7"], ["yb1"])
-    dma("S", "dm13", [(T.osc[4 * k:4 * k + 4, :], T.sX[32 * k:32 * k + 4, :]) for k in range(3)], ["qXA", "qXB"], ())
-    dma("Y", "dm14", [(T.osc[12:16, :], T.sX[96:100, :])], ["qXA", "qXB"], ())
-    dma("Y", "dm12", [(T.y[:, HC:C], T.yb[:, HC:C])], ["yb1"], ())
-    need("G", {"sent": count["sent"]})
+    for i, (a, e) in enumerate(XP):
+        mm(6 + i, "Vv", 0, "X", a, e - a)
+        dma("Y", [(T.oc[:, 4 * a:4 * e], T.qX[:, a:e].bitcast(dt.uint8))], [vw("qX", a, e)])
+        move(vw("yb", a, e), bank(6 + i, e - a), None, "SV"[i % 2])
+        dma("SY"[i], [(T.y[:, a:e], T.yb[:, a:e])], [vw("yb", a, e)])
+    dma("S", [(T.osc[4 * k:4 * k + 4, :], T.sX[32 * k:32 * k + 4, :]) for k in range(3)], [vw("sX")])
+    dma("Y", [(T.osc[12:16, :], T.sX[96:100, :])], [vw("sX")])
+
+    count, mark, knew = {}, {}, {}
+    waited = {q: {} for q in Q}
+    if not LAID:
+        LAID.extend(lay_out(tasks))
+    for i in LAID:
+        task = tasks[i]
+        q, w, todo = task["q"], waited[task["q"]], {}
+        for d, waits in task["deps"].items():
+            if waits and w.get(mark[d][0], 0) < mark[d][1]:
+                todo[mark[d][0]] = max(todo.get(mark[d][0], 0), mark[d][1])
+        for sem, val in todo.items():
+            if not any(o != sem and knew[(o, ov)].get(sem, 0) >= val for o, ov in todo.items()):
+                Q[q].wait_ge(T.sem[sem], val)
+        for sem, val in todo.items():
+            for s_, v_ in list(knew[(sem, val)].items()) + [(sem, val)]:
+                w[s_] = max(w.get(s_, 0), v_)
+        calls, sem = task["make"](), task["sem"] or "c" + q
+        if isinstance(calls, tuple):
+            count["sent"] = count.get("sent", 0) + calls[0]
+            count[sem] = calls[1]
+            knew[(sem, count[sem])] = {}
+        else:
+            for call in calls:
+                call.then_inc(T.sem[sem], 16 if task["sem"] else 1)
+                count[sem] = count.get(sem, 0) + (16 if task["sem"] else 1)
+            knew[(sem, count[sem])] = dict(w)
+        mark[i] = (sem, count[sem])
+    g.wait_ge(T.sem.sent, count["sent"])
     for s_, v_ in count.items():
         if s_ != "sent":
             Y.wait_ge(T.sem[s_], v_)

@@ -2,43 +2,50 @@ from concourse.mybir import dt, AluOpType as OP, ActivationFunctionType as AF
 
 C, K, A, R = 384, 128, 352, 3
 XP = [(0, 192), (192, 384)]
-ZP = [(0, 14), (14, 22)]
-FP = [(0, 28), (28, 56), (56, 88)]
-KH = 18
-ZA = 224
+XL = [(0, 256), (256, 384)]
+ZP = [(0, 12), (12, 22)]
+FP = [(0, 24), (24, 48), (48, 80), (80, 88)]
+RP = [(18, 24, 4), (10, 18, 5), (0, 10, 2)]
+ZA = 192
+HW = 528
 BIG = float(2 ** 80)
 TOP = float(2 ** 22)
 LIFT = 2 * TOP
 APART = 7 * 1024
-ON = dict(su="S", e="SSVV", eq="SSSS", x="SSVVSSSV", ph="SSSS", fl="VSS", phb="SSSS", z="SSSSSSSS", h="SSSVSVVV", vt="SSVV")
-ROWS = "V" * 4 + "S" * 13 + "V" * 6
+ON = dict(x="VSVSSVSS", xl="SVVSVSSS", fl="SVSS", phb="SSVV", z="SSSSSSSS", h="SVVSSVSV", vt="SVSV", y="SS", yd="SY", os="YSSY")
+ROWS = "V" * 3 + "S" * 14 + "V" * 6
 TW = [384, 320, 256, 192, 128, 64]
 TO = [0, 384, 704, 960, 1152, 1280]
 SOW = 184
 STEP = 1024.0
-CYC, GA, SC, SAME, OTHER, LOAD, TRIP = 0.83, 1.3, 3.1, 205.0, 205.0, 1900.0, 1500.0
-FIRST = 800.0
-LEAST, FIXED = dict(V=35.0, S=90.0), dict(V=30.0, S=20.0)
-TURNS = 5000
+CYC, GA, SC, SAME, OTHER, LOAD, TRIP = 0.84, 1.2, 1.5, dict(V=182.0, S=240.0, P=180.0, G=180.0, Y=180.0), 212.0, 1300.0, 1980.0
+FIRST = 300.0
+LEAST, FIXED = dict(V=15.0, S=88.0), dict(V=32.0, S=18.0)
+ISSUE = 150.0
+SLOW = dict(V=1.3, S=1.35, P=1.6, G=1.3, Y=1.0, scatter=3.0)
+LOOSE = 100.0
+BOTH = 0.5
+EARLY = 3e-4
+TURNS = 9000
 LAID = []
 
-MASKS = dict(i16=208, w16=32, v16=32, M16=192, Rst=192, rstb=384, MF=512)
+MASKS = dict(i16=208, w16=32, v16=32, M16=192, Rst=192, rstb=384, MF=512, i4=36, w4=32, v4=32)
 PART = {n: ("masks", sum(list(MASKS.values())[:i]), w) for i, (n, w) in enumerate(MASKS.items())}
 
 
 def _scratch():
     s = {"masks": ("sbuf", [128, sum(MASKS.values())], "bfloat16")}
     for n, w in dict(X=1536, ub=512, vb=512, E=512, Ph=2048, Eq=512, TT=5632, tau=4416, so=SOW * 24, dsc=384, Fl=512,
-                     Ft=1408, Z=1408, tmp=1408, Hs=2048, Vt=512, D0=2816, so2=1408, fd=352, Awin=512, cI=528, one=528,
-                     q25=528, cB=512, gm=512, Fs=1408).items():
+                     Ft=1408, Z=1408, tmp=1408, Hs=4 * HW, Vt=512, D0=2816, so2=1408, fd=352, Awin=512, cI=528, one=528,
+                     cB=512, gm=512, Fs=1408).items():
         s[n] = ("sbuf", [128, w], "bfloat16")
     for n, w in dict(n16=16, msk=384, sc=384, sc2=384, ew=384, val=384, s4o=128, eq=16, rowS=24, k16=24, pre0=24, MR=384, cst=24,
-                     rank=24, jw=24, cf=8, cg=8, Ar=352, Lf=112, P0=88, pay=88, base=88, cand=88, c1=44, xs=72,
+                     M4=128, jw=24, cf=8, cg=8, Ar=352, Lf=112, P0=88, pay=88, base=88, cand=88, c1=44, xs=72,
                      prio=88, yb=384, owb=352).items():
         s[n] = ("sbuf", [128, w], "float32")
-    for n, w in dict(pcol=1, ci=2, c2i=22, ot=44, cc=22, ti=176, cli=88, uoffi=8).items():
+    for n, w in dict(pcol=1, ci=4, c2i=22, ot=44, cc=22, cli=88, uoffi=8).items():
         s[n] = ("sbuf", [128, w], "int32")
-    for n, w in dict(uoff=8, roff=24, eoff=8, xoff=24, zoff=44, foff=8, flist=88, c2u=88, Lu=88, coff=22).items():
+    for n, w in dict(uoff=8, roff=24, eoff=32, xoff=24, zoff=44, foff=8, flist=88, c2u=88, Lu=88, coff=22).items():
         s[n] = ("sbuf", [128, w], "uint16")
     pairs = dict(U=128, U2=128, Vv=128, X=384, T=1408, I=512, B=128, L=512, Z=352)
     for t in range(R):
@@ -58,54 +65,80 @@ SEMAPHORES = ["cV", "cS", "cP", "cG", "sent"] + ["arr%d" % i for i in range(2 * 
 
 def lay_out(tasks):
     n = len(tasks)
-    q = [t["q"] for t in tasks]
-    cost = [t["cost"] for t in tasks]
-    pre, post = [[] for _ in tasks], [[] for _ in tasks]
-    for i, t in enumerate(tasks):
-        for d, waits in t["deps"].items():
-            gap = tasks[d]["lag"] + (0.0 if not waits else SAME if q[d] == q[i] and not tasks[d]["lag"] else OTHER)
-            pre[i].append((d, gap))
-            post[d].append((i, gap))
+    cost, lag = [t["cost"] for t in tasks], [t["lag"] for t in tasks]
+    pre, post = [list(t["deps"].items()) for t in tasks], [[] for _ in tasks]
+    for i in range(n):
+        for d, waits in pre[i]:
+            post[d].append((i, waits))
 
-    def lay(order, edges, lead):
+    def lay(order, q, back=False):
         busy, end = {}, [0.0] * n
         for i in order:
-            s = max([end[d] + gap for d, gap in edges[i]], default=lead[i])
+            s, c = lag[i] if back else 0.0, cost[i][q[i]]
+            for d, waits in post[i] if back else pre[i]:
+                late = lag[i if back else d]
+                s = max(s, end[d] + late + (0.0 if not waits else SAME[q[i]] if q[d] == q[i] and not late else OTHER))
             row = busy.setdefault(q[i], [])
             k = len(row)
             while k and row[k - 1][1] > s:
                 k -= 1
-            while k < len(row) and row[k][0] < s + cost[i] - 1e-6:
+            while k < len(row) and row[k][0] < s + c - 1e-6:
                 s = max(s, row[k][1])
                 k += 1
-            row.insert(k, (s, s + cost[i]))
-            end[i] = s + cost[i]
+            row.insert(k, (s, s + c))
+            end[i] = s + c
         return end
-    none, lag, seed = [0.0] * n, [t["lag"] for t in tasks], [1]
 
-    def turn(end):
-        back = lay(sorted(range(n), key=lambda i: (-end[i], -i)), post, lag)
-        return lay(sorted(range(n), key=lambda i: (-back[i], i)), pre, none)
+    def turn(end, q):
+        back = lay(sorted(range(n), key=lambda i: (-end[i], -i)), q, True)
+        return lay(sorted(range(n), key=lambda i: (-back[i], i)), q)
 
-    def span(end):
-        return max(end[i] + lag[i] for i in range(n))
+    def in_order(end, q):
+        return sorted(range(n), key=lambda i: (end[i] - cost[i][q[i]], i))
+
+    def worth(end, q):
+        free, slow = {}, [0.0] * n
+        for i in in_order(end, q):
+            s = free.get(q[i], 0.0)
+            for d, waits in pre[i]:
+                s = max(s, slow[d] + lag[d] + (0.0 if not waits else SAME[q[i]] if q[d] == q[i] and not lag[d] else OTHER))
+            free[q[i]] = slow[i] = s + cost[i][q[i]] * SLOW[tasks[i].get("kind", q[i])]
+        return max(end[i] + lag[i] for i in range(n)) + BOTH * max(slow[i] + lag[i] for i in range(n)) + EARLY * sum(end)
+    seed = [4]
 
     def draw():
         seed[0] = (seed[0] * 1103515245 + 12345) % 2 ** 31
         return seed[0] / 2 ** 31
-    best = turn(lay(range(n), pre, none))
+    place = {t["tag"]: i for i, t in enumerate(tasks)}
+    twins = [[(place[(r,) + t["tag"][1:]], place[t["tag"][:2] + (0,)], place[(r, t["tag"][1], 0)]) for r in range(R + 1)
+              if r != t["tag"][0] and (r,) + t["tag"][1:] in place] for t in tasks]
+    on = [t["q"] for t in tasks]
+    best = turn(lay(range(n), on), on)
+    least = worth(best, on)
     for j in range(TURNS):
-        at, width, amp = draw() * span(best), (2000.0, 5000.0)[j % 2], (300.0, 1000.0, 2000.0)[j % 3]
-        key = [0.0] * n
+        at, width, amp = draw() * max(best), (1500.0, 4000.0)[j % 2], (300.0, 600.0, 1000.0, 2000.0, 600.0)[j % 5]
+        q, near = list(on), [i for i in range(n) if abs(best[i] - at) < width]
+        free = [i for i in near if len(cost[i]) > 1]
+        for _ in range((0, 1, 0, 2, 0, 1, 0)[j % 7] if free else 0):
+            i = free[int(draw() * len(free))]
+            other = "V" if q[i] == "S" else "S"
+            for o in [i] + [x[0] for x in twins[i]]:
+                q[o] = other
+        key = [best[i] - cost[i][on[i]] for i in range(n)]
+        for i in near:
+            key[i] += (draw() - 0.5) * amp
+            if j % 3:
+                for o, a, b in twins[i]:
+                    key[o] = key[i] - best[a] + best[b]
         for i in range(n):
-            own = best[i] - cost[i] + ((draw() - 0.5) * amp if abs(best[i] - at) < width else 0.0)
-            key[i] = max([own] + [key[d] for d, _ in pre[i]])
-        end = lay(sorted(range(n), key=lambda i: (key[i], i)), pre, none)
+            key[i] = max([key[i]] + [key[d] for d, _ in pre[i]])
+        end = lay(sorted(range(n), key=lambda i: (key[i], i)), q)
         if j % 4 == 0:
-            end = turn(end)
-        if span(end) <= span(best):
-            best = end
-    return sorted(range(n), key=lambda i: (best[i] - cost[i], i))
+            end = turn(end, q)
+        w = worth(end, q)
+        if w <= least + LOOSE * (1.0 - j / TURNS) ** 2 * draw():
+            best, on, least = end, q, w
+    return [(i, on[i]) for i in in_order(best, on)]
 
 
 def rank_program(g, core, T, topo):
@@ -116,7 +149,7 @@ def rank_program(g, core, T, topo):
     after, before = T.cores[(rank + 1) % n], T.cores[(rank - 1) % n]
     V, S, P, Y = g.vector, g.scalar, g.tensor, g.sync
     Q = {"V": V, "S": S, "P": P, "G": g, "Y": Y}
-    tasks, touched, masks, dmas, behind = [], {}, {}, [0], []
+    tasks, touched, masks, dmas, behind, tag = [], {}, {}, [0], [], [0, "set-up", 0]
 
     def vw(name, a=0, b=None, step=1):
         if name in PART:
@@ -142,7 +175,7 @@ def rank_program(g, core, T, topo):
     def ap(x):
         return x[0] if isinstance(x, tuple) else x
 
-    def add(q, cost, make, r, w, sem=None, lag=0.0, acc=False):
+    def add(q, cost, make, r, w, sem=None, lag=0.0, acc=False, either=False):
         r = [x for x in r if isinstance(x, tuple)]
         r += [x[5] for x in r + w if x[5] is not None]
         deps, me = {d: False for d in behind if tasks[d]["q"] == q}, len(tasks)
@@ -151,13 +184,14 @@ def rank_program(g, core, T, topo):
                 if m & x[2] and d != me:
                     if wr and writes and acc:
                         deps.setdefault(d, False)
-                    elif wr or writes or x[1] == "ps" and tasks[d]["q"] != q:
+                    elif wr or writes or x[1] == "ps" and (tasks[d]["q"] != q or either or len(tasks[d]["cost"]) > 1):
                         deps[d] = True
         for x in w:
             touched[x[1]] = [e for e in touched.get(x[1], []) if e[0] & ~x[2]]
         for x, writes in [(x, False) for x in r] + [(x, True) for x in w]:
             touched.setdefault(x[1], []).append((x[2], me, writes))
-        tasks.append(dict(q=q, cost=cost, make=make, deps=deps, sem=sem, lag=lag))
+        tasks.append(dict(q=q, cost={q: cost}, make={q: make}, deps=deps, sem=sem, lag=lag, tag=tuple(tag)))
+        tag[2] += 1
 
     def length(q, out, a, each=1.0):
         if out[5] is not None:
@@ -195,37 +229,32 @@ def rank_program(g, core, T, topo):
         given = {k: ap(x) for k, x in kw.items()}
         if sums is not None:
             given["accum_out"] = sums[0]
-        add("S", length("S", out, a) + (20 if sums else 0), lambda: [S.activation(out[0], a[0], f, **given)],
+        add("S", length("S", out, a) + (30 if sums else 0), lambda: [S.activation(out[0], a[0], f, **given)],
             [a] + list(kw.values()), [out] + ([sums] if sums else []))
 
     def move(out, a, c=None, on="S"):
-        if on == "S":
-            act(out, a, AF.Copy, **({} if c is None else {"scale": c}))
-        elif c is None:
-            cp(out, a)
-        else:
-            ts(out, a, c, None, OP.mult)
+        make = dict(S=lambda: [S.activation(out[0], a[0], AF.Copy, **({} if c is None else {"scale": c}))],
+                    V=lambda: [V.tensor_copy(out[0], a[0]) if c is None else V.tensor_scalar(out[0], a[0], c, None, OP.mult)])
+        add(on, 0.0, None, [a], [out], either=True)
+        tasks[-1].update(cost=dict(S=length("S", out, a), V=length("V", out, a, half(out, a))), make=make)
 
     def quant(name, a, b, src):
         c, s = vw("q" + name, a, b), vw("s" + name, a, b)
-        add("V", 12 + 0.22 * src[3], lambda: [V.quantize_mx(c[0], s[0], src[0])], [src], [c, s])
+        add("V", 33 + 0.22 * src[3], lambda: [V.quantize_mx(c[0], s[0], src[0])], [src], [c, s])
 
     def mm(b, st, sa, mv, ma, w, start=True, stop=True):
         x = [vw("q" + st, sa, sa + 128), vw("s" + st, sa, sa + 128), vw("q" + mv, ma, ma + w), vw("s" + mv, ma, ma + w)]
         out = bank(b, w)
-        add("P", (w + 16) * CYC, lambda: [P.matmul_mx(out[0], x[0][0], x[1][0], x[2][0], x[3][0], start, stop)], x, [out],
+        add("P", (w + 16) * 0.4, lambda: [P.matmul_mx(out[0], x[0][0], x[1][0], x[2][0], x[3][0], start, stop)], x, [out],
             acc=not start)
 
     def iota(out, pat, base=0, mult=0):
         kw = {} if SCRATCH[out[1]][2] == "int32" else {"allow_small_or_imprecise_dtypes": True}
         add("G", 130 + 2 * CYC * out[3], lambda: [g.iota(out[0], pat, base, mult, **kw)], [], [out])
 
-    def where0(out, a, pat, base, mult):
-        add("G", 170 + 2 * CYC * out[3], lambda: [g.affine_select(out[0], a[0], pat, OP.is_equal, 0.0, base, mult)], [a], [out])
-
     def dma(q, pairs, r=(), w=(), lag=LOAD):
         dmas[0] += 1
-        add(q, 60.0 * len(pairs), lambda: [Q[q].dma_start(o, i) for o, i in pairs], list(r), list(w), "dm%d" % dmas[0], lag)
+        add(q, ISSUE * len(pairs), lambda: [Q[q].dma_start(o, i) for o, i in pairs], list(r), list(w), "dm%d" % dmas[0], lag)
 
     def exchange(src, dst, to, frm, sem):
         rid, pid, _ = topo.addr(to)
@@ -235,7 +264,7 @@ def rank_program(g, core, T, topo):
             g.remote_dma(T["q" + dst][:].bitcast(dt.uint8), T["q" + src][:].bitcast(dt.uint8), T.sem[sem], T.sem.sent, pid, rid, m)
             g.remote_dma(T["s" + dst][:], T["s" + src][:], T.sem[sem], T.sem.sent, pid, rid, m)
             return (2 * len(topo.engines(core, to)), 2 * len(topo.engines(frm, core)))
-        add("G", 200.0, make, [vw("q" + src), vw("s" + src)], [vw("q" + dst), vw("s" + dst)], sem, TRIP + FIRST * (sem == "arr0"))
+        add("G", 390.0 + FIRST * (sem == "arr0"), make, [vw("q" + src), vw("s" + src)], [vw("q" + dst), vw("s" + dst)], sem, TRIP)
 
     def col(name, j):
         return vw(name, j, j + 1)
@@ -246,9 +275,9 @@ def rank_program(g, core, T, topo):
     def const(out, c):
         move(out, vw("one", 0, out[3]), c)
 
-    dma("S", [(T.ub[:], T.u[:])], (), [vw("ub")])
+    dma("S", [(T.ub[:], T.u[:])], (), [vw("ub")], LOAD + 420)
     for a, b in XP:
-        dma("Y", [(T.X[:, 4 * a:4 * b], T.x[:, 4 * a:4 * b])], (), [vw("X", 4 * a, 4 * b)], LOAD + 500)
+        dma("Y", [(T.X[:, 4 * a:4 * b], T.x[:, 4 * a:4 * b])], (), [vw("X", 4 * a, 4 * b)], LOAD + 3.4 * (b - a))
     dma("Y", [(T.cli[:], T.cl[:])], (), [vw("cli")])
     dma("Y", [(T.qL[:].bitcast(dt.uint8), T.wc[:]), (T.sL[:], T.ws[:])], [vw("X")], [vw("qL"), vw("sL")])
     dma("Y", [(T.vb[:], T.v[:])], [vw("X")], [vw("vb")])
@@ -259,25 +288,36 @@ def rank_program(g, core, T, topo):
     iota(vw("i16"), [[0, 13], [1, 16]])
     iota(vw("k16"), [[16, 24]])
     iota(vw("gm"), [[1, 8], [0, 64]])
-    iota(vw("val"), [[1, C]])
+    iota(vw("val"), [[4, C]])
     iota(vw("n16"), [[1, 16]])
     iota(vw("fd", 0, ZA), [[1, ZA]])
     iota(vw("fd", ZA, A), [[2, A - ZA]], ZA)
     const(vw("Awin", 0, C), float(APART))
     fill(vw("rstb"), 1.0)
-    fill(col("rowS", 0), 0.0)
+    fill(col("rowS", 0) if ROWS[0] == "S" else col("so", SOW - 1), 0.0)
     fill(vw("rstb", 0, C, 16), 0.0)
-    const(vw("q25"), 0.25)
     for m in range(6):
         const(vw("TT", 4 * (TO[m] + 16 * (21 - 4 * m)), 4 * (TO[m] + TW[m])), 0.0)
     for b in range(4):
-        const(vw("Hs", 512 * b + ZA, 512 * b + 512), 0.0)
-    where0(vw("cI"), vw("q25"), [[-1, 528]], 3, 4)
+        const(vw("Hs", HW * b + ZA, HW * b + HW), 0.0)
+    iota(vw("cI"), [[0, 528]])
+    add("G", 170 + 2 * CYC * 528, lambda: [g.affine_select(T.cI[:], T.cI[:], [[-1, 528]], OP.not_equal, 0.25, 3, 4)],
+        [vw("cI")], [vw("cI")])
     const(vw("Ft", 0, 512), 0.0)
     ts(col("ci", 0), vw("pcol"), 15, None, OP.bitwise_and)
     ts(col("ci", 1), vw("pcol"), 4, None, OP.arith_shift_right)
     cp(vw("uoff"), vw("uoffi"))
-    cp(vw("cf", 0, 2), vw("ci"))
+    ts(col("ci", 2), vw("pcol"), 3, None, OP.bitwise_and)
+    ts(col("ci", 3), vw("pcol"), 2, 3, OP.arith_shift_right, OP.bitwise_and)
+    cp(vw("cf", 0, 4), vw("ci"))
+    iota(vw("i4"), [[0, 9], [1, 4]])
+    ts(vw("v4"), vw("i4", 0, 32), col("cf", 3), -BIG, OP.is_equal, OP.mult)
+    ts(vw("w4"), vw("i4", 3, 35), col("cf", 3), 2 * STEP, OP.is_equal, OP.mult)
+    tt(vw("M4", 0, 32), vw("w4"), vw("v4"), OP.add)
+    move(vw("M4", 32, 64), vw("M4", 0, 32))
+    move(vw("M4", 64, 128), vw("M4", 0, 64))
+    ts(col("cg", 4), col("cf", 3), 3.0, -2 * STEP, OP.is_lt, OP.mult)
+    ts(col("cg", 5), col("cg", 4), col("cf", 2), None, OP.add)
     pr, pg = col("cf", 0), col("cf", 1)
     lift = col("cg", 0)
     ts(lift, pr, 15.0, -LIFT, OP.is_lt, OP.mult)
@@ -309,8 +349,7 @@ def rank_program(g, core, T, topo):
         quant("I", 128 * b, 128 * b + 128, vw("cI", 3 - b, 515 - b))
     quant("U", 0, 128, vw("ub"))
     cp((T.qU2[:].bitcast(dt.uint32),) + vw("qU2")[1:], by(vw("qU"), vw("uoff"), True))
-    move(vw("sU2"), by(vw("sU"), vw("uoff")), None, ON["su"])
-    runs = [(k, k + len(ROWS[k - 1:].split("S")[0])) for k in range(1, 24) if ROWS[k - 1] == "V" and (k == 1 or ROWS[k - 2] == "S")]
+    move(vw("sU2"), by(vw("sU"), vw("uoff")))
 
     d2 = (None, "d2", 1, 1, True, None)
     for a in range(4):
@@ -324,8 +363,9 @@ def rank_program(g, core, T, topo):
     act(vw("prio"), vw("Lf", 22, 110), AF.Identity, scale=512.0, bias=lift)
     tt(vw("pay"), vw("prio"), vw("Lf", 0, 88), OP.add)
     for i in range(4):
-        act(vw("P0", i, 88, 4), vw("pay", 22 * i, 22 * i + 22), AF.Identity, bias=float(i * 2 ** 18))
-        act(vw("base", i, 88, 4), vw("pay", 22 * i, 22 * i + 22), AF.Identity, bias=float(i * 2 ** 18 + (3 - i) * 2 ** 20))
+        act(vw("P0", i, 88, 4), vw("pay", 22 * i, 22 * i + 22), AF.Identity, bias=float((3 - i) * 2 ** 18))
+    act(vw("base"), vw("P0"), AF.Identity, bias=float(2 ** 20))
+    const(vw("prio", 3, 88, 4), float(2 ** 20))
 
     def row(k, a, b):
         m, s = (24 - k) // 4, (24 - k) % 4
@@ -334,17 +374,32 @@ def rank_program(g, core, T, topo):
     def position(m):
         return (16 * m, 1) if 16 * m < ZA else (32 * m - ZA, 2)
 
+    def new_places():
+        xa, xb, xc = (vw("xs", 24 * j, 24 * j + 24) for j in range(3))
+        ts(xa, vw("roff"), float(K), STEP, OP.is_lt, OP.mult)
+        ts(xb, vw("roff"), float(C), None, OP.add)
+        tt(xc, xa, xb, OP.min)
+        tt(xa, xc, vw("jw"), OP.max)
+        cp(vw("xoff"), xa)
+
+    def sums_of(a):
+        last = min((27 - a) // 4 - 1, 4)
+        return last, min(16 * a, TW[last] - 128)
+
     for t in range(R + 1):
         behind.clear()
+        tag[:] = [t, "state" if t < R else "last state", 0]
         if t > 0:
             for b in range(4):
                 mm(b, "I", 128 * b, "H%d" % (t - 1), 0, K)
             for b in range(4):
                 tt(vw("Ph", 512 * b + C, 512 * b + 512), bank(b, K), vw("Eq", K * b, K * b + K), OP.add)
-            for i, (a, e) in enumerate(XP):
+            for i, (a, e) in enumerate(XP if t < R else XL):
                 for b in range(4):
-                    move(vw("X", 4 * a + b, 4 * e, 4), by(plane("Ph", b), vw("xoff", a // 16, e // 16)), 2.0, ON["x"][4 * i + b])
-        for a, e in XP:
+                    move(vw("X", 4 * a + b, 4 * e, 4), by(plane("Ph", b), vw("xoff", a // 16, e // 16)), 2.0,
+                         ON["x" if t < R else "xl"][4 * i + b])
+        tag[:] = [t, "ranks" if t < R else "outputs", 0]
+        for a, e in XP if t < R else XL:
             quant("X", a, e, vw("X", 4 * a, 4 * e))
         if t == R:
             break
@@ -372,27 +427,42 @@ def rank_program(g, core, T, topo):
         for m in range(5):
             w = TW[m] + TW[5] * (m == 4)
             quant("T", TO[m], TO[m] + w, vw("TT", 4 * TO[m], 4 * (TO[m] + w)))
-            if m < 2:
-                mm(4, "B", 0, "T", TO[m] + 192, TW[m] - 192, m == 0, m == 1)
-            mm(2, "B", 0, "T", TO[m], min(TW[m], 16 * KH), m == 0, False)
-        mm(2, "B", 0, "T", TO[5], 128, False, True)
+            for a, e, b in RP:
+                last, c0 = sums_of(a)
+                if m <= last:
+                    mm(b, "B", 0, "T", TO[m] + c0, min(TW[m], 16 * e) - c0, m == 0, m == last and a > 0)
+        mm(RP[-1][2], "B", 0, "T", TO[5], 128, False, True)
         tt(vw("pre0"), vw("cst"), vw("dsc", 15, C, 16), OP.subtract)
-        for a, e in runs:
-            cp(vw("rowS", a, e), vw("so", SOW * (a + 1) - 1, SOW * e, SOW))
-        for a, e, sums in ((KH, 24, bank(4, 192, 16 * KH - 192)), (0, KH, bank(2, 16 * KH))):
-            tt(vw("MR", 16 * a + 15, 16 * e, 16), vw("pre0", a, e), vw("rowS", a, e), OP.subtract)
+        for a, e, b in RP:
+            sums = bank(b, 16 * e - sums_of(a)[1], 16 * a - sums_of(a)[1])
+            k = a
+            while k < e:
+                j, q = k + 1, (ROWS[0] + ROWS)[k]
+                while j < e and ROWS[j - 1] == q:
+                    j += 1
+                got = vw("so", SOW * (k + 1) - 1, SOW * j, SOW) if q == "V" else vw("rowS", k, j)
+                tt(vw("MR", 16 * k + 15, 16 * j, 16), vw("pre0", k, j), got, OP.subtract)
+                k = j
             scan(vw("sc2", 16 * a, 16 * e), sums, vw("MR", 16 * a, 16 * e), -1.0, OP.max, OP.add)
             ts(vw("roff", a, e), vw("sc2", 16 * a + 15, 16 * e, 16), STEP, None, OP.add)
             cp(by(vw("ew"), vw("roff", a, e)), vw("val", 16 * a, 16 * e))
-        wrap(vw("s4o"), vw("ew", 0, K))
-        ts(vw("eoff"), vw("s4o", 15, K, 16), lift, None, OP.add)
+            tasks[-1]["kind"] = "scatter"
+        scan(vw("s4o"), vw("M4"), vw("ew", 0, K), 0.0, OP.add, OP.max)
+        ts(vw("eoff"), vw("s4o", 3, K, 4), col("cg", 5), None, OP.add)
+        for a in (0, 16):
+            move(vw("E", 16 * a, 16 * a + 256), by(vw("X"), vw("eoff", a, a + 16)), None, "VS"[a // 16])
         for b in range(4):
-            move(plane("Ph", b, C), vw("X", b, 4 * C, 4), 0.5, ON["ph"][b])
-            move(vw("E", b, 512, 4), by(plane("Ph", b, C), vw("eoff")), 2.0, ON["e"][b])
+            move(plane("Ph", b, C), vw("X", b, 4 * C, 4), 0.5)
         act(vw("Fl", 0, C), bank(1, C), AF.Sign)
         act(vw("Fl", 0, C), vw("Fl", 0, C), AF.Relu, scale=TOP)
         quant("E%d" % t, 0, K, vw("E"))
+        behind.append(len(tasks) - 1)
         exchange("E%d" % t, "G%d" % t, after, before, "arr%d" % (2 * t))
+        if t:
+            tag[:] = [t, "lists", 0]
+            new_places()
+        behind.clear()
+        tag[:] = [t, "layer", 0]
         Gn = "G%d" % t
         mm(3, "U2", 0, Gn, 0, K)
         for b in range(4):
@@ -421,7 +491,7 @@ def rank_program(g, core, T, topo):
             o, step = position(a)
             for b in range(4):
                 mm(4 * (i % 2) + b, "L", 128 * b, "Z", 16 * a, 16 * (e - a))
-                move(vw("Hs", 512 * b + o, 512 * b + o + 16 * (e - a) * step, step), bank(4 * (i % 2) + b, 16 * (e - a)), 0.03125,
+                move(vw("Hs", HW * b + o, HW * b + o + 16 * (e - a) * step, step), bank(4 * (i % 2) + b, 16 * (e - a)), 0.03125,
                      ON["h"][4 * i + b])
         for s in range(8):
             if s:
@@ -431,49 +501,40 @@ def rank_program(g, core, T, topo):
                  float(2 * A - ZA), OP.min, OP.min)
         cp(vw("foff"), vw("so2", A // 2 - 1, 4 * A, A // 2))
         for b in range(4):
-            move(vw("Vt", b, 512, 4), by(plane("Hs", b), vw("foff")), None, ON["vt"][b])
+            move(vw("Vt", b, 512, 4), by(vw("Hs", HW * b, HW * b + HW), vw("foff")), None, ON["vt"][b])
         quant("V%d" % t, 0, K, vw("Vt"))
         behind.append(len(tasks) - 1)
+        tag[:] = [t, "rest %d" % t, 0]
         exchange("V%d" % t, "H%d" % t, before, after, "arr%d" % (2 * t + 1))
         for b in range(4):
-            move(vw("Eq", K * b, K * b + K), vw("E", b, 512, 4), 0.25, ON["eq"][b])
-        xa, xb, xc = (vw("xs", 24 * j, 24 * j + 24) for j in range(3))
-        cp(vw("rank"), vw("roff"))
-        ts(xa, vw("rank"), float(K), None, OP.is_lt)
-        tt(xb, vw("rank"), vw("jw"), OP.subtract)
-        ts(xc, xb, float(C), None, OP.add)
-        tt(xb, xc, xa, OP.mult)
-        tt(xc, xb, vw("jw"), OP.add)
-        cp(vw("xoff"), xc)
+            move(vw("Eq", K * b, K * b + K), vw("E", b, 512, 4), 0.25)
         if t == 0:
+            new_places()
             quant("Vv", 0, 128, vw("vb"))
         ts(vw("cc"), vw("c2i"), 18, 3, OP.arith_shift_right, OP.bitwise_and)
         if t + 1 < R:
-            for i in range(4):
-                ts(vw("ti", i, 88, 4), vw("cc"), float(3 - i), None, OP.add)
-            ts(vw("ti", 88), vw("ti", 0, 88), 3, None, OP.bitwise_and)
-            ts(vw("prio"), vw("ti", 88), float(2 ** 20), None, OP.mult)
+            for i in range(3):
+                ts(vw("prio", i, 88, 4), vw("cc"), float(3 - i), float(2 ** 20), OP.is_ge, OP.mult)
             tt(vw("base"), vw("prio"), vw("P0"), OP.add)
         else:
-            cp(vw("coff"), vw("cc"))
+            ts(vw("coff"), vw("cc"), -1.0, 3.0, OP.mult, OP.add)
             move(vw("owb"), by(vw("n16"), vw("coff")))
             dma("Y", [(T.ow[:], T.owb[0:128:16, :])], [vw("owb")])
 
-    for i, (a, e) in enumerate(XP):
-        mm(6 + i, "Vv", 0, "X", a, e - a)
-        dma("Y", [(T.oc[:, 4 * a:4 * e], T.qX[:, a:e].bitcast(dt.uint8))], [vw("qX", a, e)])
-        move(vw("yb", a, e), bank(6 + i, e - a), None, "SV"[i % 2])
-        dma("SY"[i], [(T.y[:, a:e], T.yb[:, a:e])], [vw("yb", a, e)])
-    dma("S", [(T.osc[4 * k:4 * k + 4, :], T.sX[32 * k:32 * k + 4, :]) for k in range(3)], [vw("sX")])
-    dma("Y", [(T.osc[12:16, :], T.sX[96:100, :])], [vw("sX")])
+    for i, (a, e) in enumerate(XL):
+        mm(5 + i, "Vv", 0, "X", a, e - a)
+        dma("Y", [(T.oc[:, 4 * a:4 * e], T.qX[:, a:e].bitcast(dt.uint8))], [vw("qX", a, e)], (), LOAD + 1.7 * (e - a))
+        move(vw("yb", a, e), bank(5 + i, e - a), None, ON["y"][i])
+        dma(ON["yd"][i], [(T.y[:, a:e], T.yb[:, a:e])], [vw("yb", a, e)], (), LOAD + 1.7 * (e - a))
+    for k in range(4):
+        dma(ON["os"][k], [(T.osc[4 * k:4 * k + 4, :], T.sX[32 * k:32 * k + 4, :])], [vw("sX")], (), LOAD - 200)
 
     count, mark, knew = {}, {}, {}
     waited = {q: {} for q in Q}
     if not LAID:
         LAID.extend(lay_out(tasks))
-    for i in LAID:
-        task = tasks[i]
-        q, w, todo = task["q"], waited[task["q"]], {}
+    for i, q in LAID:
+        task, w, todo = tasks[i], waited[q], {}
         for d, waits in task["deps"].items():
             if waits and w.get(mark[d][0], 0) < mark[d][1]:
                 todo[mark[d][0]] = max(todo.get(mark[d][0], 0), mark[d][1])
@@ -483,7 +544,7 @@ def rank_program(g, core, T, topo):
         for sem, val in todo.items():
             for s_, v_ in list(knew[(sem, val)].items()) + [(sem, val)]:
                 w[s_] = max(w.get(s_, 0), v_)
-        calls, sem = task["make"](), task["sem"] or "c" + q
+        calls, sem = task["make"][q](), task["sem"] or "c" + q
         if isinstance(calls, tuple):
             count["sent"] = count.get("sent", 0) + calls[0]
             count[sem] = calls[1]

from concourse.mybir import dt, AluOpType as OP, ActivationFunctionType as AF

C, K, A, R = 384, 128, 352, 3
XP = [(0, 192), (192, 384)]
XL = [(0, 256), (256, 384)]
ZP = [(0, 12), (12, 22)]
FP = [(0, 24), (24, 48), (48, 80), (80, 88)]
RP = [(18, 24, 4), (10, 18, 5), (0, 10, 2)]
ZA = 192
HW = 528
BIG = float(2 ** 80)
TOP = float(2 ** 22)
LIFT = 2 * TOP
APART = 7 * 1024
ON = dict(x="VSVSSVSS", xl="SVVSVSSS", fl="SVSS", phb="SSVV", z="SSSSSSSS", h="SVVSSVSV", vt="SVSV", y="SS", yd="SY", os="YSSY")
ROWS = "V" * 3 + "S" * 14 + "V" * 6
TW = [384, 320, 256, 192, 128, 64]
TO = [0, 384, 704, 960, 1152, 1280]
SOW = 184
STEP = 1024.0
CYC, GA, SC, SAME, OTHER, LOAD, TRIP = 0.84, 1.2, 1.5, dict(V=182.0, S=240.0, P=180.0, G=180.0, Y=180.0), 212.0, 1300.0, 1980.0
FIRST = 300.0
LEAST, FIXED = dict(V=15.0, S=88.0), dict(V=32.0, S=18.0)
ISSUE = 150.0
SLOW = dict(V=1.3, S=1.35, P=1.6, G=1.3, Y=1.0, scatter=3.0)
LOOSE = 100.0
BOTH = 0.5
EARLY = 3e-4
TURNS = 9000
LAID = []

MASKS = dict(i16=208, w16=32, v16=32, M16=192, Rst=192, rstb=384, MF=512, i4=36, w4=32, v4=32)
PART = {n: ("masks", sum(list(MASKS.values())[:i]), w) for i, (n, w) in enumerate(MASKS.items())}


def _scratch():
    s = {"masks": ("sbuf", [128, sum(MASKS.values())], "bfloat16")}
    for n, w in dict(X=1536, ub=512, vb=512, E=512, Ph=2048, Eq=512, TT=5632, tau=4416, so=SOW * 24, dsc=384, Fl=512,
                     Ft=1408, Z=1408, tmp=1408, Hs=4 * HW, Vt=512, D0=2816, so2=1408, fd=352, Awin=512, cI=528, one=528,
                     cB=512, gm=512, Fs=1408).items():
        s[n] = ("sbuf", [128, w], "bfloat16")
    for n, w in dict(n16=16, msk=384, sc=384, sc2=384, ew=384, val=384, s4o=128, eq=16, rowS=24, k16=24, pre0=24, MR=384, cst=24,
                     M4=128, jw=24, cf=8, cg=8, Ar=352, Lf=112, P0=88, pay=88, base=88, cand=88, c1=44, xs=72,
                     prio=88, yb=384, owb=352).items():
        s[n] = ("sbuf", [128, w], "float32")
    for n, w in dict(pcol=1, ci=4, c2i=22, ot=44, cc=22, cli=88, uoffi=8).items():
        s[n] = ("sbuf", [128, w], "int32")
    for n, w in dict(uoff=8, roff=24, eoff=32, xoff=24, zoff=44, foff=8, flist=88, c2u=88, Lu=88, coff=22).items():
        s[n] = ("sbuf", [128, w], "uint16")
    pairs = dict(U=128, U2=128, Vv=128, X=384, T=1408, I=512, B=128, L=512, Z=352)
    for t in range(R):
        for n in ("E", "G", "V", "H"):
            pairs[n + str(t)] = 128
    for n, w in pairs.items():
        s["q" + n] = ("sbuf", [128, w], "float8_e4m3fn_x4")
        s["s" + n] = ("sbuf", [128, w], "uint8")
    s["d2"] = ("dram", [8, 4, 4, 4, 22], "uint16")
    s["ps"] = ("psum", [128, 4096], "float32")
    return s


SCRATCH = _scratch()
SEMAPHORES = ["cV", "cS", "cP", "cG", "sent"] + ["arr%d" % i for i in range(2 * R)] + ["dm%d" % i for i in range(24)]


def lay_out(tasks):
    n = len(tasks)
    cost, lag = [t["cost"] for t in tasks], [t["lag"] for t in tasks]
    pre, post = [list(t["deps"].items()) for t in tasks], [[] for _ in tasks]
    for i in range(n):
        for d, waits in pre[i]:
            post[d].append((i, waits))

    def lay(order, q, back=False):
        busy, end = {}, [0.0] * n
        for i in order:
            s, c = lag[i] if back else 0.0, cost[i][q[i]]
            for d, waits in post[i] if back else pre[i]:
                late = lag[i if back else d]
                s = max(s, end[d] + late + (0.0 if not waits else SAME[q[i]] if q[d] == q[i] and not late else OTHER))
            row = busy.setdefault(q[i], [])
            k = len(row)
            while k and row[k - 1][1] > s:
                k -= 1
            while k < len(row) and row[k][0] < s + c - 1e-6:
                s = max(s, row[k][1])
                k += 1
            row.insert(k, (s, s + c))
            end[i] = s + c
        return end

    def turn(end, q):
        back = lay(sorted(range(n), key=lambda i: (-end[i], -i)), q, True)
        return lay(sorted(range(n), key=lambda i: (-back[i], i)), q)

    def in_order(end, q):
        return sorted(range(n), key=lambda i: (end[i] - cost[i][q[i]], i))

    def worth(end, q):
        free, slow = {}, [0.0] * n
        for i in in_order(end, q):
            s = free.get(q[i], 0.0)
            for d, waits in pre[i]:
                s = max(s, slow[d] + lag[d] + (0.0 if not waits else SAME[q[i]] if q[d] == q[i] and not lag[d] else OTHER))
            free[q[i]] = slow[i] = s + cost[i][q[i]] * SLOW[tasks[i].get("kind", q[i])]
        return max(end[i] + lag[i] for i in range(n)) + BOTH * max(slow[i] + lag[i] for i in range(n)) + EARLY * sum(end)
    seed = [4]

    def draw():
        seed[0] = (seed[0] * 1103515245 + 12345) % 2 ** 31
        return seed[0] / 2 ** 31
    place = {t["tag"]: i for i, t in enumerate(tasks)}
    twins = [[(place[(r,) + t["tag"][1:]], place[t["tag"][:2] + (0,)], place[(r, t["tag"][1], 0)]) for r in range(R + 1)
              if r != t["tag"][0] and (r,) + t["tag"][1:] in place] for t in tasks]
    on = [t["q"] for t in tasks]
    best = turn(lay(range(n), on), on)
    least = worth(best, on)
    for j in range(TURNS):
        at, width, amp = draw() * max(best), (1500.0, 4000.0)[j % 2], (300.0, 600.0, 1000.0, 2000.0, 600.0)[j % 5]
        q, near = list(on), [i for i in range(n) if abs(best[i] - at) < width]
        free = [i for i in near if len(cost[i]) > 1]
        for _ in range((0, 1, 0, 2, 0, 1, 0)[j % 7] if free else 0):
            i = free[int(draw() * len(free))]
            other = "V" if q[i] == "S" else "S"
            for o in [i] + [x[0] for x in twins[i]]:
                q[o] = other
        key = [best[i] - cost[i][on[i]] for i in range(n)]
        for i in near:
            key[i] += (draw() - 0.5) * amp
            if j % 3:
                for o, a, b in twins[i]:
                    key[o] = key[i] - best[a] + best[b]
        for i in range(n):
            key[i] = max([key[i]] + [key[d] for d, _ in pre[i]])
        end = lay(sorted(range(n), key=lambda i: (key[i], i)), q)
        if j % 4 == 0:
            end = turn(end, q)
        w = worth(end, q)
        if w <= least + LOOSE * (1.0 - j / TURNS) ** 2 * draw():
            best, on, least = end, q, w
    return [(i, on[i]) for i in in_order(best, on)]


def rank_program(g, core, T, topo):
    rank = T.rank_of(core)
    if rank is None:
        return
    n = len(T.cores)
    after, before = T.cores[(rank + 1) % n], T.cores[(rank - 1) % n]
    V, S, P, Y = g.vector, g.scalar, g.tensor, g.sync
    Q = {"V": V, "S": S, "P": P, "G": g, "Y": Y}
    tasks, touched, masks, dmas, behind, tag = [], {}, {}, [0], [], [0, "set-up", 0]

    def vw(name, a=0, b=None, step=1):
        if name in PART:
            name, o, w = PART[name]
            a, b = o + a, o + (w if b is None else b)
        where, shape, kind = SCRATCH[name]
        b = shape[1] if b is None else b
        if (a, b, step) not in masks:
            masks[(a, b, step)] = sum(1 << i for i in range(a, b, step))
        m = masks[(a, b, step)]
        if where == "psum":
            m = ((1 << 512) - 1) << (a // 512 * 512)
        return (T[name][:, a:b:step] if step > 1 else T[name][:, a:b], name, m, len(range(a, b, step)),
                kind in ("bfloat16", "uint16"), None)

    def by(win, off, words=False):
        ap = win[0].bitcast(dt.uint32) if words else win[0]
        return (ap.indirect(off[0]), win[1], win[2], 16 * off[3], win[4], off)

    def bank(b, w, a=0):
        return vw("ps", 512 * b + a, 512 * b + w)

    def ap(x):
        return x[0] if isinstance(x, tuple) else x

    def add(q, cost, make, r, w, sem=None, lag=0.0, acc=False, either=False):
        r = [x for x in r if isinstance(x, tuple)]
        r += [x[5] for x in r + w if x[5] is not None]
        deps, me = {d: False for d in behind if tasks[d]["q"] == q}, len(tasks)
        for x, writes in [(x, False) for x in r] + [(x, True) for x in w]:
            for m, d, wr in touched.get(x[1], []):
                if m & x[2] and d != me:
                    if wr and writes and acc:
                        deps.setdefault(d, False)
                    elif wr or writes or x[1] == "ps" and (tasks[d]["q"] != q or either or len(tasks[d]["cost"]) > 1):
                        deps[d] = True
        for x in w:
            touched[x[1]] = [e for e in touched.get(x[1], []) if e[0] & ~x[2]]
        for x, writes in [(x, False) for x in r] + [(x, True) for x in w]:
            touched.setdefault(x[1], []).append((x[2], me, writes))
        tasks.append(dict(q=q, cost={q: cost}, make={q: make}, deps=deps, sem=sem, lag=lag, tag=tuple(tag)))
        tag[2] += 1

    def length(q, out, a, each=1.0):
        if out[5] is not None:
            return 50 + SC * out[3]
        if a[5] is not None:
            return (50 if q == "V" else 65) + GA * out[3]
        return max(LEAST[q], each * out[3]) * CYC + FIXED[q]

    def half(*xs):
        return 0.5 if all(x[4] for x in xs) else 1.0

    def ts(out, a, s1, s2, o0, o1=None):
        more = () if o1 is None else (o1,)
        add("V", length("V", out, a, half(out, a)), lambda: [V.tensor_scalar(out[0], a[0], ap(s1), ap(s2), o0, *more)],
            [a, s1, s2], [out])

    def tt(out, a, b, o):
        add("V", length("V", out, a, 1.0 if "ps" in (a[1], b[1]) else 2.0), lambda: [V.tensor_tensor(out[0], a[0], b[0], o)],
            [a, b], [out])

    def cp(out, a):
        add("V", length("V", out, a, half(out, a)), lambda: [V.tensor_copy(out[0], a[0])], [a], [out])

    def scan(out, d0, d1, init, o0, o1):
        add("V", length("V", out, d0, half(out, d0, d1)), lambda: [V.tensor_tensor_scan(out[0], d0[0], d1[0], init, o0, o1)],
            [d0, d1], [out])

    def wrap(out, data):
        scan(out, vw("MF", 0, out[3]), data, 0.0, OP.add, OP.max)

    def fill(out, c):
        add("V", length("V", out, out, half(out)), lambda: [V.memset(out[0], c)], [], [out])

    def act(out, a, f, sums=None, **kw):
        given = {k: ap(x) for k, x in kw.items()}
        if sums is not None:
            given["accum_out"] = sums[0]
        add("S", length("S", out, a) + (30 if sums else 0), lambda: [S.activation(out[0], a[0], f, **given)],
            [a] + list(kw.values()), [out] + ([sums] if sums else []))

    def move(out, a, c=None, on="S"):
        make = dict(S=lambda: [S.activation(out[0], a[0], AF.Copy, **({} if c is None else {"scale": c}))],
                    V=lambda: [V.tensor_copy(out[0], a[0]) if c is None else V.tensor_scalar(out[0], a[0], c, None, OP.mult)])
        add(on, 0.0, None, [a], [out], either=True)
        tasks[-1].update(cost=dict(S=length("S", out, a), V=length("V", out, a, half(out, a))), make=make)

    def quant(name, a, b, src):
        c, s = vw("q" + name, a, b), vw("s" + name, a, b)
        add("V", 33 + 0.22 * src[3], lambda: [V.quantize_mx(c[0], s[0], src[0])], [src], [c, s])

    def mm(b, st, sa, mv, ma, w, start=True, stop=True):
        x = [vw("q" + st, sa, sa + 128), vw("s" + st, sa, sa + 128), vw("q" + mv, ma, ma + w), vw("s" + mv, ma, ma + w)]
        out = bank(b, w)
        add("P", (w + 16) * 0.4, lambda: [P.matmul_mx(out[0], x[0][0], x[1][0], x[2][0], x[3][0], start, stop)], x, [out],
            acc=not start)

    def iota(out, pat, base=0, mult=0):
        kw = {} if SCRATCH[out[1]][2] == "int32" else {"allow_small_or_imprecise_dtypes": True}
        add("G", 130 + 2 * CYC * out[3], lambda: [g.iota(out[0], pat, base, mult, **kw)], [], [out])

    def dma(q, pairs, r=(), w=(), lag=LOAD):
        dmas[0] += 1
        add(q, ISSUE * len(pairs), lambda: [Q[q].dma_start(o, i) for o, i in pairs], list(r), list(w), "dm%d" % dmas[0], lag)

    def exchange(src, dst, to, frm, sem):
        rid, pid, _ = topo.addr(to)
        m = topo.mask(core, to)

        def make():
            g.remote_dma(T["q" + dst][:].bitcast(dt.uint8), T["q" + src][:].bitcast(dt.uint8), T.sem[sem], T.sem.sent, pid, rid, m)
            g.remote_dma(T["s" + dst][:], T["s" + src][:], T.sem[sem], T.sem.sent, pid, rid, m)
            return (2 * len(topo.engines(core, to)), 2 * len(topo.engines(frm, core)))
        add("G", 390.0 + FIRST * (sem == "arr0"), make, [vw("q" + src), vw("s" + src)], [vw("q" + dst), vw("s" + dst)], sem, TRIP)

    def col(name, j):
        return vw(name, j, j + 1)

    def plane(name, b, w=512):
        return vw(name, 512 * b, 512 * b + w)

    def const(out, c):
        move(out, vw("one", 0, out[3]), c)

    dma("S", [(T.ub[:], T.u[:])], (), [vw("ub")], LOAD + 420)
    for a, b in XP:
        dma("Y", [(T.X[:, 4 * a:4 * b], T.x[:, 4 * a:4 * b])], (), [vw("X", 4 * a, 4 * b)], LOAD + 3.4 * (b - a))
    dma("Y", [(T.cli[:], T.cl[:])], (), [vw("cli")])
    dma("Y", [(T.qL[:].bitcast(dt.uint8), T.wc[:]), (T.sL[:], T.ws[:])], [vw("X")], [vw("qL"), vw("sL")])
    dma("Y", [(T.vb[:], T.v[:])], [vw("X")], [vw("vb")])

    fill(vw("one"), 1.0)
    iota(vw("pcol"), [[0, 1]], 0, 1)
    iota(vw("uoffi"), [[16, 8]])
    iota(vw("i16"), [[0, 13], [1, 16]])
    iota(vw("k16"), [[16, 24]])
    iota(vw("gm"), [[1, 8], [0, 64]])
    iota(vw("val"), [[4, C]])
    iota(vw("n16"), [[1, 16]])
    iota(vw("fd", 0, ZA), [[1, ZA]])
    iota(vw("fd", ZA, A), [[2, A - ZA]], ZA)
    const(vw("Awin", 0, C), float(APART))
    fill(vw("rstb"), 1.0)
    fill(col("rowS", 0) if ROWS[0] == "S" else col("so", SOW - 1), 0.0)
    fill(vw("rstb", 0, C, 16), 0.0)
    for m in range(6):
        const(vw("TT", 4 * (TO[m] + 16 * (21 - 4 * m)), 4 * (TO[m] + TW[m])), 0.0)
    for b in range(4):
        const(vw("Hs", HW * b + ZA, HW * b + HW), 0.0)
    iota(vw("cI"), [[0, 528]])
    add("G", 170 + 2 * CYC * 528, lambda: [g.affine_select(T.cI[:], T.cI[:], [[-1, 528]], OP.not_equal, 0.25, 3, 4)],
        [vw("cI")], [vw("cI")])
    const(vw("Ft", 0, 512), 0.0)
    ts(col("ci", 0), vw("pcol"), 15, None, OP.bitwise_and)
    ts(col("ci", 1), vw("pcol"), 4, None, OP.arith_shift_right)
    cp(vw("uoff"), vw("uoffi"))
    ts(col("ci", 2), vw("pcol"), 3, None, OP.bitwise_and)
    ts(col("ci", 3), vw("pcol"), 2, 3, OP.arith_shift_right, OP.bitwise_and)
    cp(vw("cf", 0, 4), vw("ci"))
    iota(vw("i4"), [[0, 9], [1, 4]])
    ts(vw("v4"), vw("i4", 0, 32), col("cf", 3), -BIG, OP.is_equal, OP.mult)
    ts(vw("w4"), vw("i4", 3, 35), col("cf", 3), 2 * STEP, OP.is_equal, OP.mult)
    tt(vw("M4", 0, 32), vw("w4"), vw("v4"), OP.add)
    move(vw("M4", 32, 64), vw("M4", 0, 32))
    move(vw("M4", 64, 128), vw("M4", 0, 64))
    ts(col("cg", 4), col("cf", 3), 3.0, -2 * STEP, OP.is_lt, OP.mult)
    ts(col("cg", 5), col("cg", 4), col("cf", 2), None, OP.add)
    pr, pg = col("cf", 0), col("cf", 1)
    lift = col("cg", 0)
    ts(lift, pr, 15.0, -LIFT, OP.is_lt, OP.mult)
    ts(col("cg", 1), pr, 15.0, -STEP, OP.is_lt, OP.mult)
    ts(col("cg", 2), col("cg", 1), pr, 15.0 - STEP, OP.subtract, OP.add)
    ts(vw("MR", 0, 32), vw("i16", 1, 33), pr, -BIG, OP.is_equal, OP.mult)
    ts(vw("MR", 32, 64), vw("i16", 0, 32), pr, STEP, OP.is_equal, OP.mult)
    tt(vw("MR", 64, 96), vw("MR", 0, 32), vw("MR", 32, 64), OP.add)
    for a, w in ((0, 32), (32, 32), (96, 96), (192, 192)):
        move(vw("MR", a, a + w), vw("MR", 64, 96) if a < 64 else vw("MR", 0, w))
    ts(vw("Rst"), vw("i16", 0, 192), 0.5, 2 * BIG, OP.subtract, OP.mult)
    ts(vw("M16"), vw("i16", 0, 192), pr, -BIG, OP.not_equal, OP.mult)
    ts(vw("v16"), vw("i16", 0, 32), pr, -BIG, OP.is_equal, OP.mult)
    ts(vw("w16"), vw("i16", 15, 47), pr, LIFT, OP.is_equal, OP.mult)
    tt(vw("MF", 0, 32), vw("w16"), vw("v16"), OP.add)
    for a, w in ((32, 32), (64, 64), (128, 128), (256, 256)):
        move(vw("MF", a, a + w), vw("MF", 0, w))
    ts(vw("jw"), vw("k16"), pr, None, OP.add)
    ts(vw("cB"), vw("gm"), pg, None, OP.is_equal)
    kc = min([k for k in range(17, 24) if ROWS[k - 1] == "V"] + [24])
    ts(vw("cst", 0, kc), vw("k16", 0, kc), col("cg", 2), None, OP.add)
    ts(vw("cst", kc, 24), vw("k16", kc, 24), 0.5, col("cg", 2), OP.mult, OP.add)
    ts(vw("eq"), vw("i16", 0, 16), pr, None, OP.is_equal)
    for j in range(8):
        act(vw("Awin", C + 16 * j, C + 16 * j + 16), vw("eq"), AF.Identity, scale=2048.0 * j - APART, bias=float(APART))
    quant("B", 0, 128, vw("cB"))
    quant("T", TO[5], TO[5] + 128, vw("Ft", 0, 512))
    for b in range(4):
        quant("I", 128 * b, 128 * b + 128, vw("cI", 3 - b, 515 - b))
    quant("U", 0, 128, vw("ub"))
    cp((T.qU2[:].bitcast(dt.uint32),) + vw("qU2")[1:], by(vw("qU"), vw("uoff"), True))
    move(vw("sU2"), by(vw("sU"), vw("uoff")))

    d2 = (None, "d2", 1, 1, True, None)
    for a in range(4):
        cp(vw("c2u", 22 * a, 22 * a + 22), vw("cli", a, 88, 4))
    dma("Y", [(T.d2[:, a], T.c2u[:, 22 * a:22 * a + 22]) for a in range(4)], [vw("c2u")], [d2])
    dma("Y", [(T.Lu[:], T.d2[:])], [d2], [vw("Lu")])
    for i in range(4):
        cp(vw("flist", i, 88, 4), vw("Lu", 22 * i, 22 * i + 22))
    cp(vw("Lf", 0, 88), vw("Lu"))
    move(vw("Lf", 88, 110), vw("Lf", 0, 22))
    act(vw("prio"), vw("Lf", 22, 110), AF.Identity, scale=512.0, bias=lift)
    tt(vw("pay"), vw("prio"), vw("Lf", 0, 88), OP.add)
    for i in range(4):
        act(vw("P0", i, 88, 4), vw("pay", 22 * i, 22 * i + 22), AF.Identity, bias=float((3 - i) * 2 ** 18))
    act(vw("base"), vw("P0"), AF.Identity, bias=float(2 ** 20))
    const(vw("prio", 3, 88, 4), float(2 ** 20))

    def row(k, a, b):
        m, s = (24 - k) // 4, (24 - k) % 4
        return vw("TT", 4 * (TO[m] + a) + s, 4 * (TO[m] + b), 4)

    def position(m):
        return (16 * m, 1) if 16 * m < ZA else (32 * m - ZA, 2)

    def new_places():
        xa, xb, xc = (vw("xs", 24 * j, 24 * j + 24) for j in range(3))
        ts(xa, vw("roff"), float(K), STEP, OP.is_lt, OP.mult)
        ts(xb, vw("roff"), float(C), None, OP.add)
        tt(xc, xa, xb, OP.min)
        tt(xa, xc, vw("jw"), OP.max)
        cp(vw("xoff"), xa)

    def sums_of(a):
        last = min((27 - a) // 4 - 1, 4)
        return last, min(16 * a, TW[last] - 128)

    for t in range(R + 1):
        behind.clear()
        tag[:] = [t, "state" if t < R else "last state", 0]
        if t > 0:
            for b in range(4):
                mm(b, "I", 128 * b, "H%d" % (t - 1), 0, K)
            for b in range(4):
                tt(vw("Ph", 512 * b + C, 512 * b + 512), bank(b, K), vw("Eq", K * b, K * b + K), OP.add)
            for i, (a, e) in enumerate(XP if t < R else XL):
                for b in range(4):
                    move(vw("X", 4 * a + b, 4 * e, 4), by(plane("Ph", b), vw("xoff", a // 16, e // 16)), 2.0,
                         ON["x" if t < R else "xl"][4 * i + b])
        tag[:] = [t, "ranks" if t < R else "outputs", 0]
        for a, e in XP if t < R else XL:
            quant("X", a, e, vw("X", 4 * a, 4 * e))
        if t == R:
            break
        (_, h), _ = XP
        mm(6, "U2", 0, "X", 0, h)
        mm(7, "U2", 0, "X", 0, h)
        mm(3, "U2", 0, "X", h, C - h)
        mm(0, "U2", 0, "X", 0, C)
        mm(1, "U2", 0, "X", 0, C)
        for (a, e), b in zip(XP, (6, 3)):
            tt(vw("msk", a, e), bank(b, e - a), vw("M16", 0, e - a), OP.add)
            scan(vw("sc", a, e), vw("Rst", 0, e - a), vw("msk", a, e), -BIG, OP.min, OP.max)
            tt(row(24, a, e), bank(b, e - a), vw("sc", a, e), OP.is_le)
        scan(vw("dsc"), vw("rstb"), row(24, 0, C), 0.0, OP.mult, OP.add)
        for k in range(23, 0, -1):
            mine = col("sc", 16 * k + 15)
            if ROWS[k - 1] == "V":
                e = SOW * (k + 1)
                ts(row(k, 0, 16 * k), bank(6 if 16 * k < h else 0, 16 * k), mine, None, OP.is_lt)
                scan(vw("so", e - 8 * k, e), row(k, 0, 8 * k), row(k, 8 * k, 16 * k), -8.0 * k * (k >= kc), OP.add, OP.add)
            else:
                o = 8 * k * (k - 1)
                act(vw("tau", o, o + 16 * k), bank(7 if 16 * k < h else 1, 16 * k), AF.Sign, scale=-1.0, bias=mine)
                act(row(k, 0, 16 * k), vw("tau", o, o + 16 * k), AF.Relu, col("rowS", k))
        for m in range(5):
            w = TW[m] + TW[5] * (m == 4)
            quant("T", TO[m], TO[m] + w, vw("TT", 4 * TO[m], 4 * (TO[m] + w)))
            for a, e, b in RP:
                last, c0 = sums_of(a)
                if m <= last:
                    mm(b, "B", 0, "T", TO[m] + c0, min(TW[m], 16 * e) - c0, m == 0, m == last and a > 0)
        mm(RP[-1][2], "B", 0, "T", TO[5], 128, False, True)
        tt(vw("pre0"), vw("cst"), vw("dsc", 15, C, 16), OP.subtract)
        for a, e, b in RP:
            sums = bank(b, 16 * e - sums_of(a)[1], 16 * a - sums_of(a)[1])
            k = a
            while k < e:
                j, q = k + 1, (ROWS[0] + ROWS)[k]
                while j < e and ROWS[j - 1] == q:
                    j += 1
                got = vw("so", SOW * (k + 1) - 1, SOW * j, SOW) if q == "V" else vw("rowS", k, j)
                tt(vw("MR", 16 * k + 15, 16 * j, 16), vw("pre0", k, j), got, OP.subtract)
                k = j
            scan(vw("sc2", 16 * a, 16 * e), sums, vw("MR", 16 * a, 16 * e), -1.0, OP.max, OP.add)
            ts(vw("roff", a, e), vw("sc2", 16 * a + 15, 16 * e, 16), STEP, None, OP.add)
            cp(by(vw("ew"), vw("roff", a, e)), vw("val", 16 * a, 16 * e))
            tasks[-1]["kind"] = "scatter"
        scan(vw("s4o"), vw("M4"), vw("ew", 0, K), 0.0, OP.add, OP.max)
        ts(vw("eoff"), vw("s4o", 3, K, 4), col("cg", 5), None, OP.add)
        for a in (0, 16):
            move(vw("E", 16 * a, 16 * a + 256), by(vw("X"), vw("eoff", a, a + 16)), None, "VS"[a // 16])
        for b in range(4):
            move(plane("Ph", b, C), vw("X", b, 4 * C, 4), 0.5)
        act(vw("Fl", 0, C), bank(1, C), AF.Sign)
        act(vw("Fl", 0, C), vw("Fl", 0, C), AF.Relu, scale=TOP)
        quant("E%d" % t, 0, K, vw("E"))
        behind.append(len(tasks) - 1)
        exchange("E%d" % t, "G%d" % t, after, before, "arr%d" % (2 * t))
        if t:
            tag[:] = [t, "lists", 0]
            new_places()
        behind.clear()
        tag[:] = [t, "layer", 0]
        Gn = "G%d" % t
        mm(3, "U2", 0, Gn, 0, K)
        for b in range(4):
            mm(4 + b, "I", 128 * b, Gn, 0, K)
        ts(vw("Fl", C, 512), bank(3, K), 0.0, TOP, OP.is_gt, OP.mult)
        for i, (a, b) in enumerate(FP):
            move(vw("Ft", 16 * a, 16 * b), by(vw("Fl"), vw("flist", a, b)), None, ON["fl"][i])
            wrap(vw("Fs", 16 * a, 16 * b), vw("Ft", 16 * a, 16 * b))
        for b in range(4):
            move(vw("Ph", 512 * b + C, 512 * b + 512), bank(4 + b, K), 2.0, ON["phb"][b])
        for a, e in ZP:
            tt(vw("cand", 4 * a, 4 * e), vw("Fs", 64 * a + 15, 64 * e, 16), vw("base", 4 * a, 4 * e), OP.add)
            tt(vw("c1", 2 * a, 2 * e), vw("cand", 4 * a, 4 * e, 2), vw("cand", 4 * a + 1, 4 * e, 2), OP.max)
            tt(vw("c2i", a, e), vw("c1", 2 * a, 2 * e, 2), vw("c1", 2 * a + 1, 2 * e, 2), OP.max)
            ts(vw("ot", 2 * a, a + e), vw("c2i", a, e), 511, None, OP.bitwise_and)
            ts(vw("ot", a + e, 2 * e), vw("c2i", a, e), 9, 511, OP.arith_shift_right, OP.bitwise_and)
            cp(vw("zoff", 2 * a, 2 * e), vw("ot", 2 * a, 2 * e))
            tt(vw("Ar", 16 * a, 16 * e), by(vw("Awin"), vw("zoff", 2 * a, a + e)), vw("fd", 16 * a, 16 * e), OP.add)
        for i, (a, e) in enumerate(ZP):
            one, two = vw("zoff", 2 * a, a + e), vw("zoff", a + e, 2 * e)
            for b in range(4):
                part = vw("tmp", A * b + 16 * a, A * b + 16 * e)
                move(part, by(plane("Ph", b), two), None, ON["z"][4 * i + b])
                tt(vw("Z", 64 * a + b, 64 * e, 4), by(plane("Ph", b), one), part, OP.add)
            quant("Z", 16 * a, 16 * e, vw("Z", 64 * a, 64 * e))
            o, step = position(a)
            for b in range(4):
                mm(4 * (i % 2) + b, "L", 128 * b, "Z", 16 * a, 16 * (e - a))
                move(vw("Hs", HW * b + o, HW * b + o + 16 * (e - a) * step, step), bank(4 * (i % 2) + b, 16 * (e - a)), 0.03125,
                     ON["h"][4 * i + b])
        for s in range(8):
            if s:
                act(vw("D0", A * s, A * s + A), vw("Ar"), AF.Abs, bias=-2048.0 * s)
            name, o = ("D0", A * s) if s else ("Ar", 0)
            scan(vw("so2", A // 2 * s, A // 2 * (s + 1)), vw(name, o, o + A // 2), vw(name, o + A // 2, o + A),
                 float(2 * A - ZA), OP.min, OP.min)
        cp(vw("foff"), vw("so2", A // 2 - 1, 4 * A, A // 2))
        for b in range(4):
            move(vw("Vt", b, 512, 4), by(vw("Hs", HW * b, HW * b + HW), vw("foff")), None, ON["vt"][b])
        quant("V%d" % t, 0, K, vw("Vt"))
        behind.append(len(tasks) - 1)
        tag[:] = [t, "rest %d" % t, 0]
        exchange("V%d" % t, "H%d" % t, before, after, "arr%d" % (2 * t + 1))
        for b in range(4):
            move(vw("Eq", K * b, K * b + K), vw("E", b, 512, 4), 0.25)
        if t == 0:
            new_places()
            quant("Vv", 0, 128, vw("vb"))
        ts(vw("cc"), vw("c2i"), 18, 3, OP.arith_shift_right, OP.bitwise_and)
        if t + 1 < R:
            for i in range(3):
                ts(vw("prio", i, 88, 4), vw("cc"), float(3 - i), float(2 ** 20), OP.is_ge, OP.mult)
            tt(vw("base"), vw("prio"), vw("P0"), OP.add)
        else:
            ts(vw("coff"), vw("cc"), -1.0, 3.0, OP.mult, OP.add)
            move(vw("owb"), by(vw("n16"), vw("coff")))
            dma("Y", [(T.ow[:], T.owb[0:128:16, :])], [vw("owb")])

    for i, (a, e) in enumerate(XL):
        mm(5 + i, "Vv", 0, "X", a, e - a)
        dma("Y", [(T.oc[:, 4 * a:4 * e], T.qX[:, a:e].bitcast(dt.uint8))], [vw("qX", a, e)], (), LOAD + 1.7 * (e - a))
        move(vw("yb", a, e), bank(5 + i, e - a), None, ON["y"][i])
        dma(ON["yd"][i], [(T.y[:, a:e], T.yb[:, a:e])], [vw("yb", a, e)], (), LOAD + 1.7 * (e - a))
    for k in range(4):
        dma(ON["os"][k], [(T.osc[4 * k:4 * k + 4, :], T.sX[32 * k:32 * k + 4, :])], [vw("sX")], (), LOAD - 200)

    count, mark, knew = {}, {}, {}
    waited = {q: {} for q in Q}
    if not LAID:
        LAID.extend(lay_out(tasks))
    for i, q in LAID:
        task, w, todo = tasks[i], waited[q], {}
        for d, waits in task["deps"].items():
            if waits and w.get(mark[d][0], 0) < mark[d][1]:
                todo[mark[d][0]] = max(todo.get(mark[d][0], 0), mark[d][1])
        for sem, val in todo.items():
            if not any(o != sem and knew[(o, ov)].get(sem, 0) >= val for o, ov in todo.items()):
                Q[q].wait_ge(T.sem[sem], val)
        for sem, val in todo.items():
            for s_, v_ in list(knew[(sem, val)].items()) + [(sem, val)]:
                w[s_] = max(w.get(s_, 0), v_)
        calls, sem = task["make"][q](), task["sem"] or "c" + q
        if isinstance(calls, tuple):
            count["sent"] = count.get("sent", 0) + calls[0]
            count[sem] = calls[1]
            knew[(sem, count[sem])] = {}
        else:
            for call in calls:
                call.then_inc(T.sem[sem], 16 if task["sem"] else 1)
                count[sem] = count.get(sem, 0) + (16 if task["sem"] else 1)
            knew[(sem, count[sem])] = dict(w)
        mark[i] = (sem, count[sem])
    g.wait_ge(T.sem.sent, count["sent"])
    for s_, v_ in count.items():
        if s_ != "sent":
            Y.wait_ge(T.sem[s_], v_)
